import numpy as np
import ml_dtypes


def mxq(x, axis, fmt="e4m3"):
    dtype, down = {"e4m3": (ml_dtypes.float8_e4m3fn, 7), "e5m2": (ml_dtypes.float8_e5m2, 14)}[fmt]
    v = np.moveaxis(np.asarray(x, np.float32).astype(ml_dtypes.bfloat16).astype(np.float64), axis, -1)
    blocks = v.reshape(v.shape[:-1] + (-1, 32))
    amax = np.abs(blocks).max(-1, keepdims=True)
    byte = np.maximum(np.where(amax > 0, np.frexp(amax)[1] - 1 + 127, 0) - down, 1)
    scale = np.exp2(byte - 127.0)
    codes = (blocks / scale).astype(np.float32).astype(dtype).astype(np.float64)
    return np.moveaxis((codes * scale).reshape(v.shape), -1, axis)


WIDE = False


def mx_kscale(k):
    if not WIDE:
        return np.ones(k)
    levels = np.array([10, -10, 5, -5, 0])
    if k % 512:
        return np.exp2(np.random.permutation(np.resize(levels, k // 32))).repeat(32)
    a = np.empty((k // 512, 16))
    for p in range(k // 512):
        a[p, :8] = np.random.permutation(np.resize(levels, 8))
        for g in range(8):
            far = levels[np.abs(levels - a[p, g]) >= 10]
            a[p, g + 8] = far[np.random.randint(len(far))]
    return np.exp2(a.ravel()).repeat(32)


def f64(x):
    return np.asarray(x).astype(np.float64)


def striped(idx):
    return np.tile(idx.reshape(-1, 16).T, (8, 1)).astype(np.uint16)


def unstriped(offs):
    return offs[:16].T.reshape(-1).astype(np.int64)


E2M1 = np.array([0.0, 0.5, 1.0, 1.5, 2.0, 3.0, 4.0, 6.0, -0.0, -0.5, -1.0, -1.5, -2.0, -3.0, -4.0, -6.0])


def pack_weight(w, fmt):
    k, n = w.shape
    w = f64(np.asarray(w, np.float32).astype(ml_dtypes.bfloat16)).reshape(k // 32, 32, n)
    amax = np.abs(w).max(1)
    if fmt == "e4m3":
        byte = np.frexp(amax)[1] - 1 + 127 - 7
    else:
        mant, ex = np.frexp(amax / 6.0)
        byte = np.where(mant > 0.5, ex, ex - 1) + 127
    byte = np.clip(np.where(amax > 0, byte, 1), 1, 254)
    scaled = (w * np.exp2(127.0 - byte)[:, None, :]).reshape(k, n).astype(np.float32)
    by_word = np.ascontiguousarray(scaled.reshape(k // 512, 128, 4, n).transpose(0, 1, 3, 2))
    if fmt == "e4m3":
        words = by_word.astype(ml_dtypes.float8_e4m3fn).view(np.uint8)
    else:
        c = by_word.astype(ml_dtypes.float4_e2m1fn).view(np.uint8) & 0xF
        words = (c[..., 0::2] | (c[..., 1::2] << 4)).reshape(k // 512, 128, 2 * n)
    return np.ascontiguousarray(words), np.ascontiguousarray(byte.astype(np.uint8).reshape(k // 512, 16, n))


def unpack_weight(words, scales, fmt):
    g, _, n = scales.shape
    words = np.ascontiguousarray(words).reshape(g, 128, n, -1)
    if fmt == "e4m3":
        vals = words.view(ml_dtypes.float8_e4m3fn).astype(np.float64)
    else:
        nib = np.empty((g, 128, n, 4), np.uint8)
        nib[..., 0::2] = words & 0xF
        nib[..., 1::2] = words >> 4
        vals = E2M1[nib]
    vals = vals * np.repeat(np.exp2(scales.astype(np.float64) - 127.0), 8, axis=1)[..., None]
    return vals.transpose(0, 1, 3, 2).reshape(g * 512, n)


def relu(v):
    return np.maximum(v, 0.0)


def d_relu(v):
    return (v > 0).astype(np.float64)


K, T, E, C, H, N = 512, 512, 4, 256, 512, 1536


def by_expert(wq, xq):
    return np.concatenate([wq[e].T @ xq[:, e * C:(e + 1) * C] for e in range(E)], axis=1)


def setup_inputs():
    n = np.random.standard_normal
    s = mx_kscale(N)[:, None]
    u = mx_kscale(H)
    first = np.random.permutation(np.repeat(np.arange(E), T // E))
    second = (first + 1 + np.random.permutation(np.repeat(np.arange(E - 1), -(-T // (E - 1)))[:T])) % E
    while np.bincount(second, minlength=E).max() != T // E:
        load = np.bincount(second, minlength=E); hi, lo = int(load.argmax()), int(load.argmin())
        t = np.flatnonzero((second == hi) & (first != lo))[0]; second[t] = lo
    slot_token = np.empty(E * C, np.int64); pos = np.empty((2, T), np.int64); fill = np.zeros(E, np.int64)
    place = np.stack([np.random.permutation(C) for _ in range(E)])
    for r, deal in enumerate((first, second)):
        for t in np.random.permutation(T):
            e = deal[t]; j = e * C + place[e, fill[e]]; fill[e] += 1; slot_token[j] = t; pos[r, t] = j
    g = np.random.uniform(0.2, 0.8, T)
    w_slot = np.empty(E * C); w_slot[pos[0]] = g; w_slot[pos[1]] = 1.0 - g
    w2 = [pack_weight(m, "e2m1") for m in n((E, N, H)) / np.sqrt(N) / s[None] * u[None, None, :]]
    w1 = [pack_weight(m, "e2m1") for m in n((E, H, K)) / np.sqrt(H) / u[None, :, None]]
    w3 = [pack_weight(m, "e2m1") for m in n((E, H, K)) / np.sqrt(H) / u[None, :, None]]
    return {
        "dyT": (n((N, T)) * s).astype(np.float32),
        "a1": n((H, E * C)).astype(np.float32),
        "a3": n((H, E * C)).astype(np.float32),
        "w2_words": np.stack([m[0] for m in w2]),
        "w2_scales": np.stack([m[1] for m in w2]),
        "w1_words": np.stack([m[0] for m in w1]),
        "w1_scales": np.stack([m[1] for m in w1]),
        "w3_words": np.stack([m[0] for m in w3]),
        "w3_scales": np.stack([m[1] for m in w3]),
        "gate": np.tile(w_slot, (N, 1)).astype(np.float32),
        "offs": striped(slot_token),
        "pos1": striped(pos[0]),
        "pos2": striped(pos[1]),
    }


def reference(dyT, a1, a3, w2_words, w2_scales, w1_words, w1_scales, w3_words, w3_scales, gate, offs, pos1, pos2):
    idx = unstriped(offs)
    w2 = np.stack([unpack_weight(w2_words[e], w2_scales[e], "e2m1") for e in range(E)])
    w1 = np.stack([unpack_weight(w1_words[e], w1_scales[e], "e2m1") for e in range(E)])
    w3 = np.stack([unpack_weight(w3_words[e], w3_scales[e], "e2m1") for e in range(E)])
    gq = mxq(f64(gate) * f64(dyT)[:, idx], 0, "e4m3")
    dh = by_expert(w2, gq)
    da1 = dh * f64(a3) * d_relu(f64(a1))
    da3 = dh * relu(f64(a1))
    dx = by_expert(w1, mxq(da1, 0, "e4m3")) + by_expert(w3, mxq(da3, 0, "e4m3"))
    return dx[:, unstriped(pos1)] + dx[:, unstriped(pos2)]

@@ -1,0 +1,254 @@
+from contextlib import ExitStack
+
+import concourse.mybir as mybir
+from concourse.masks import make_identity
+
+K, T, E, C, H, N = 512, 512, 4, 256, 512, 1536
+P = 128
+S = N // 512
+SLOTS = E * C
+CUT = 384
+PIECES = ((0, 256), (256, 384), (384, 512), (512, 768), (768, 896), (768, 1024), (896, 1024))
+
+FLOPS = 2 * SLOTS * (N * H + 2 * H * K)
+BYTES = 11210752
+
+F32 = mybir.dt.float32
+BF16 = mybir.dt.bfloat16
+I32 = mybir.dt.int32
+U32 = mybir.dt.uint32
+U16 = mybir.dt.uint16
+U8 = mybir.dt.uint8
+FP8 = mybir.dt.float8_e4m3fn_x4
+FP4 = mybir.dt.float4_e2m1fn_x4
+MULT = mybir.AluOpType.mult
+ADD = mybir.AluOpType.add
+IS_GT = mybir.AluOpType.is_gt
+RELU = mybir.ActivationFunctionType.Relu
+
+PROGRAM = (
+    ("g", 0, 0, 0, 0, 384), ("g", 0, 0, 1, 0, 384), ("g", 0, 0, 2, 0, 384), ("g", 0, 0, 3, 0, 384),
+    ("m", 0), ("g", 0, 1, 0, 0, 384), ("g", 0, 1, 1, 0, 384), ("g", 0, 1, 2, 0, 384),
+    ("g", 0, 1, 3, 0, 384), ("g", 0, 2, 0, 0, 384), ("g", 0, 2, 1, 0, 384), ("g", 0, 2, 2, 0, 384),
+    ("m", 1), ("g", 0, 2, 3, 0, 384), ("g", 1, 0, 0, 384, 768), ("q", 256, 384, 0),
+    ("q", 256, 384, 1), ("g", 1, 0, 1, 384, 768), ("q", 0, 256, 1), ("g", 1, 0, 2, 384, 768),
+    ("q", 0, 256, 2), ("q", 256, 384, 2), ("q", 0, 256, 0), ("g", 1, 0, 3, 384, 768),
+    ("g", 1, 1, 0, 384, 768), ("m", 2), ("q", 384, 512, 0), ("g", 1, 1, 1, 384, 768),
+    ("g", 1, 1, 2, 384, 768), ("g", 1, 1, 3, 384, 768), ("dh", 0), ("da", 0),
+    ("g", 1, 2, 0, 384, 768), ("g", 1, 2, 1, 384, 768), ("q", 384, 512, 1), ("g", 1, 2, 2, 384, 768),
+    ("g", 1, 2, 3, 384, 768), ("dh", 1), ("dh", 2), ("da", 1),
+    ("dq", 0), ("g", 2, 0, 0, 768, 1024), ("m", 3), ("q", 384, 512, 2),
+    ("q", 512, 768, 0), ("g", 2, 0, 1, 768, 1024), ("dh", 3), ("da", 2),
+    ("g", 2, 0, 2, 768, 1024), ("g", 2, 0, 3, 768, 1024), ("g", 2, 1, 0, 768, 1024), ("m", 4),
+    ("da", 3), ("g", 2, 1, 1, 768, 1024), ("g", 2, 1, 2, 768, 1024), ("q", 512, 768, 1),
+    ("m", 5), ("g", 2, 1, 3, 768, 1024), ("q", 512, 768, 2), ("g", 2, 2, 0, 768, 896),
+    ("g", 2, 2, 1, 768, 896), ("dq", 1), ("g", 2, 2, 2, 768, 896), ("dh", 4),
+    ("dq", 2), ("dh", 5), ("g", 2, 2, 3, 768, 896), ("m", 6),
+    ("da", 4), ("q", 768, 1024, 0), ("da", 5), ("q", 768, 1024, 1),
+    ("g", 2, 2, 0, 896, 1024), ("g", 2, 2, 1, 896, 1024), ("g", 2, 2, 2, 896, 1024), ("g", 2, 2, 3, 896, 1024),
+    ("q", 768, 896, 2), ("dq", 3), ("dh", 6), ("q", 896, 1024, 2),
+    ("m", 7), ("dh", 7), ("dq", 4), ("da", 6),
+    ("da", 7), ("dq", 5), ("dq", 6), ("dq", 7),
+)
+
+
+def tile_moe_bdx_glu_relu_kernel(
+    tc, dyT, a1, a3, w2_words, w2_scales, w1_words, w1_scales, w3_words, w3_scales, gate, offs, pos1, pos2, out
+):
+    nc = tc.nc
+    with ExitStack() as ctx:
+        keep = ctx.enter_context(tc.tile_pool(name="keep", bufs=1))
+        work = ctx.enter_context(tc.tile_pool(name="work", bufs=3))
+        psum = ctx.enter_context(tc.psum_pool(name="psum", bufs=1))
+
+        offs_t = keep.tile([P, SLOTS // 16], U16, name="offs_t")
+        nc.sync.dma_start(offs_t[:], offs)
+
+        w2_pl = keep.tile([P, E * S, H], U8, name="w2_pl", align_bytes=64)
+        w1_pl = keep.tile([P, E, K], U8, name="w1_pl", align_bytes=64)
+        w3_pl = keep.tile([P, E, K], U8, name="w3_pl", align_bytes=64)
+        for pl in (w2_pl, w1_pl, w3_pl):
+            nc.vector.memset(pl[:].rearrange("p a b -> p (a b)").bitcast(I32), 0)
+        ident = keep.tile([P, P], F32, name="ident")
+        make_identity(nc, ident[:])
+
+        gates, planes, w2_t, a1_t, a3_t = [], [], [], [], []
+        dy_v = dyT.rearrange("(s p t) c -> s t p c", p=P, t=4)
+        g0 = keep.tile([P, CUT], F32, name="gate_a")
+        g1 = keep.tile([P, SLOTS - CUT], F32, name="gate_b")
+        for i in range(S * 4):
+            pt = keep.tile([P, T], F32, name=f"plane{i}")
+            planes.append(pt)
+        for e in range(E):
+            w = keep.tile([P, S, 2 * H], U8, name=f"w2_{e}", align_bytes=64)
+            w2_t.append(w)
+        w1_t = keep.tile([P, E, 2 * K], U8, name="w1_t", align_bytes=64)
+        w3_t = keep.tile([P, E, 2 * K], U8, name="w3_t", align_bytes=64)
+        for e in range(2):
+            x1 = keep.tile([P, 4, 2 * C], F32, name=f"a1_{e}")
+            x3 = keep.tile([P, 4, 2 * C], F32, name=f"a3_{e}")
+            a1_t.append(x1)
+            a3_t.append(x3)
+
+        def load_w2(e):
+            nc.sync.dma_start(w2_t[e][:].bitcast(I32), w2_words[e].bitcast(I32).rearrange("s p c -> p s c"))
+
+        def load_a(e):
+            nc.scalar.dma_start(a1_t[e][:], a1.rearrange("(b p) j -> p b j", p=P)[:, :, 2 * C * e : 2 * C * (e + 1)])
+            nc.scalar.dma_start(a3_t[e][:], a3.rearrange("(b p) j -> p b j", p=P)[:, :, 2 * C * e : 2 * C * (e + 1)])
+
+        def load_scales(pl, sc):
+            for q in range(4):
+                nc.sync.dma_start(
+                    pl[32 * q : 32 * q + 4].bitcast(I32),
+                    sc.bitcast(I32).rearrange("e s f i -> f (e s) i")[4 * q : 4 * q + 4],
+                )
+
+        nc.scalar.dma_start(g0[:], gate[0:P, 0:CUT])
+        for i in range(S * 4):
+            (nc.scalar if i % 2 else nc.sync).dma_start(planes[i][:], dy_v[i // 4, i % 4])
+        nc.scalar.dma_start(g1[:], gate[0:P, CUT:SLOTS])
+        load_a(0)
+        load_w2(0)
+        load_scales(w2_pl, w2_scales)
+        load_w2(1)
+        for wt, ww in ((w1_t, w1_words), (w3_t, w3_words)):
+            nc.sync.dma_start(wt[:].bitcast(I32), ww.bitcast(I32).rearrange("e s p c -> p (e s) c"))
+        load_scales(w1_pl, w1_scales)
+        load_scales(w3_pl, w3_scales)
+        load_w2(2)
+        load_w2(3)
+        pos_t = []
+        for i, ps in enumerate((pos1, pos2)):
+            pp = keep.tile([P, T // 16], U16, name=f"pos_t{i}")
+            nc.sync.dma_start(pp[:], ps)
+            pos_t.append(pp)
+
+        dx = keep.tile([P, 4, SLOTS], F32, name="dx")
+        gq, gs = {}, {}
+        gf, gb, rm, dh, dag, dq, ds = {}, {}, {}, {}, {}, {}, {}
+
+        def gather(c, s, t, lo, hi):
+            base = 2 * P * 3 // 2 * c
+            if (c, s) not in gf:
+                g = work.tile([P, 4, CUT], F32, name="gf", bufs=4)
+                gf[c, s] = g
+            nc.vector.tensor_tensor(
+                gf[c, s][:, t, lo - base : hi - base],
+                planes[4 * s + t][:].indirect(offs_t[:, lo // 16 : hi // 16]),
+                g0[:, lo:hi] if c == 0 else g1[:, lo - CUT : hi - CUT],
+                MULT,
+            )
+            if t == 3:
+                at = lo
+                for a, b in PIECES:
+                    if a == at and b <= hi and (b == hi or b % C == 0):
+                        x = work.tile([P, C, 4], BF16, name="gb", bufs=7, align_bytes=64)
+                        nc.scalar.copy(
+                            x[:, 0 : b - a, :].rearrange("p (c i) t -> p c t i", i=4),
+                            gf[c, s][:, :, a - base : b - base].rearrange("p t (c i) -> p c t i", i=4),
+                        )
+                        gb[a, s] = x
+                        at = b
+                if (c, s) == (0, 2):
+                    load_a(1)
+
+        def quantize(lo, hi, s):
+            q = keep.tile([P, hi - lo], U32, name=f"gq{s}_{lo}", align_bytes=64)
+            z = keep.tile([P, hi - lo], U8, name=f"gs{s}_{lo}", align_bytes=64)
+            for i in range(lo // P, hi // P):
+                gq[i, s] = q[:, P * i - lo : P * i - lo + P]
+                gs[i, s] = z[:, P * i - lo : P * i - lo + P]
+            nc.vector.quantize_mx(
+                out=q[:].bitcast(FP8),
+                scales=z[:],
+                in_=gb[lo, s][:, 0 : hi - lo, :].rearrange("p c t -> p (c t)"),
+            )
+
+        def saved(i):
+            e, col = i // 4, P * (i % 4)
+            a1p = psum.tile([P, H], F32, name="a1p", bufs=1)
+            a3p = psum.tile([P, H], F32, name="a3p", bufs=1)
+            for b in range(4):
+                nc.tensor.transpose(a1p[:, P * b : P * (b + 1)], a1_t[e][:, b, col : col + P], ident[:])
+            for b in range(4):
+                nc.tensor.transpose(a3p[:, P * b : P * (b + 1)], a3_t[e][:, b, col : col + P], ident[:])
+            x = work.tile([P, 2, H], F32, name="rm", bufs=5)
+            nc.scalar.activation(x[:, 1, :], a1p[:], RELU)
+            nc.vector.scalar_tensor_tensor(x[:, 0, :], x[:, 1, :], 0.0, a3p[:], IS_GT, MULT)
+            rm[i] = x
+
+        def first(i):
+            e = i // 2
+            acc = psum.tile([P, H], F32, name="dh", bufs=2)
+            for s in range(S):
+                nc.tensor.matmul_mx(
+                    out=acc[:],
+                    lhsT=gq[i, s].bitcast(FP8),
+                    lhsT_scale=gs[i, s],
+                    rhs=w2_t[e][:, s, :].bitcast(FP4),
+                    rhs_scale=w2_pl[:, S * e + s, :],
+                    start=(s == 0),
+                    stop=(s == S - 1),
+                )
+            dh[i] = acc
+
+        def grads(i):
+            last = i == 7
+            da = work.tile([P, 2, H], BF16, name="da", bufs=3, align_bytes=64)
+            if last:
+                for w in range(2):
+                    nc.vector.tensor_tensor(da[:, w, :], dh[i][:], rm[i][:, w, :], MULT)
+            else:
+                nc.vector.tensor_tensor(da[:], dh[i][:].unsqueeze(1).to_broadcast([P, 2, H]), rm[i][:], MULT)
+            dap = psum.tile([P, 2, 2, P], F32, name="dap", bufs=2)
+            for w in range(2):
+                words = da[:, w, :].bitcast(F32)
+                for u in range(2):
+                    nc.tensor.transpose(dap[:, w, u, :], words[:, u:256:2], ident[:])
+            g = work.tile([P, 2 * P * 4], BF16, name="dag", bufs=3, align_bytes=64)
+            g_v = g[:].bitcast(F32).rearrange("p (w r u) -> p w r u", w=2, u=2)
+            dap_v = dap[:].rearrange("p w u r -> p w r u")
+            if last:
+                for w in range(2):
+                    nc.scalar.copy(g_v[:, w], dap_v[:, w])
+            else:
+                nc.scalar.copy(g_v, dap_v)
+            dag[i] = g
+
+        def second(i):
+            last = i == 7
+            q = work.tile([P, 2 * P], U32, name="dq", bufs=3, align_bytes=64)
+            z = work.tile([P, 2 * P], U8, name="ds", bufs=3, align_bytes=64)
+            for a, b in ((0, P), (P, 2 * P)) if last else ((0, 2 * P),):
+                nc.vector.quantize_mx(out=q[:, a:b].bitcast(FP8), scales=z[:, a:b], in_=dag[i][:, 4 * a : 4 * b])
+            dxp = psum.tile([P, 4, P], F32, name="dxp", bufs=2)
+            j0 = P * i
+            for kt in range(4):
+                for w, (wt, pl) in enumerate(((w1_t, w1_pl), (w3_t, w3_pl))):
+                    nc.tensor.matmul_mx(
+                        out=dxp[:, kt, :],
+                        lhsT=wt[:, i // 2, 256 * kt : 256 * (kt + 1)].bitcast(FP4),
+                        lhsT_scale=pl[:, i // 2, P * kt : P * (kt + 1)],
+                        rhs=q[:, P * w : P * (w + 1)].bitcast(FP8),
+                        rhs_scale=z[:, P * w : P * (w + 1)],
+                        start=(w == 0),
+                        stop=(w == 1),
+                    )
+                if last:
+                    nc.scalar.copy(dx[:, kt, j0 : j0 + P], dxp[:, kt, :])
+            if not last:
+                nc.scalar.copy(dx[:, :, j0 : j0 + P], dxp[:])
+
+        steps = {"g": gather, "q": quantize, "m": saved, "dh": first, "da": grads, "dq": second}
+        for step in PROGRAM:
+            steps[step[0]](*step[1:])
+
+        for kt in range(4):
+            o1 = work.tile([P, T], F32, name="o1", bufs=2)
+            o2 = work.tile([P, T], F32, name="o2", bufs=2)
+            o = work.tile([P, T], F32, name="o", bufs=2)
+            nc.vector.tensor_copy(o1[:], dx[:, kt, :].indirect(pos_t[0][:]))
+            nc.vector.tensor_copy(o2[:], dx[:, kt, :].indirect(pos_t[1][:]))
+            (nc.vector if kt == 3 else nc.gpsimd).tensor_tensor(o[:], o1[:], o2[:], ADD)
+            nc.sync.dma_start(out[P * kt : P * (kt + 1), :], o[:])

@@ -7,8 +7,9 @@ K, T, E, C, H, N = 512, 512, 4, 256, 512, 1536
 P = 128
 S = N // 512
 SLOTS = E * C
-CUT = 384
-PIECES = ((0, 256), (256, 384), (384, 512), (512, 768), (768, 896), (768, 1024), (896, 1024))
+TILES = SLOTS // P
+CUT = 640
+WINDOW = max(CUT, SLOTS - CUT, T - 16) + 16
 
 FLOPS = 2 * SLOTS * (N * H + 2 * H * K)
 BYTES = 11210752
@@ -23,33 +24,8 @@ FP8 = mybir.dt.float8_e4m3fn_x4
 FP4 = mybir.dt.float4_e2m1fn_x4
 MULT = mybir.AluOpType.mult
 ADD = mybir.AluOpType.add
-IS_GT = mybir.AluOpType.is_gt
 RELU = mybir.ActivationFunctionType.Relu
-
-PROGRAM = (
-    ("g", 0, 0, 0, 0, 384), ("g", 0, 0, 1, 0, 384), ("g", 0, 0, 2, 0, 384), ("g", 0, 0, 3, 0, 384),
-    ("m", 0), ("g", 0, 1, 0, 0, 384), ("g", 0, 1, 1, 0, 384), ("g", 0, 1, 2, 0, 384),
-    ("g", 0, 1, 3, 0, 384), ("g", 0, 2, 0, 0, 384), ("g", 0, 2, 1, 0, 384), ("g", 0, 2, 2, 0, 384),
-    ("m", 1), ("g", 0, 2, 3, 0, 384), ("g", 1, 0, 0, 384, 768), ("q", 256, 384, 0),
-    ("q", 256, 384, 1), ("g", 1, 0, 1, 384, 768), ("q", 0, 256, 1), ("g", 1, 0, 2, 384, 768),
-    ("q", 0, 256, 2), ("q", 256, 384, 2), ("q", 0, 256, 0), ("g", 1, 0, 3, 384, 768),
-    ("g", 1, 1, 0, 384, 768), ("m", 2), ("q", 384, 512, 0), ("g", 1, 1, 1, 384, 768),
-    ("g", 1, 1, 2, 384, 768), ("g", 1, 1, 3, 384, 768), ("dh", 0), ("da", 0),
-    ("g", 1, 2, 0, 384, 768), ("g", 1, 2, 1, 384, 768), ("q", 384, 512, 1), ("g", 1, 2, 2, 384, 768),
-    ("g", 1, 2, 3, 384, 768), ("dh", 1), ("dh", 2), ("da", 1),
-    ("dq", 0), ("g", 2, 0, 0, 768, 1024), ("m", 3), ("q", 384, 512, 2),
-    ("q", 512, 768, 0), ("g", 2, 0, 1, 768, 1024), ("dh", 3), ("da", 2),
-    ("g", 2, 0, 2, 768, 1024), ("g", 2, 0, 3, 768, 1024), ("g", 2, 1, 0, 768, 1024), ("m", 4),
-    ("da", 3), ("g", 2, 1, 1, 768, 1024), ("g", 2, 1, 2, 768, 1024), ("q", 512, 768, 1),
-    ("m", 5), ("g", 2, 1, 3, 768, 1024), ("q", 512, 768, 2), ("g", 2, 2, 0, 768, 896),
-    ("g", 2, 2, 1, 768, 896), ("dq", 1), ("g", 2, 2, 2, 768, 896), ("dh", 4),
-    ("dq", 2), ("dh", 5), ("g", 2, 2, 3, 768, 896), ("m", 6),
-    ("da", 4), ("q", 768, 1024, 0), ("da", 5), ("q", 768, 1024, 1),
-    ("g", 2, 2, 0, 896, 1024), ("g", 2, 2, 1, 896, 1024), ("g", 2, 2, 2, 896, 1024), ("g", 2, 2, 3, 896, 1024),
-    ("q", 768, 896, 2), ("dq", 3), ("dh", 6), ("q", 896, 1024, 2),
-    ("m", 7), ("dh", 7), ("dq", 4), ("da", 6),
-    ("da", 7), ("dq", 5), ("dq", 6), ("dq", 7),
-)
+SIGN = mybir.ActivationFunctionType.Sign
 
 
 def tile_moe_bdx_glu_relu_kernel(
@@ -64,38 +40,33 @@ def tile_moe_bdx_glu_relu_kernel(
         offs_t = keep.tile([P, SLOTS // 16], U16, name="offs_t")
         nc.sync.dma_start(offs_t[:], offs)
 
+        planes = [keep.tile([P, WINDOW], F32, name=f"plane{i}") for i in range(4 * S)]
+        for pt in planes:
+            nc.vector.memset(pt[:, T:WINDOW], 0.0)
         w2_pl = keep.tile([P, E * S, H], U8, name="w2_pl", align_bytes=64)
         w1_pl = keep.tile([P, E, K], U8, name="w1_pl", align_bytes=64)
         w3_pl = keep.tile([P, E, K], U8, name="w3_pl", align_bytes=64)
-        for pl in (w2_pl, w1_pl, w3_pl):
-            nc.vector.memset(pl[:].rearrange("p a b -> p (a b)").bitcast(I32), 0)
         ident = keep.tile([P, P], F32, name="ident")
         make_identity(nc, ident[:])
+        for pl in (w2_pl, w1_pl, w3_pl):
+            nc.gpsimd.memset(pl[:].rearrange("p a b -> p (a b)").bitcast(I32), 0)
 
-        gates, planes, w2_t, a1_t, a3_t = [], [], [], [], []
         dy_v = dyT.rearrange("(s p t) c -> s t p c", p=P, t=4)
-        g0 = keep.tile([P, CUT], F32, name="gate_a")
-        g1 = keep.tile([P, SLOTS - CUT], F32, name="gate_b")
-        for i in range(S * 4):
-            pt = keep.tile([P, T], F32, name=f"plane{i}")
-            planes.append(pt)
-        for e in range(E):
-            w = keep.tile([P, S, 2 * H], U8, name=f"w2_{e}", align_bytes=64)
-            w2_t.append(w)
+        gates = [keep.tile([P, CUT], F32, name="gate_a"), keep.tile([P, SLOTS - CUT], F32, name="gate_b")]
+        w2_t = [keep.tile([P, S, 2 * H], U8, name=f"w2_{e}", align_bytes=64) for e in range(E)]
         w1_t = keep.tile([P, E, 2 * K], U8, name="w1_t", align_bytes=64)
         w3_t = keep.tile([P, E, 2 * K], U8, name="w3_t", align_bytes=64)
-        for e in range(2):
-            x1 = keep.tile([P, 4, 2 * C], F32, name=f"a1_{e}")
-            x3 = keep.tile([P, 4, 2 * C], F32, name=f"a3_{e}")
-            a1_t.append(x1)
-            a3_t.append(x3)
+        a1_t = [keep.tile([P, 4, 2 * C], F32, name=f"a1_{h}") for h in range(2)]
+        a3_t = [keep.tile([P, 4, 2 * C], F32, name=f"a3_{h}") for h in range(2)]
+        pos_t = [keep.tile([P, T // 16], U16, name=f"pos_t{i}") for i in range(2)]
+        dx = [keep.tile([P, SLOTS], F32, name=f"dx{kt}") for kt in range(4)]
 
         def load_w2(e):
             nc.sync.dma_start(w2_t[e][:].bitcast(I32), w2_words[e].bitcast(I32).rearrange("s p c -> p s c"))
 
-        def load_a(e):
-            nc.scalar.dma_start(a1_t[e][:], a1.rearrange("(b p) j -> p b j", p=P)[:, :, 2 * C * e : 2 * C * (e + 1)])
-            nc.scalar.dma_start(a3_t[e][:], a3.rearrange("(b p) j -> p b j", p=P)[:, :, 2 * C * e : 2 * C * (e + 1)])
+        def load_a(h, queue):
+            for tile, src in ((a1_t[h], a1), (a3_t[h], a3)):
+                queue.dma_start(tile[:], src.rearrange("(p t) j -> p t j", t=4)[:, :, 2 * C * h : 2 * C * (h + 1)])
 
         def load_scales(pl, sc):
             for q in range(4):
@@ -104,79 +75,68 @@ def tile_moe_bdx_glu_relu_kernel(
                     sc.bitcast(I32).rearrange("e s f i -> f (e s) i")[4 * q : 4 * q + 4],
                 )
 
-        nc.scalar.dma_start(g0[:], gate[0:P, 0:CUT])
-        for i in range(S * 4):
-            (nc.scalar if i % 2 else nc.sync).dma_start(planes[i][:], dy_v[i // 4, i % 4])
-        nc.scalar.dma_start(g1[:], gate[0:P, CUT:SLOTS])
-        load_a(0)
+        nc.scalar.dma_start(gates[0][:], gate[0:P, 0:CUT])
+        for i in range(4 * S):
+            (nc.scalar if i % 2 else nc.sync).dma_start(planes[i][:, 0:T], dy_v[i // 4, i % 4])
+        load_a(0, nc.scalar)
         load_w2(0)
         load_scales(w2_pl, w2_scales)
+        nc.sync.dma_start(gates[1][:], gate[0:P, CUT:SLOTS])
         load_w2(1)
         for wt, ww in ((w1_t, w1_words), (w3_t, w3_words)):
             nc.sync.dma_start(wt[:].bitcast(I32), ww.bitcast(I32).rearrange("e s p c -> p (e s) c"))
         load_scales(w1_pl, w1_scales)
         load_scales(w3_pl, w3_scales)
         load_w2(2)
+        load_a(1, nc.sync)
         load_w2(3)
-        pos_t = []
-        for i, ps in enumerate((pos1, pos2)):
-            pp = keep.tile([P, T // 16], U16, name=f"pos_t{i}")
-            nc.sync.dma_start(pp[:], ps)
-            pos_t.append(pp)
+        for tile, src in zip(pos_t, (pos1, pos2)):
+            nc.sync.dma_start(tile[:], src)
 
-        dx = keep.tile([P, 4, SLOTS], F32, name="dx")
         gq, gs = {}, {}
-        gf, gb, rm, dh, dag, dq, ds = {}, {}, {}, {}, {}, {}, {}
+        gf, gb, rm, mk, dh, da, dht, dxp = {}, {}, {}, {}, {}, {}, {}, {}
+        ranges = ((0, CUT), (CUT, SLOTS))
 
-        def gather(c, s, t, lo, hi):
-            base = 2 * P * 3 // 2 * c
-            if (c, s) not in gf:
-                g = work.tile([P, 4, CUT], F32, name="gf", bufs=4)
-                gf[c, s] = g
+        def gather(c, s, t):
+            lo, hi = ranges[c]
+            if t == 0:
+                gf[c, s] = work.tile([P, 4, hi - lo], F32, name="gf", tag="gf", bufs=3)
             nc.vector.tensor_tensor(
-                gf[c, s][:, t, lo - base : hi - base],
-                planes[4 * s + t][:].indirect(offs_t[:, lo // 16 : hi // 16]),
-                g0[:, lo:hi] if c == 0 else g1[:, lo - CUT : hi - CUT],
-                MULT,
-            )
-            if t == 3:
-                at = lo
-                for a, b in PIECES:
-                    if a == at and b <= hi and (b == hi or b % C == 0):
-                        x = work.tile([P, C, 4], BF16, name="gb", bufs=7, align_bytes=64)
-                        nc.scalar.copy(
-                            x[:, 0 : b - a, :].rearrange("p (c i) t -> p c t i", i=4),
-                            gf[c, s][:, :, a - base : b - base].rearrange("p t (c i) -> p c t i", i=4),
-                        )
-                        gb[a, s] = x
-                        at = b
-                if (c, s) == (0, 2):
-                    load_a(1)
-
-        def quantize(lo, hi, s):
-            q = keep.tile([P, hi - lo], U32, name=f"gq{s}_{lo}", align_bytes=64)
-            z = keep.tile([P, hi - lo], U8, name=f"gs{s}_{lo}", align_bytes=64)
-            for i in range(lo // P, hi // P):
-                gq[i, s] = q[:, P * i - lo : P * i - lo + P]
-                gs[i, s] = z[:, P * i - lo : P * i - lo + P]
-            nc.vector.quantize_mx(
-                out=q[:].bitcast(FP8),
-                scales=z[:],
-                in_=gb[lo, s][:, 0 : hi - lo, :].rearrange("p c t -> p (c t)"),
+                gf[c, s][:, t, :], planes[4 * s + t][:].indirect(offs_t[:, lo // 16 : hi // 16]), gates[c][:], MULT
             )
 
-        def saved(i):
-            e, col = i // 4, P * (i % 4)
-            a1p = psum.tile([P, H], F32, name="a1p", bufs=1)
-            a3p = psum.tile([P, H], F32, name="a3p", bufs=1)
-            for b in range(4):
-                nc.tensor.transpose(a1p[:, P * b : P * (b + 1)], a1_t[e][:, b, col : col + P], ident[:])
-            for b in range(4):
-                nc.tensor.transpose(a3p[:, P * b : P * (b + 1)], a3_t[e][:, b, col : col + P], ident[:])
-            x = work.tile([P, 2, H], F32, name="rm", bufs=5)
-            nc.scalar.activation(x[:, 1, :], a1p[:], RELU)
-            nc.vector.scalar_tensor_tensor(x[:, 0, :], x[:, 1, :], 0.0, a3p[:], IS_GT, MULT)
-            rm[i] = x
+        def weave(c, s, a, b):
+            base = ranges[c][0]
+            x = work.tile([P, b - a, 4], BF16, name="gb", tag="gb", bufs=6, align_bytes=64)
+            nc.scalar.copy(
+                x[:].rearrange("p (c i) t -> p c t i", i=4),
+                gf[c, s][:, :, a - base : b - base].rearrange("p t (c i) -> p c t i", i=4),
+            )
+            gb[a, s] = x
+
+        def quantize(s, a, b):
+            q = keep.tile([P, b - a], U32, name=f"gq{s}_{a}", align_bytes=64)
+            z = keep.tile([P, b - a], U8, name=f"gs{s}_{a}", align_bytes=64)
+            for i in range(a // P, b // P):
+                gq[i, s] = q[:, P * i - a : P * i - a + P]
+                gs[i, s] = z[:, P * i - a : P * i - a + P]
+            nc.vector.quantize_mx(out=q[:].bitcast(FP8), scales=z[:], in_=gb[a, s][:].rearrange("p c t -> p (c t)"))
+
+        def saved(e):
+            h, cols = e // 2, slice(C * (e % 2), C * (e % 2 + 1))
+            x = work.tile([P, 2, C, 4], F32, name="rm", tag="rm", bufs=3)
+            y = work.tile([P, C * 4], BF16, name="mk", bufs=3)
+            nc.scalar.activation(
+                x[:, 1].rearrange("p (c i) t -> p c t i", i=4),
+                a1_t[h][:, :, cols].rearrange("p t (c i) -> p c t i", i=4),
+                RELU,
+            )
+            nc.scalar.copy(
+                x[:, 0].rearrange("p (c i) t -> p c t i", i=4),
+                a3_t[h][:, :, cols].rearrange("p t (c i) -> p c t i", i=4),
+            )
+            nc.scalar.activation(y[:], x[:, 1].rearrange("p c t -> p (c t)"), SIGN)
+            rm[e], mk[e] = x, y
 
         def first(i):
             e = i // 2
@@ -193,62 +153,110 @@ def tile_moe_bdx_glu_relu_kernel(
                 )
             dh[i] = acc
 
+        def turn(i):
+            x = work.tile([P, 4, P], F32, name="dhs", bufs=2)
+            nc.scalar.copy(x[:], dh[i][:].rearrange("j (p t) -> j t p", t=4))
+            y = psum.tile([P, 4, P], F32, name="dht", bufs=2)
+            for t in range(4):
+                nc.tensor.transpose(y[:, t, :], x[:, t, :], ident[:])
+            dht[i] = y
+
         def grads(i):
-            last = i == 7
-            da = work.tile([P, 2, H], BF16, name="da", bufs=3, align_bytes=64)
-            if last:
-                for w in range(2):
-                    nc.vector.tensor_tensor(da[:, w, :], dh[i][:], rm[i][:, w, :], MULT)
-            else:
-                nc.vector.tensor_tensor(da[:], dh[i][:].unsqueeze(1).to_broadcast([P, 2, H]), rm[i][:], MULT)
-            dap = psum.tile([P, 2, 2, P], F32, name="dap", bufs=2)
-            for w in range(2):
-                words = da[:, w, :].bitcast(F32)
-                for u in range(2):
-                    nc.tensor.transpose(dap[:, w, u, :], words[:, u:256:2], ident[:])
-            g = work.tile([P, 2 * P * 4], BF16, name="dag", bufs=3, align_bytes=64)
-            g_v = g[:].bitcast(F32).rearrange("p (w r u) -> p w r u", w=2, u=2)
-            dap_v = dap[:].rearrange("p w u r -> p w r u")
-            if last:
-                for w in range(2):
-                    nc.scalar.copy(g_v[:, w], dap_v[:, w])
-            else:
-                nc.scalar.copy(g_v, dap_v)
-            dag[i] = g
+            e, j = i // 2, i % 2
+            x = work.tile([P, 2, P, 4], BF16, name="da", bufs=3, align_bytes=64)
+            nc.vector.tensor_tensor(
+                x[:],
+                dht[i][:].rearrange("p t j -> p j t").unsqueeze(1).to_broadcast([P, 2, P, 4]),
+                rm[e][:, :, P * j : P * (j + 1), :],
+                MULT,
+            )
+            da[i] = x
+
+        def masked(i):
+            e, j = i // 2, i % 2
+            x = da[i][:, 0].rearrange("p j t -> p (j t)")
+            nc.vector.tensor_tensor(x, x, mk[e][:, H * j : H * (j + 1)], MULT)
 
         def second(i):
-            last = i == 7
+            e, j = i // 2, i % 2
             q = work.tile([P, 2 * P], U32, name="dq", bufs=3, align_bytes=64)
             z = work.tile([P, 2 * P], U8, name="ds", bufs=3, align_bytes=64)
-            for a, b in ((0, P), (P, 2 * P)) if last else ((0, 2 * P),):
-                nc.vector.quantize_mx(out=q[:, a:b].bitcast(FP8), scales=z[:, a:b], in_=dag[i][:, 4 * a : 4 * b])
-            dxp = psum.tile([P, 4, P], F32, name="dxp", bufs=2)
-            j0 = P * i
+            nc.vector.quantize_mx(out=q[:].bitcast(FP8), scales=z[:], in_=da[i][:].rearrange("p w j t -> p (w j t)"))
+            if j == 0:
+                dxp[e] = [psum.tile([P, 2, C], F32, name=f"dxp{b}", bufs=1) for b in range(2)]
             for kt in range(4):
+                acc = dxp[e][kt // 2][:, kt % 2, :]
                 for w, (wt, pl) in enumerate(((w1_t, w1_pl), (w3_t, w3_pl))):
                     nc.tensor.matmul_mx(
-                        out=dxp[:, kt, :],
-                        lhsT=wt[:, i // 2, 256 * kt : 256 * (kt + 1)].bitcast(FP4),
-                        lhsT_scale=pl[:, i // 2, P * kt : P * (kt + 1)],
+                        out=acc[:, P * j : P * (j + 1)],
+                        lhsT=wt[:, e, 256 * kt : 256 * (kt + 1)].bitcast(FP4),
+                        lhsT_scale=pl[:, e, P * kt : P * (kt + 1)],
                         rhs=q[:, P * w : P * (w + 1)].bitcast(FP8),
                         rhs_scale=z[:, P * w : P * (w + 1)],
                         start=(w == 0),
                         stop=(w == 1),
                     )
-                if last:
-                    nc.scalar.copy(dx[:, kt, j0 : j0 + P], dxp[:, kt, :])
-            if not last:
-                nc.scalar.copy(dx[:, :, j0 : j0 + P], dxp[:])
+            if j == 1:
+                for kt in range(4):
+                    nc.scalar.copy(dx[kt][:, C * e : C * (e + 1)], dxp[e][kt // 2][:, kt % 2, :])
 
-        steps = {"g": gather, "q": quantize, "m": saved, "dh": first, "da": grads, "dq": second}
-        for step in PROGRAM:
-            steps[step[0]](*step[1:])
+        def pieces(c):
+            lo, hi = ranges[c]
+            cuts = [lo] + list(range(lo // C * C + C, hi, C)) + [hi]
+            return list(zip(cuts, cuts[1:]))
 
-        for kt in range(4):
-            o1 = work.tile([P, T], F32, name="o1", bufs=2)
-            o2 = work.tile([P, T], F32, name="o2", bufs=2)
-            o = work.tile([P, T], F32, name="o", bufs=2)
-            nc.vector.tensor_copy(o1[:], dx[:, kt, :].indirect(pos_t[0][:]))
-            nc.vector.tensor_copy(o2[:], dx[:, kt, :].indirect(pos_t[1][:]))
-            (nc.vector if kt == 3 else nc.gpsimd).tensor_tensor(o[:], o1[:], o2[:], ADD)
+        stages = (first, turn, grads, masked, second)
+
+        def step(n):
+            for d, stage in enumerate(stages):
+                if 0 <= n - d < TILES:
+                    stage(n - d)
+
+        def run(c, between):
+            waiting = []
+            for s in range(S):
+                for t in range(4):
+                    gather(c, s, t)
+                    if t >= 1 and waiting:
+                        quantize(*waiting.pop(0))
+                    between(4 * s + t)
+                for w in waiting:
+                    quantize(*w)
+                waiting = []
+                for a, b in pieces(c):
+                    weave(c, s, a, b)
+                    waiting.append((s, a, b))
+            return waiting
+
+        head = CUT // P
+        left = run(0, lambda n: saved(n // 2 - 3) if n in (6, 8, 10) else None)
+
+        def between(n):
+            if n < len(left):
+                quantize(*left[n])
+            if n >= 2 and n % 2 == 0 and n // 2 - 1 < head:
+                step(n // 2 - 1)
+            if n == 10:
+                saved(E - 1)
+
+        for w in run(1, between):
+            quantize(*w)
+        for n in range(head, TILES + len(stages) - 1):
+            step(n)
+
+        o1 = {}
+
+        def fetch(kt):
+            o1[kt] = work.tile([P, T], F32, name="o1", tag="gf", bufs=3)
+            nc.vector.tensor_copy(o1[kt][:], dx[kt][:].indirect(pos_t[0][:]))
+
+        def combine(kt):
+            o = work.tile([P, T], F32, name="o", tag="rm", bufs=3)
+            nc.vector.tensor_tensor(o[:], dx[kt][:].indirect(pos_t[1][:]), o1[kt][:], ADD)
             nc.sync.dma_start(out[P * kt : P * (kt + 1), :], o[:])
+
+        fetch(0)
+        for kt in range(4):
+            if kt < 3:
+                fetch(kt + 1)
+            combine(kt)

@@ -9,6 +9,9 @@ S = N // 512
 SLOTS = E * C
 TILES = SLOTS // P
 CUT = 640
+EARLY = 6
+RM = 8
+AFTER = {1: 0, 2: 2}
 WINDOW = max(CUT, SLOTS - CUT, T - 16) + 16
 
 FLOPS = 2 * SLOTS * (N * H + 2 * H * K)
@@ -56,39 +59,41 @@ def tile_moe_bdx_glu_relu_kernel(
         w2_t = [keep.tile([P, S, 2 * H], U8, name=f"w2_{e}", align_bytes=64) for e in range(E)]
         w1_t = keep.tile([P, E, 2 * K], U8, name="w1_t", align_bytes=64)
         w3_t = keep.tile([P, E, 2 * K], U8, name="w3_t", align_bytes=64)
-        a1_t = [keep.tile([P, 4, 2 * C], F32, name=f"a1_{h}") for h in range(2)]
-        a3_t = [keep.tile([P, 4, 2 * C], F32, name=f"a3_{h}") for h in range(2)]
+        a1_t, a3_t = {}, {}
         pos_t = [keep.tile([P, T // 16], U16, name=f"pos_t{i}") for i in range(2)]
         dx = [keep.tile([P, SLOTS], F32, name=f"dx{kt}") for kt in range(4)]
 
         def load_w2(e):
             nc.sync.dma_start(w2_t[e][:].bitcast(I32), w2_words[e].bitcast(I32).rearrange("s p c -> p s c"))
 
-        def load_a(h, queue):
-            for tile, src in ((a1_t[h], a1), (a3_t[h], a3)):
-                queue.dma_start(tile[:], src.rearrange("(p t) j -> p t j", t=4)[:, :, 2 * C * h : 2 * C * (h + 1)])
+        def load_a(e):
+            a1_t[e] = work.tile([P, 4, C], F32, name="a1_t", bufs=2)
+            a3_t[e] = work.tile([P, 4, C], F32, name="a3_t", bufs=2)
+            for tile, src in ((a1_t[e], a1), (a3_t[e], a3)):
+                nc.scalar.dma_start(tile[:], src.rearrange("(p t) j -> p t j", t=4)[:, :, C * e : C * (e + 1)])
 
-        def load_scales(pl, sc):
-            for q in range(4):
-                nc.sync.dma_start(
-                    pl[32 * q : 32 * q + 4].bitcast(I32),
-                    sc.bitcast(I32).rearrange("e s f i -> f (e s) i")[4 * q : 4 * q + 4],
-                )
+        def load_scales(pl, sc, q):
+            nc.sync.dma_start(
+                pl[32 * q : 32 * q + 4].bitcast(I32),
+                sc.bitcast(I32).rearrange("e s f i -> f (e s) i")[4 * q : 4 * q + 4],
+            )
 
         nc.scalar.dma_start(gates[0][:], gate[0:P, 0:CUT])
+        load_a(0)
+        load_a(1)
+        nc.scalar.dma_start(gates[1][:], gate[0:P, CUT:SLOTS])
         for i in range(4 * S):
-            (nc.scalar if i % 2 else nc.sync).dma_start(planes[i][:, 0:T], dy_v[i // 4, i % 4])
-        load_a(0, nc.scalar)
+            nc.sync.dma_start(planes[i][:, 0:T], dy_v[i // 4, i % 4])
+            if i >= 8:
+                load_scales(w2_pl, w2_scales, i - 8)
         load_w2(0)
-        load_scales(w2_pl, w2_scales)
-        nc.sync.dma_start(gates[1][:], gate[0:P, CUT:SLOTS])
         load_w2(1)
         for wt, ww in ((w1_t, w1_words), (w3_t, w3_words)):
             nc.sync.dma_start(wt[:].bitcast(I32), ww.bitcast(I32).rearrange("e s p c -> p (e s) c"))
-        load_scales(w1_pl, w1_scales)
-        load_scales(w3_pl, w3_scales)
+        for q in range(4):
+            load_scales(w1_pl, w1_scales, q)
+            load_scales(w3_pl, w3_scales, q)
         load_w2(2)
-        load_a(1, nc.sync)
         load_w2(3)
         for tile, src in zip(pos_t, (pos1, pos2)):
             nc.sync.dma_start(tile[:], src)
@@ -97,17 +102,29 @@ def tile_moe_bdx_glu_relu_kernel(
         gf, gb, rm, mk, dh, da, dht, dxp = {}, {}, {}, {}, {}, {}, {}, {}
         ranges = ((0, CUT), (CUT, SLOTS))
 
+        rest = SLOTS - CUT
+        shared = keep.tile([P, 4 * rest], F32, name="shared", align_bytes=64)
+
         def gather(c, s, t):
             lo, hi = ranges[c]
             if t == 0:
-                gf[c, s] = work.tile([P, 4, hi - lo], F32, name="gf", tag="gf", bufs=3)
+                if (c, s) == (1, 0):
+                    gf[c, s] = shared[:].rearrange("p (t j) -> p t j", t=4)
+                elif c == 1:
+                    gf[c, s] = work.tile([P, 4, hi - lo], F32, name="gf", tag=f"rm{AFTER[s]}", bufs=1)
+                else:
+                    gf[c, s] = work.tile([P, 4, hi - lo], F32, name="gf", tag="gf", bufs=2)
             nc.vector.tensor_tensor(
                 gf[c, s][:, t, :], planes[4 * s + t][:].indirect(offs_t[:, lo // 16 : hi // 16]), gates[c][:], MULT
             )
 
         def weave(c, s, a, b):
             base = ranges[c][0]
-            x = work.tile([P, b - a, 4], BF16, name="gb", tag="gb", bufs=6, align_bytes=64)
+            if (c, s) == (0, S - 1) and b < CUT:
+                at = rest * (1 if a == 0 else 2)
+                x = shared[:, at : at + 2 * (b - a)].bitcast(BF16).rearrange("p (j t) -> p j t", t=4)
+            else:
+                x = work.tile([P, b - a, 4], BF16, name="gb", tag="gb", bufs=4, align_bytes=64)
             nc.scalar.copy(
                 x[:].rearrange("p (c i) t -> p c t i", i=4),
                 gf[c, s][:, :, a - base : b - base].rearrange("p t (c i) -> p c t i", i=4),
@@ -122,10 +139,10 @@ def tile_moe_bdx_glu_relu_kernel(
                 gs[i, s] = z[:, P * i - a : P * i - a + P]
             nc.vector.quantize_mx(out=q[:].bitcast(FP8), scales=z[:], in_=gb[a, s][:].rearrange("p c t -> p (c t)"))
 
-        def saved(e):
-            h, cols = e // 2, slice(C * (e % 2), C * (e % 2 + 1))
-            x = work.tile([P, 2, C, 4], F32, name="rm", tag="rm", bufs=3)
-            y = work.tile([P, C * 4], BF16, name="mk", bufs=3)
+        def saved(i):
+            h, cols = i // 2, slice(P * (i % 2), P * (i % 2 + 1))
+            x = work.tile([P, 2, P, 4], F32, name="rm", tag=f"rm{i % RM}", bufs=1)
+            y = work.tile([P, H], BF16, name="mk", bufs=RM)
             nc.scalar.activation(
                 x[:, 1].rearrange("p (c i) t -> p c t i", i=4),
                 a1_t[h][:, :, cols].rearrange("p t (c i) -> p c t i", i=4),
@@ -136,11 +153,13 @@ def tile_moe_bdx_glu_relu_kernel(
                 a3_t[h][:, :, cols].rearrange("p t (c i) -> p c t i", i=4),
             )
             nc.scalar.activation(y[:], x[:, 1].rearrange("p c t -> p (c t)"), SIGN)
-            rm[e], mk[e] = x, y
+            rm[i], mk[i] = x, y
+            if i % 2 == 1 and h + 2 < E:
+                load_a(h + 2)
 
         def first(i):
             e = i // 2
-            acc = psum.tile([P, H], F32, name="dh", bufs=2)
+            acc = psum.tile([P, H], F32, name="dh", bufs=4)
             for s in range(S):
                 nc.tensor.matmul_mx(
                     out=acc[:],
@@ -162,20 +181,18 @@ def tile_moe_bdx_glu_relu_kernel(
             dht[i] = y
 
         def grads(i):
-            e, j = i // 2, i % 2
-            x = work.tile([P, 2, P, 4], BF16, name="da", bufs=3, align_bytes=64)
+            x = work.tile([P, 2, P, 4], BF16, name="da", bufs=4, align_bytes=64)
             nc.vector.tensor_tensor(
                 x[:],
                 dht[i][:].rearrange("p t j -> p j t").unsqueeze(1).to_broadcast([P, 2, P, 4]),
-                rm[e][:, :, P * j : P * (j + 1), :],
+                rm[i][:],
                 MULT,
             )
             da[i] = x
 
         def masked(i):
-            e, j = i // 2, i % 2
             x = da[i][:, 0].rearrange("p j t -> p (j t)")
-            nc.vector.tensor_tensor(x, x, mk[e][:, H * j : H * (j + 1)], MULT)
+            nc.vector.tensor_tensor(x, x, mk[i][:], MULT)
 
         def second(i):
             e, j = i // 2, i % 2
@@ -200,9 +217,14 @@ def tile_moe_bdx_glu_relu_kernel(
                 for kt in range(4):
                     nc.scalar.copy(dx[kt][:, C * e : C * (e + 1)], dxp[e][kt // 2][:, kt % 2, :])
 
-        def pieces(c):
+        def pieces(c, s):
             lo, hi = ranges[c]
-            cuts = [lo] + list(range(lo // C * C + C, hi, C)) + [hi]
+            if s < S - 1:
+                cuts = [lo, (lo // 512 + 1) * 512 if c == 0 else lo + P, hi]
+            elif c == 0:
+                cuts = [lo] + list(range(lo + P, hi, C)) + [hi]
+            else:
+                cuts = list(range(lo, hi + 1, P))
             return list(zip(cuts, cuts[1:]))
 
         stages = (first, turn, grads, masked, second)
@@ -211,47 +233,43 @@ def tile_moe_bdx_glu_relu_kernel(
             for d, stage in enumerate(stages):
                 if 0 <= n - d < TILES:
                     stage(n - d)
+            if EARLY <= n + 4 < TILES:
+                saved(n + 4)
 
-        def run(c, between):
-            waiting = []
-            for s in range(S):
-                for t in range(4):
-                    gather(c, s, t)
-                    if t >= 1 and waiting:
-                        quantize(*waiting.pop(0))
-                    between(4 * s + t)
-                for w in waiting:
-                    quantize(*w)
-                waiting = []
-                for a, b in pieces(c):
-                    weave(c, s, a, b)
-                    waiting.append((s, a, b))
-            return waiting
+        def sweep(c, s):
+            for t in range(4):
+                gather(c, s, t)
 
-        head = CUT // P
-        left = run(0, lambda n: saved(n // 2 - 3) if n in (6, 8, 10) else None)
+        def pack(c, s):
+            for a, b in pieces(c, s):
+                weave(c, s, a, b)
+                quantize(s, a, b)
 
-        def between(n):
-            if n < len(left):
-                quantize(*left[n])
-            if n >= 2 and n % 2 == 0 and n // 2 - 1 < head:
-                step(n // 2 - 1)
-            if n == 10:
-                saved(E - 1)
-
-        for w in run(1, between):
-            quantize(*w)
-        for n in range(head, TILES + len(stages) - 1):
+        for s in range(S):
+            saved(2 * s)
+            saved(2 * s + 1)
+            sweep(0, s)
+            pack(0, s)
+        sweep(1, 0)
+        done = 0
+        for s in (1, 2):
+            for n in range(done, AFTER[s] + 3):
+                step(n)
+            done = AFTER[s] + 3
+            pack(1, s - 1)
+            sweep(1, s)
+        pack(1, S - 1)
+        for n in range(done, TILES + len(stages) - 1):
             step(n)
 
         o1 = {}
 
         def fetch(kt):
-            o1[kt] = work.tile([P, T], F32, name="o1", tag="gf", bufs=3)
+            o1[kt] = work.tile([P, T], F32, name="o1", bufs=3)
             nc.vector.tensor_copy(o1[kt][:], dx[kt][:].indirect(pos_t[0][:]))
 
         def combine(kt):
-            o = work.tile([P, T], F32, name="o", tag="rm", bufs=3)
+            o = work.tile([P, T], F32, name="o", tag=f"rm{4 + kt}", bufs=1)
             nc.vector.tensor_tensor(o[:], dx[kt][:].indirect(pos_t[1][:]), o1[kt][:], ADD)
             nc.sync.dma_start(out[P * kt : P * (kt + 1), :], o[:])
 

@@ -10,6 +10,7 @@ SLOTS = E * C
 TILES = SLOTS // P
 CUT = 640
 EARLY = 6
+LAST = 384
 RM = 8
 AFTER = {1: 0, 2: 2}
 WINDOW = max(CUT, SLOTS - CUT, T - 16) + 16
@@ -81,11 +82,11 @@ def tile_moe_bdx_glu_relu_kernel(
         nc.scalar.dma_start(gates[0][:], gate[0:P, 0:CUT])
         load_a(0)
         load_a(1)
-        nc.scalar.dma_start(gates[1][:], gate[0:P, CUT:SLOTS])
         for i in range(4 * S):
             nc.sync.dma_start(planes[i][:, 0:T], dy_v[i // 4, i % 4])
             if i >= 8:
                 load_scales(w2_pl, w2_scales, i - 8)
+        nc.sync.dma_start(gates[1][:], gate[0:P, CUT:SLOTS])
         load_w2(0)
         load_w2(1)
         for wt, ww in ((w1_t, w1_words), (w3_t, w3_words)):
@@ -174,17 +175,19 @@ def tile_moe_bdx_glu_relu_kernel(
 
         def turn(i):
             x = work.tile([P, 4, P], F32, name="dhs", bufs=2)
-            nc.scalar.copy(x[:], dh[i][:].rearrange("j (p t) -> j t p", t=4))
-            y = psum.tile([P, 4, P], F32, name="dht", bufs=2)
+            nc.scalar.copy(
+                x[:].rearrange("j t (c i) -> j c t i", i=4), dh[i][:].rearrange("j (c i t) -> j c t i", i=4, t=4)
+            )
+            y = psum.tile([P, P, 4], F32, name="dht", bufs=2)
             for t in range(4):
-                nc.tensor.transpose(y[:, t, :], x[:, t, :], ident[:])
+                nc.tensor.transpose(y[:, :, t], x[:, t, :], ident[:])
             dht[i] = y
 
         def grads(i):
             x = work.tile([P, 2, P, 4], BF16, name="da", bufs=4, align_bytes=64)
             nc.vector.tensor_tensor(
                 x[:],
-                dht[i][:].rearrange("p t j -> p j t").unsqueeze(1).to_broadcast([P, 2, P, 4]),
+                dht[i][:].unsqueeze(1).to_broadcast([P, 2, P, 4]),
                 rm[i][:],
                 MULT,
             )
@@ -199,13 +202,17 @@ def tile_moe_bdx_glu_relu_kernel(
             q = work.tile([P, 2 * P], U32, name="dq", bufs=3, align_bytes=64)
             z = work.tile([P, 2 * P], U8, name="ds", bufs=3, align_bytes=64)
             nc.vector.quantize_mx(out=q[:].bitcast(FP8), scales=z[:], in_=da[i][:].rearrange("p w j t -> p (w j t)"))
-            if j == 0:
-                dxp[e] = [psum.tile([P, 2, C], F32, name=f"dxp{b}", bufs=1) for b in range(2)]
+            last = i == TILES - 1
+            if last:
+                accs = [psum.tile([P, P], F32, name="dxl", tag="dh", bufs=4)[:] for kt in range(4)]
+            else:
+                if j == 0:
+                    dxp[e] = [psum.tile([P, 2, C], F32, name=f"dxp{b}", bufs=1) for b in range(2)]
+                accs = [dxp[e][kt // 2][:, kt % 2, P * j : P * (j + 1)] for kt in range(4)]
             for kt in range(4):
-                acc = dxp[e][kt // 2][:, kt % 2, :]
                 for w, (wt, pl) in enumerate(((w1_t, w1_pl), (w3_t, w3_pl))):
                     nc.tensor.matmul_mx(
-                        out=acc[:, P * j : P * (j + 1)],
+                        out=accs[kt],
                         lhsT=wt[:, e, 256 * kt : 256 * (kt + 1)].bitcast(FP4),
                         lhsT_scale=pl[:, e, P * kt : P * (kt + 1)],
                         rhs=q[:, P * w : P * (w + 1)].bitcast(FP8),
@@ -213,8 +220,10 @@ def tile_moe_bdx_glu_relu_kernel(
                         start=(w == 0),
                         stop=(w == 1),
                     )
-            if j == 1:
-                for kt in range(4):
+            for kt in range(4):
+                if e == E - 1:
+                    nc.scalar.copy(dx[kt][:, P * i : P * (i + 1)], accs[kt])
+                elif j == 1:
                     nc.scalar.copy(dx[kt][:, C * e : C * (e + 1)], dxp[e][kt // 2][:, kt % 2, :])
 
         def pieces(c, s):
@@ -270,8 +279,11 @@ def tile_moe_bdx_glu_relu_kernel(
 
         def combine(kt):
             o = work.tile([P, T], F32, name="o", tag=f"rm{4 + kt}", bufs=1)
-            nc.vector.tensor_tensor(o[:], dx[kt][:].indirect(pos_t[1][:]), o1[kt][:], ADD)
-            nc.sync.dma_start(out[P * kt : P * (kt + 1), :], o[:])
+            for a, b in ((0, LAST), (LAST, T)) if kt == 3 else ((0, T),):
+                nc.vector.tensor_tensor(
+                    o[:, a:b], dx[kt][:].indirect(pos_t[1][:, a // 16 : b // 16]), o1[kt][:, a:b], ADD
+                )
+                nc.sync.dma_start(out[P * kt : P * (kt + 1), a:b], o[:, a:b])
 
         fetch(0)
         for kt in range(4):

@@ -11,6 +11,7 @@ TILES = SLOTS // P
 CUT = 640
 EARLY = 6
 LAST = 384
+HALF = SLOTS // 2
 RM = 8
 AFTER = {1: 0, 2: 2}
 WINDOW = max(CUT, SLOTS - CUT, T - 16) + 16
@@ -62,38 +63,40 @@ def tile_moe_bdx_glu_relu_kernel(
         w3_t = keep.tile([P, E, 2 * K], U8, name="w3_t", align_bytes=64)
         a1_t, a3_t = {}, {}
         pos_t = [keep.tile([P, T // 16], U16, name=f"pos_t{i}") for i in range(2)]
-        dx = [keep.tile([P, SLOTS], F32, name=f"dx{kt}") for kt in range(4)]
+        dx = []
 
         def load_w2(e):
             nc.sync.dma_start(w2_t[e][:].bitcast(I32), w2_words[e].bitcast(I32).rearrange("s p c -> p s c"))
 
-        def load_a(e):
-            a1_t[e] = work.tile([P, 4, C], F32, name="a1_t", bufs=2)
-            a3_t[e] = work.tile([P, 4, C], F32, name="a3_t", bufs=2)
+        def load_a(e, queue):
+            a1_t[e] = work.tile([P, 4, C], F32, name="a1_t", tag=f"a1_{e}", bufs=1)
+            a3_t[e] = work.tile([P, 4, C], F32, name="a3_t", tag=f"a3_{e}", bufs=1)
             for tile, src in ((a1_t[e], a1), (a3_t[e], a3)):
-                nc.scalar.dma_start(tile[:], src.rearrange("(p t) j -> p t j", t=4)[:, :, C * e : C * (e + 1)])
+                queue.dma_start(tile[:], src.rearrange("(p t) j -> p t j", t=4)[:, :, C * e : C * (e + 1)])
 
-        def load_scales(pl, sc, q):
-            nc.sync.dma_start(
+        def load_scales(pl, sc, q, queue):
+            queue.dma_start(
                 pl[32 * q : 32 * q + 4].bitcast(I32),
                 sc.bitcast(I32).rearrange("e s f i -> f (e s) i")[4 * q : 4 * q + 4],
             )
 
         nc.scalar.dma_start(gates[0][:], gate[0:P, 0:CUT])
-        load_a(0)
-        load_a(1)
+        load_a(0, nc.scalar)
+        for q in range(4):
+            load_scales(w2_pl, w2_scales, q, nc.gpsimd)
         for i in range(4 * S):
             nc.sync.dma_start(planes[i][:, 0:T], dy_v[i // 4, i % 4])
-            if i >= 8:
-                load_scales(w2_pl, w2_scales, i - 8)
-        nc.sync.dma_start(gates[1][:], gate[0:P, CUT:SLOTS])
+            if i in (5, 9):
+                load_a(i // 4, nc.sync)
         load_w2(0)
+        nc.sync.dma_start(gates[1][:], gate[0:P, CUT:SLOTS])
         load_w2(1)
+        load_a(3, nc.sync)
         for wt, ww in ((w1_t, w1_words), (w3_t, w3_words)):
             nc.sync.dma_start(wt[:].bitcast(I32), ww.bitcast(I32).rearrange("e s p c -> p (e s) c"))
         for q in range(4):
-            load_scales(w1_pl, w1_scales, q)
-            load_scales(w3_pl, w3_scales, q)
+            load_scales(w1_pl, w1_scales, q, nc.sync)
+            load_scales(w3_pl, w3_scales, q, nc.sync)
         load_w2(2)
         load_w2(3)
         for tile, src in zip(pos_t, (pos1, pos2)):
@@ -124,13 +127,19 @@ def tile_moe_bdx_glu_relu_kernel(
             if (c, s) == (0, S - 1) and b < CUT:
                 at = rest * (1 if a == 0 else 2)
                 x = shared[:, at : at + 2 * (b - a)].bitcast(BF16).rearrange("p (j t) -> p j t", t=4)
+                gb[a, s] = x
+            elif s < S - 1 and a == CUT:
+                x = gb[HALF, s][:, CUT - HALF :, :]
+            elif s < S - 1 and a == HALF:
+                gb[a, s] = keep.tile([P, HALF, 4], BF16, name=f"gb_late{s}", align_bytes=64)
+                x = gb[a, s][:, 0 : CUT - HALF, :]
             else:
-                x = work.tile([P, b - a, 4], BF16, name="gb", tag="gb", bufs=4, align_bytes=64)
+                x = work.tile([P, b - a, 4], BF16, name="gb", tag="gb", bufs=3, align_bytes=64)
+                gb[a, s] = x
             nc.scalar.copy(
                 x[:].rearrange("p (c i) t -> p c t i", i=4),
                 gf[c, s][:, :, a - base : b - base].rearrange("p t (c i) -> p c t i", i=4),
             )
-            gb[a, s] = x
 
         def quantize(s, a, b):
             q = keep.tile([P, b - a], U32, name=f"gq{s}_{a}", align_bytes=64)
@@ -155,8 +164,9 @@ def tile_moe_bdx_glu_relu_kernel(
             )
             nc.scalar.activation(y[:], x[:, 1].rearrange("p c t -> p (c t)"), SIGN)
             rm[i], mk[i] = x, y
-            if i % 2 == 1 and h + 2 < E:
-                load_a(h + 2)
+            if i in (1, 3):
+                for name in ("a1", "a3"):
+                    dx.append(work.tile([P, SLOTS], F32, name="dx", tag=f"{name}_{h}", bufs=1))
 
         def first(i):
             e = i // 2
@@ -178,16 +188,16 @@ def tile_moe_bdx_glu_relu_kernel(
             nc.scalar.copy(
                 x[:].rearrange("j t (c i) -> j c t i", i=4), dh[i][:].rearrange("j (c i t) -> j c t i", i=4, t=4)
             )
-            y = psum.tile([P, P, 4], F32, name="dht", bufs=2)
+            y = psum.tile([P, 4, P], F32, name="dht", bufs=2)
             for t in range(4):
-                nc.tensor.transpose(y[:, :, t], x[:, t, :], ident[:])
+                nc.tensor.transpose(y[:, t, :], x[:, t, :], ident[:])
             dht[i] = y
 
         def grads(i):
             x = work.tile([P, 2, P, 4], BF16, name="da", bufs=4, align_bytes=64)
             nc.vector.tensor_tensor(
                 x[:],
-                dht[i][:].unsqueeze(1).to_broadcast([P, 2, P, 4]),
+                dht[i][:].rearrange("p t j -> p j t").unsqueeze(1).to_broadcast([P, 2, P, 4]),
                 rm[i][:],
                 MULT,
             )
@@ -226,14 +236,9 @@ def tile_moe_bdx_glu_relu_kernel(
                 elif j == 1:
                     nc.scalar.copy(dx[kt][:, C * e : C * (e + 1)], dxp[e][kt // 2][:, kt % 2, :])
 
-        def pieces(c, s):
+        def pieces(c):
             lo, hi = ranges[c]
-            if s < S - 1:
-                cuts = [lo, (lo // 512 + 1) * 512 if c == 0 else lo + P, hi]
-            elif c == 0:
-                cuts = [lo] + list(range(lo + P, hi, C)) + [hi]
-            else:
-                cuts = list(range(lo, hi + 1, P))
+            cuts = [lo] + list(range(lo + P, hi, C if c == 0 else P)) + [hi]
             return list(zip(cuts, cuts[1:]))
 
         stages = (first, turn, grads, masked, second)
@@ -250,9 +255,17 @@ def tile_moe_bdx_glu_relu_kernel(
                 gather(c, s, t)
 
         def pack(c, s):
-            for a, b in pieces(c, s):
-                weave(c, s, a, b)
-                quantize(s, a, b)
+            if s == S - 1:
+                for a, b in pieces(c):
+                    weave(c, s, a, b)
+                    quantize(s, a, b)
+            elif c == 0:
+                weave(c, s, 0, HALF)
+                quantize(s, 0, HALF)
+                weave(c, s, HALF, CUT)
+            else:
+                weave(c, s, CUT, SLOTS)
+                quantize(s, HALF, SLOTS)
 
         for s in range(S):
             saved(2 * s)
@@ -262,10 +275,11 @@ def tile_moe_bdx_glu_relu_kernel(
         sweep(1, 0)
         done = 0
         for s in (1, 2):
-            for n in range(done, AFTER[s] + 3):
+            for n in range(done, AFTER[s] + 2):
                 step(n)
-            done = AFTER[s] + 3
             pack(1, s - 1)
+            step(AFTER[s] + 2)
+            done = AFTER[s] + 3
             sweep(1, s)
         pack(1, S - 1)
         for n in range(done, TILES + len(stages) - 1):

@@ -7,14 +7,17 @@ K, T, E, C, H, N = 512, 512, 4, 256, 512, 1536
 P = 128
 S = N // 512
 SLOTS = E * C
+HALF = SLOTS // 2
 TILES = SLOTS // P
 CUT = 640
-EARLY = 6
-LAST = 384
-HALF = SLOTS // 2
-RM = 8
+REST = SLOTS - CUT
+RANGES = ((0, CUT), (CUT, SLOTS))
+WINDOW = CUT + 16
 AFTER = {1: 0, 2: 2}
-WINDOW = max(CUT, SLOTS - CUT, T - 16) + 16
+EARLY = 2 * S
+AHEAD = 4
+PAIRED = 2
+LAST = 384
 
 FLOPS = 2 * SLOTS * (N * H + 2 * H * K)
 BYTES = 11210752
@@ -45,259 +48,277 @@ def tile_moe_bdx_glu_relu_kernel(
         offs_t = keep.tile([P, SLOTS // 16], U16, name="offs_t")
         nc.sync.dma_start(offs_t[:], offs)
 
-        planes = [keep.tile([P, WINDOW], F32, name=f"plane{i}") for i in range(4 * S)]
-        for pt in planes:
-            nc.vector.memset(pt[:, T:WINDOW], 0.0)
-        w2_pl = keep.tile([P, E * S, H], U8, name="w2_pl", align_bytes=64)
-        w1_pl = keep.tile([P, E, K], U8, name="w1_pl", align_bytes=64)
-        w3_pl = keep.tile([P, E, K], U8, name="w3_pl", align_bytes=64)
+        planes = [keep.tile([P, WINDOW], F32, name=f"plane{row}") for row in range(4 * S)]
+        for plane in planes:
+            nc.vector.memset(plane[:, T:WINDOW], 0.0)
+        w2_sc = keep.tile([P, E * S, H], U8, name="w2_sc", align_bytes=64)
+        w1_sc = keep.tile([P, E, K], U8, name="w1_sc", align_bytes=64)
+        w3_sc = keep.tile([P, E, K], U8, name="w3_sc", align_bytes=64)
         ident = keep.tile([P, P], F32, name="ident")
         make_identity(nc, ident[:])
-        for pl in (w2_pl, w1_pl, w3_pl):
-            nc.gpsimd.memset(pl[:].rearrange("p a b -> p (a b)").bitcast(I32), 0)
+        for sc in (w2_sc, w1_sc, w3_sc):
+            nc.gpsimd.memset(sc[:].rearrange("p pas col -> p (pas col)").bitcast(I32), 0)
 
-        dy_v = dyT.rearrange("(s p t) c -> s t p c", p=P, t=4)
-        gates = [keep.tile([P, CUT], F32, name="gate_a"), keep.tile([P, SLOTS - CUT], F32, name="gate_b")]
+        dy_rows = dyT.rearrange("(s p t) token -> s t p token", p=P, t=4)
+        gates = [keep.tile([P, hi - lo], F32, name=f"gate{c}") for c, (lo, hi) in enumerate(RANGES)]
         w2_t = [keep.tile([P, S, 2 * H], U8, name=f"w2_{e}", align_bytes=64) for e in range(E)]
         w1_t = keep.tile([P, E, 2 * K], U8, name="w1_t", align_bytes=64)
         w3_t = keep.tile([P, E, 2 * K], U8, name="w3_t", align_bytes=64)
+        pos_t = [keep.tile([P, T // 16], U16, name=f"pos_t{r}") for r in range(2)]
         a1_t, a3_t = {}, {}
-        pos_t = [keep.tile([P, T // 16], U16, name=f"pos_t{i}") for i in range(2)]
-        dx = []
+
+        def load_gate(c, queue):
+            queue.dma_start(gates[c][:], gate[0:P, RANGES[c][0] : RANGES[c][1]])
 
         def load_w2(e):
-            nc.sync.dma_start(w2_t[e][:].bitcast(I32), w2_words[e].bitcast(I32).rearrange("s p c -> p s c"))
+            nc.sync.dma_start(w2_t[e][:].bitcast(I32), w2_words[e].bitcast(I32).rearrange("s p col -> p s col"))
 
-        def load_a(e, queue):
+        def load_saved(e, queue):
             a1_t[e] = work.tile([P, 4, C], F32, name="a1_t", tag=f"a1_{e}", bufs=1)
             a3_t[e] = work.tile([P, 4, C], F32, name="a3_t", tag=f"a3_{e}", bufs=1)
             for tile, src in ((a1_t[e], a1), (a3_t[e], a3)):
-                queue.dma_start(tile[:], src.rearrange("(p t) j -> p t j", t=4)[:, :, C * e : C * (e + 1)])
+                queue.dma_start(tile[:], src.rearrange("(p t) x -> p t x", t=4)[:, :, C * e : C * (e + 1)])
 
-        def load_scales(pl, sc, q, queue):
+        def load_scales(sc, src, q, queue):
             queue.dma_start(
-                pl[32 * q : 32 * q + 4].bitcast(I32),
-                sc.bitcast(I32).rearrange("e s f i -> f (e s) i")[4 * q : 4 * q + 4],
+                sc[32 * q : 32 * q + 4].bitcast(I32),
+                src.bitcast(I32).rearrange("e s f col -> f (e s) col")[4 * q : 4 * q + 4],
             )
 
-        nc.scalar.dma_start(gates[0][:], gate[0:P, 0:CUT])
-        load_a(0, nc.scalar)
+        load_gate(0, nc.scalar)
+        load_saved(0, nc.scalar)
         for q in range(4):
-            load_scales(w2_pl, w2_scales, q, nc.gpsimd)
-        for i in range(4 * S):
-            nc.sync.dma_start(planes[i][:, 0:T], dy_v[i // 4, i % 4])
-            if i in (5, 9):
-                load_a(i // 4, nc.sync)
+            load_scales(w2_sc, w2_scales, q, nc.gpsimd)
+        for s in range(S):
+            for t in range(4):
+                nc.sync.dma_start(planes[4 * s + t][:, 0:T], dy_rows[s, t])
+                if s > 0 and t == 1:
+                    load_saved(s, nc.sync)
         load_w2(0)
-        nc.sync.dma_start(gates[1][:], gate[0:P, CUT:SLOTS])
+        load_gate(1, nc.sync)
         load_w2(1)
-        load_a(3, nc.sync)
-        for wt, ww in ((w1_t, w1_words), (w3_t, w3_words)):
-            nc.sync.dma_start(wt[:].bitcast(I32), ww.bitcast(I32).rearrange("e s p c -> p (e s) c"))
+        load_saved(E - 1, nc.sync)
+        for tile, src in ((w1_t, w1_words), (w3_t, w3_words)):
+            nc.sync.dma_start(tile[:].bitcast(I32), src.bitcast(I32).rearrange("e s p col -> p (e s) col"))
         for q in range(4):
-            load_scales(w1_pl, w1_scales, q, nc.sync)
-            load_scales(w3_pl, w3_scales, q, nc.sync)
+            load_scales(w1_sc, w1_scales, q, nc.sync)
+            load_scales(w3_sc, w3_scales, q, nc.sync)
         load_w2(2)
         load_w2(3)
         for tile, src in zip(pos_t, (pos1, pos2)):
             nc.sync.dma_start(tile[:], src)
 
-        gq, gs = {}, {}
-        gf, gb, rm, mk, dh, da, dht, dxp = {}, {}, {}, {}, {}, {}, {}, {}
-        ranges = ((0, CUT), (CUT, SLOTS))
+        g_raw, g_woven, g_codes, g_scales = {}, {}, {}, {}
+        factors, relu_mask, dh, dh_turned, da, da_codes, da_scales, dx_banks = {}, {}, {}, {}, {}, {}, {}, {}
+        dx = []
 
-        rest = SLOTS - CUT
-        shared = keep.tile([P, 4 * rest], F32, name="shared", align_bytes=64)
+        shared = keep.tile([P, 4 * REST], F32, name="shared", align_bytes=64)
 
-        def gather(c, s, t):
-            lo, hi = ranges[c]
-            if t == 0:
-                if (c, s) == (1, 0):
-                    gf[c, s] = shared[:].rearrange("p (t j) -> p t j", t=4)
-                elif c == 1:
-                    gf[c, s] = work.tile([P, 4, hi - lo], F32, name="gf", tag=f"rm{AFTER[s]}", bufs=1)
-                else:
-                    gf[c, s] = work.tile([P, 4, hi - lo], F32, name="gf", tag="gf", bufs=2)
-            nc.vector.tensor_tensor(
-                gf[c, s][:, t, :], planes[4 * s + t][:].indirect(offs_t[:, lo // 16 : hi // 16]), gates[c][:], MULT
-            )
+        def gather(c, s):
+            lo, hi = RANGES[c]
+            if c == 0:
+                g_raw[c, s] = work.tile([P, 4, CUT], F32, name="g_raw", tag="g_raw", bufs=2)
+            elif s == 0:
+                g_raw[c, s] = shared[:].rearrange("p (t x) -> p t x", t=4)
+            else:
+                g_raw[c, s] = work.tile([P, 4, REST], F32, name="g_late", tag=f"factors{AFTER[s]}", bufs=1)
+            for t in range(4):
+                nc.vector.tensor_tensor(
+                    g_raw[c, s][:, t, :],
+                    planes[4 * s + t][:].indirect(offs_t[:, lo // 16 : hi // 16]),
+                    gates[c][:],
+                    MULT,
+                )
 
         def weave(c, s, a, b):
-            base = ranges[c][0]
+            base = RANGES[c][0]
             if (c, s) == (0, S - 1) and b < CUT:
-                at = rest * (1 if a == 0 else 2)
-                x = shared[:, at : at + 2 * (b - a)].bitcast(BF16).rearrange("p (j t) -> p j t", t=4)
-                gb[a, s] = x
+                at = REST * (1 if a == 0 else 2)
+                woven = shared[:, at : at + 2 * (b - a)].bitcast(BF16).rearrange("p (x t) -> p x t", t=4)
+                g_woven[a, s] = woven
             elif s < S - 1 and a == CUT:
-                x = gb[HALF, s][:, CUT - HALF :, :]
+                woven = g_woven[HALF, s][:, CUT - HALF :, :]
             elif s < S - 1 and a == HALF:
-                gb[a, s] = keep.tile([P, HALF, 4], BF16, name=f"gb_late{s}", align_bytes=64)
-                x = gb[a, s][:, 0 : CUT - HALF, :]
+                g_woven[a, s] = keep.tile([P, HALF, 4], BF16, name=f"g_upper{s}", align_bytes=64)
+                woven = g_woven[a, s][:, 0 : CUT - HALF, :]
             else:
-                x = work.tile([P, b - a, 4], BF16, name="gb", tag="gb", bufs=3, align_bytes=64)
-                gb[a, s] = x
+                woven = work.tile([P, b - a, 4], BF16, name="g_woven", tag="g_woven", bufs=3, align_bytes=64)
+                g_woven[a, s] = woven
             nc.scalar.copy(
-                x[:].rearrange("p (c i) t -> p c t i", i=4),
-                gf[c, s][:, :, a - base : b - base].rearrange("p t (c i) -> p c t i", i=4),
+                woven[:].rearrange("p (g r) t -> p g t r", r=4),
+                g_raw[c, s][:, :, a - base : b - base].rearrange("p t (g r) -> p g t r", r=4),
             )
 
-        def quantize(s, a, b):
-            q = keep.tile([P, b - a], U32, name=f"gq{s}_{a}", align_bytes=64)
-            z = keep.tile([P, b - a], U8, name=f"gs{s}_{a}", align_bytes=64)
-            for i in range(a // P, b // P):
-                gq[i, s] = q[:, P * i - a : P * i - a + P]
-                gs[i, s] = z[:, P * i - a : P * i - a + P]
-            nc.vector.quantize_mx(out=q[:].bitcast(FP8), scales=z[:], in_=gb[a, s][:].rearrange("p c t -> p (c t)"))
+        def quantize_g(s, a, b):
+            codes = keep.tile([P, b - a], U32, name=f"g_codes{s}_{a}", align_bytes=64)
+            scales = keep.tile([P, b - a], U8, name=f"g_scales{s}_{a}", align_bytes=64)
+            for m in range(a // P, b // P):
+                g_codes[m, s] = codes[:, P * m - a : P * m - a + P]
+                g_scales[m, s] = scales[:, P * m - a : P * m - a + P]
+            nc.vector.quantize_mx(
+                out=codes[:].bitcast(FP8), scales=scales[:], in_=g_woven[a, s][:].rearrange("p x t -> p (x t)")
+            )
 
-        def saved(i):
-            h, cols = i // 2, slice(P * (i % 2), P * (i % 2 + 1))
-            x = work.tile([P, 2, P, 4], F32, name="rm", tag=f"rm{i % RM}", bufs=1)
-            y = work.tile([P, H], BF16, name="mk", bufs=RM)
+        def pack(c, s):
+            lo, hi = RANGES[c]
+            if s == S - 1:
+                cuts = [lo] + list(range(lo + P, hi, C if c == 0 else P)) + [hi]
+                for a, b in zip(cuts, cuts[1:]):
+                    weave(c, s, a, b)
+                    quantize_g(s, a, b)
+            elif c == 0:
+                weave(c, s, 0, HALF)
+                quantize_g(s, 0, HALF)
+                weave(c, s, HALF, CUT)
+            else:
+                weave(c, s, CUT, SLOTS)
+                quantize_g(s, HALF, SLOTS)
+
+        def saved(m):
+            e, cols = m // 2, slice(P * (m % 2), P * (m % 2 + 1))
+            factors[m] = work.tile([P, 2, P, 4], F32, name="factors", tag=f"factors{m}", bufs=1)
+            if m % 2 == 0:
+                relu_mask[e] = work.tile([P, 2, H], BF16, name="relu_mask", bufs=E)
             nc.scalar.activation(
-                x[:, 1].rearrange("p (c i) t -> p c t i", i=4),
-                a1_t[h][:, :, cols].rearrange("p t (c i) -> p c t i", i=4),
+                factors[m][:, 1].rearrange("p (g r) t -> p g t r", r=4),
+                a1_t[e][:, :, cols].rearrange("p t (g r) -> p g t r", r=4),
                 RELU,
             )
             nc.scalar.copy(
-                x[:, 0].rearrange("p (c i) t -> p c t i", i=4),
-                a3_t[h][:, :, cols].rearrange("p t (c i) -> p c t i", i=4),
+                factors[m][:, 0].rearrange("p (g r) t -> p g t r", r=4),
+                a3_t[e][:, :, cols].rearrange("p t (g r) -> p g t r", r=4),
             )
-            nc.scalar.activation(y[:], x[:, 1].rearrange("p c t -> p (c t)"), SIGN)
-            rm[i], mk[i] = x, y
-            if i in (1, 3):
+            nc.scalar.activation(relu_mask[e][:, m % 2, :], factors[m][:, 1].rearrange("p x t -> p (x t)"), SIGN)
+            if m % 2 == 1 and e < 2:
                 for name in ("a1", "a3"):
-                    dx.append(work.tile([P, SLOTS], F32, name="dx", tag=f"{name}_{h}", bufs=1))
+                    dx.append(work.tile([P, SLOTS], F32, name="dx", tag=f"{name}_{e}", bufs=1))
 
-        def first(i):
-            e = i // 2
-            acc = psum.tile([P, H], F32, name="dh", bufs=4)
+        def first(m):
+            e = m // 2
+            dh[m] = psum.tile([P, H], F32, name="dh", bufs=4)
             for s in range(S):
                 nc.tensor.matmul_mx(
-                    out=acc[:],
-                    lhsT=gq[i, s].bitcast(FP8),
-                    lhsT_scale=gs[i, s],
+                    out=dh[m][:],
+                    lhsT=g_codes[m, s].bitcast(FP8),
+                    lhsT_scale=g_scales[m, s],
                     rhs=w2_t[e][:, s, :].bitcast(FP4),
-                    rhs_scale=w2_pl[:, S * e + s, :],
+                    rhs_scale=w2_sc[:, S * e + s, :],
                     start=(s == 0),
                     stop=(s == S - 1),
                 )
-            dh[i] = acc
 
-        def turn(i):
-            x = work.tile([P, 4, P], F32, name="dhs", bufs=2)
+        def turn(m):
+            sorted_dh = work.tile([P, 4, P], F32, name="sorted_dh", bufs=2)
             nc.scalar.copy(
-                x[:].rearrange("j t (c i) -> j c t i", i=4), dh[i][:].rearrange("j (c i t) -> j c t i", i=4, t=4)
+                sorted_dh[:].rearrange("x t (g r) -> x g t r", r=4),
+                dh[m][:].rearrange("x (g r t) -> x g t r", r=4, t=4),
             )
-            y = psum.tile([P, 4, P], F32, name="dht", bufs=2)
+            dh_turned[m] = psum.tile([P, 4, P], F32, name="dh_turned", bufs=2)
             for t in range(4):
-                nc.tensor.transpose(y[:, t, :], x[:, t, :], ident[:])
-            dht[i] = y
+                nc.tensor.transpose(dh_turned[m][:, t, :], sorted_dh[:, t, :], ident[:])
 
-        def grads(i):
-            x = work.tile([P, 2, P, 4], BF16, name="da", bufs=4, align_bytes=64)
+        def products(m):
+            e, j = m // 2, m % 2
+            if j == 0:
+                da[e] = work.tile([P, 2, 2, P, 4], BF16, name="da", bufs=3, align_bytes=64)
+                da_codes[e] = keep.tile([P, 4 * P], U32, name=f"da_codes{e}", align_bytes=64)
+                da_scales[e] = keep.tile([P, 4 * P], U8, name=f"da_scales{e}", align_bytes=64)
             nc.vector.tensor_tensor(
-                x[:],
-                dht[i][:].rearrange("p t j -> p j t").unsqueeze(1).to_broadcast([P, 2, P, 4]),
-                rm[i][:],
+                da[e][:, j],
+                dh_turned[m][:].rearrange("p t x -> p x t").unsqueeze(1).to_broadcast([P, 2, P, 4]),
+                factors[m][:],
                 MULT,
             )
-            da[i] = x
 
-        def masked(i):
-            x = da[i][:, 0].rearrange("p j t -> p (j t)")
-            nc.vector.tensor_tensor(x, x, mk[i][:], MULT)
+        def group(m):
+            if m // 2 < PAIRED:
+                return range(2 * (m % 2))
+            return range(m % 2, m % 2 + 1)
 
-        def second(i):
-            e, j = i // 2, i % 2
-            q = work.tile([P, 2 * P], U32, name="dq", bufs=3, align_bytes=64)
-            z = work.tile([P, 2 * P], U8, name="ds", bufs=3, align_bytes=64)
-            nc.vector.quantize_mx(out=q[:].bitcast(FP8), scales=z[:], in_=da[i][:].rearrange("p w j t -> p (w j t)"))
-            last = i == TILES - 1
-            if last:
-                accs = [psum.tile([P, P], F32, name="dxl", tag="dh", bufs=4)[:] for kt in range(4)]
-            else:
-                if j == 0:
-                    dxp[e] = [psum.tile([P, 2, C], F32, name=f"dxp{b}", bufs=1) for b in range(2)]
-                accs = [dxp[e][kt // 2][:, kt % 2, P * j : P * (j + 1)] for kt in range(4)]
+        def quantize_da(e, a, b):
+            nc.vector.quantize_mx(
+                out=da_codes[e][:, P * a : P * b].bitcast(FP8),
+                scales=da_scales[e][:, P * a : P * b],
+                in_=da[e][:].rearrange("p j w x t -> p (j w x t)")[:, H * a : H * b],
+            )
+
+        def masked(m):
+            e, tiles = m // 2, group(m)
+            if m == TILES - 1:
+                quantize_da(e, 3, 4)
+            if tiles:
+                da1 = da[e][:, tiles.start : tiles.stop, 0].rearrange("p j x t -> p j (x t)")
+                nc.vector.tensor_tensor(da1, da1, relu_mask[e][:, tiles.start : tiles.stop, :], MULT)
+
+        def second(m):
+            e, tiles = m // 2, group(m)
+            if tiles:
+                quantize_da(e, 2 * tiles.start, 2 * tiles.stop - (1 if m == TILES - 1 else 0))
+            for j in tiles:
+                back(e, j)
+
+        def back(e, j):
+            if j == 0 and e == E - 1:
+                dx_banks[e] = [psum.tile([P, C], F32, name="dx_last", tag="dh", bufs=4)[:] for kt in range(4)]
+            elif j == 0:
+                pairs = [psum.tile([P, 2, C], F32, name=f"dx_pair{b}", bufs=1) for b in range(2)]
+                dx_banks[e] = [pairs[kt // 2][:, kt % 2, :] for kt in range(4)]
             for kt in range(4):
-                for w, (wt, pl) in enumerate(((w1_t, w1_pl), (w3_t, w3_pl))):
+                for w, words, sc in ((1, w3_t, w3_sc), (0, w1_t, w1_sc)):
                     nc.tensor.matmul_mx(
-                        out=accs[kt],
-                        lhsT=wt[:, e, 256 * kt : 256 * (kt + 1)].bitcast(FP4),
-                        lhsT_scale=pl[:, e, P * kt : P * (kt + 1)],
-                        rhs=q[:, P * w : P * (w + 1)].bitcast(FP8),
-                        rhs_scale=z[:, P * w : P * (w + 1)],
-                        start=(w == 0),
-                        stop=(w == 1),
+                        out=dx_banks[e][kt][:, P * j : P * (j + 1)],
+                        lhsT=words[:, e, 2 * P * kt : 2 * P * (kt + 1)].bitcast(FP4),
+                        lhsT_scale=sc[:, e, P * kt : P * (kt + 1)],
+                        rhs=da_codes[e][:, P * (2 * j + w) : P * (2 * j + w + 1)].bitcast(FP8),
+                        rhs_scale=da_scales[e][:, P * (2 * j + w) : P * (2 * j + w + 1)],
+                        start=(w == 1),
+                        stop=(w == 0),
                     )
-            for kt in range(4):
-                if e == E - 1:
-                    nc.scalar.copy(dx[kt][:, P * i : P * (i + 1)], accs[kt])
-                elif j == 1:
-                    nc.scalar.copy(dx[kt][:, C * e : C * (e + 1)], dxp[e][kt // 2][:, kt % 2, :])
+            if j == 1:
+                for kt in range(4):
+                    nc.scalar.copy(dx[kt][:, C * e : C * (e + 1)], dx_banks[e][kt])
 
-        def pieces(c):
-            lo, hi = ranges[c]
-            cuts = [lo] + list(range(lo + P, hi, C if c == 0 else P)) + [hi]
-            return list(zip(cuts, cuts[1:]))
-
-        stages = (first, turn, grads, masked, second)
+        stages = (first, turn, products, masked, second)
+        lag = stages.index(products)
 
         def step(n):
             for d, stage in enumerate(stages):
                 if 0 <= n - d < TILES:
                     stage(n - d)
-            if EARLY <= n + 4 < TILES:
-                saved(n + 4)
-
-        def sweep(c, s):
-            for t in range(4):
-                gather(c, s, t)
-
-        def pack(c, s):
-            if s == S - 1:
-                for a, b in pieces(c):
-                    weave(c, s, a, b)
-                    quantize(s, a, b)
-            elif c == 0:
-                weave(c, s, 0, HALF)
-                quantize(s, 0, HALF)
-                weave(c, s, HALF, CUT)
-            else:
-                weave(c, s, CUT, SLOTS)
-                quantize(s, HALF, SLOTS)
+            if EARLY <= n + AHEAD < TILES:
+                saved(n + AHEAD)
 
         for s in range(S):
             saved(2 * s)
             saved(2 * s + 1)
-            sweep(0, s)
+            gather(0, s)
             pack(0, s)
-        sweep(1, 0)
+        gather(1, 0)
         done = 0
-        for s in (1, 2):
-            for n in range(done, AFTER[s] + 2):
+        for s in sorted(AFTER):
+            for n in range(done, AFTER[s] + lag):
                 step(n)
             pack(1, s - 1)
-            step(AFTER[s] + 2)
-            done = AFTER[s] + 3
-            sweep(1, s)
+            step(AFTER[s] + lag)
+            done = AFTER[s] + lag + 1
+            gather(1, s)
         pack(1, S - 1)
         for n in range(done, TILES + len(stages) - 1):
             step(n)
 
-        o1 = {}
+        by_pos1 = {}
 
         def fetch(kt):
-            o1[kt] = work.tile([P, T], F32, name="o1", bufs=3)
-            nc.vector.tensor_copy(o1[kt][:], dx[kt][:].indirect(pos_t[0][:]))
+            by_pos1[kt] = work.tile([P, T], F32, name="by_pos1", bufs=3)
+            nc.vector.tensor_copy(by_pos1[kt][:], dx[kt][:].indirect(pos_t[0][:]))
 
         def combine(kt):
-            o = work.tile([P, T], F32, name="o", tag=f"rm{4 + kt}", bufs=1)
+            total = work.tile([P, T], F32, name="total", tag=f"factors{TILES - 4 + kt}", bufs=1)
             for a, b in ((0, LAST), (LAST, T)) if kt == 3 else ((0, T),):
                 nc.vector.tensor_tensor(
-                    o[:, a:b], dx[kt][:].indirect(pos_t[1][:, a // 16 : b // 16]), o1[kt][:, a:b], ADD
+                    total[:, a:b], dx[kt][:].indirect(pos_t[1][:, a // 16 : b // 16]), by_pos1[kt][:, a:b], ADD
                 )
-                nc.sync.dma_start(out[P * kt : P * (kt + 1), a:b], o[:, a:b])
+                nc.sync.dma_start(out[P * kt : P * (kt + 1), a:b], total[:, a:b])
 
         fetch(0)
         for kt in range(4):

@@ -15,7 +15,8 @@ RANGES = ((0, CUT), (CUT, SLOTS))
 WINDOW = CUT + 16
 AFTER = {1: 0, 2: 2}
 EARLY = 2 * S
-AHEAD = 4
+HOME = (0, 1, 2, 3, 4, 5, 1, 0)
+AHEAD = 3
 PAIRED = 2
 LAST = 384
 
@@ -73,11 +74,9 @@ def tile_moe_bdx_glu_relu_kernel(
         def load_w2(e):
             nc.sync.dma_start(w2_t[e][:].bitcast(I32), w2_words[e].bitcast(I32).rearrange("s p col -> p s col"))
 
-        def load_saved(e, queue):
-            a1_t[e] = work.tile([P, 4, C], F32, name="a1_t", tag=f"a1_{e}", bufs=1)
-            a3_t[e] = work.tile([P, 4, C], F32, name="a3_t", tag=f"a3_{e}", bufs=1)
-            for tile, src in ((a1_t[e], a1), (a3_t[e], a3)):
-                queue.dma_start(tile[:], src.rearrange("(p t) x -> p t x", t=4)[:, :, C * e : C * (e + 1)])
+        def load_saved(e, name, src, tiles):
+            tiles[e] = work.tile([P, 4, C], F32, name=name, tag=f"{name}_{e}", bufs=1)
+            nc.sync.dma_start(tiles[e][:], src.rearrange("(p t) x -> p t x", t=4)[:, :, C * e : C * (e + 1)])
 
         def load_scales(sc, src, q, queue):
             queue.dma_start(
@@ -86,18 +85,21 @@ def tile_moe_bdx_glu_relu_kernel(
             )
 
         load_gate(0, nc.scalar)
-        load_saved(0, nc.scalar)
         for q in range(4):
             load_scales(w2_sc, w2_scales, q, nc.gpsimd)
         for s in range(S):
             for t in range(4):
                 nc.sync.dma_start(planes[4 * s + t][:, 0:T], dy_rows[s, t])
-                if s > 0 and t == 1:
-                    load_saved(s, nc.sync)
-        load_w2(0)
+                if t == 2 and s < S - 1:
+                    load_saved(s, "a1", a1, a1_t)
+                if t == (3 if s < S - 1 else 2):
+                    load_saved(s, "a3", a3, a3_t)
         load_gate(1, nc.sync)
+        load_w2(0)
+        load_saved(S - 1, "a1", a1, a1_t)
         load_w2(1)
-        load_saved(E - 1, nc.sync)
+        load_saved(E - 1, "a1", a1, a1_t)
+        load_saved(E - 1, "a3", a3, a3_t)
         for tile, src in ((w1_t, w1_words), (w3_t, w3_words)):
             nc.sync.dma_start(tile[:].bitcast(I32), src.bitcast(I32).rearrange("e s p col -> p (e s) col"))
         for q in range(4):
@@ -174,19 +176,22 @@ def tile_moe_bdx_glu_relu_kernel(
                 weave(c, s, CUT, SLOTS)
                 quantize_g(s, HALF, SLOTS)
 
-        def saved(m):
+        def saved_a3(m):
             e, cols = m // 2, slice(P * (m % 2), P * (m % 2 + 1))
-            factors[m] = work.tile([P, 2, P, 4], F32, name="factors", tag=f"factors{m}", bufs=1)
+            factors[m] = work.tile([P, 2, P, 4], F32, name="factors", tag=f"factors{HOME[m]}", bufs=1)
+            nc.scalar.copy(
+                factors[m][:, 0].rearrange("p (g r) t -> p g t r", r=4),
+                a3_t[e][:, :, cols].rearrange("p t (g r) -> p g t r", r=4),
+            )
+
+        def saved_a1(m):
+            e, cols = m // 2, slice(P * (m % 2), P * (m % 2 + 1))
             if m % 2 == 0:
                 relu_mask[e] = work.tile([P, 2, H], BF16, name="relu_mask", bufs=E)
             nc.scalar.activation(
                 factors[m][:, 1].rearrange("p (g r) t -> p g t r", r=4),
                 a1_t[e][:, :, cols].rearrange("p t (g r) -> p g t r", r=4),
                 RELU,
-            )
-            nc.scalar.copy(
-                factors[m][:, 0].rearrange("p (g r) t -> p g t r", r=4),
-                a3_t[e][:, :, cols].rearrange("p t (g r) -> p g t r", r=4),
             )
             nc.scalar.activation(relu_mask[e][:, m % 2, :], factors[m][:, 1].rearrange("p x t -> p (x t)"), SIGN)
             if m % 2 == 1 and e < 2:
@@ -285,12 +290,16 @@ def tile_moe_bdx_glu_relu_kernel(
             for d, stage in enumerate(stages):
                 if 0 <= n - d < TILES:
                     stage(n - d)
-            if EARLY <= n + AHEAD < TILES:
-                saved(n + AHEAD)
+            if 6 <= n + AHEAD < TILES:
+                saved_a3(n + AHEAD)
+            if 4 <= n + AHEAD < TILES:
+                saved_a1(n + AHEAD)
 
         for s in range(S):
-            saved(2 * s)
-            saved(2 * s + 1)
+            for m in (2 * s, 2 * s + 1):
+                saved_a3(m)
+                if s < S - 1:
+                    saved_a1(m)
             gather(0, s)
             pack(0, s)
         gather(1, 0)
@@ -313,7 +322,7 @@ def tile_moe_bdx_glu_relu_kernel(
             nc.vector.tensor_copy(by_pos1[kt][:], dx[kt][:].indirect(pos_t[0][:]))
 
         def combine(kt):
-            total = work.tile([P, T], F32, name="total", tag=f"factors{TILES - 4 + kt}", bufs=1)
+            total = work.tile([P, T], F32, name="total", tag=f"factors{HOME[TILES - 4 + kt]}", bufs=1)
             for a, b in ((0, LAST), (LAST, T)) if kt == 3 else ((0, T),):
                 nc.vector.tensor_tensor(
                     total[:, a:b], dx[kt][:].indirect(pos_t[1][:, a // 16 : b // 16]), by_pos1[kt][:, a:b], ADD

@@ -78,15 +78,16 @@ def tile_moe_bdx_glu_relu_kernel(
             tiles[e] = work.tile([P, 4, C], F32, name=name, tag=f"{name}_{e}", bufs=1)
             nc.sync.dma_start(tiles[e][:], src.rearrange("(p t) x -> p t x", t=4)[:, :, C * e : C * (e + 1)])
 
-        def load_scales(sc, src, q, queue):
+        def load_scales(sc, src, q, queue, passes=slice(None)):
             queue.dma_start(
-                sc[32 * q : 32 * q + 4].bitcast(I32),
-                src.bitcast(I32).rearrange("e s f col -> f (e s) col")[4 * q : 4 * q + 4],
+                sc[32 * q : 32 * q + 4, passes].bitcast(I32),
+                src.bitcast(I32).rearrange("e s f col -> f (e s) col")[4 * q : 4 * q + 4, passes],
             )
 
         load_gate(0, nc.scalar)
-        for q in range(4):
-            load_scales(w2_sc, w2_scales, q, nc.gpsimd)
+        for first_e, last_e in ((2, E), (0, 2)):
+            for q in (0, 2, 1, 3):
+                load_scales(w2_sc, w2_scales, q, nc.gpsimd, slice(S * first_e, S * last_e))
         for s in range(S):
             for t in range(4):
                 nc.sync.dma_start(planes[4 * s + t][:, 0:T], dy_rows[s, t])

@@ -18,6 +18,7 @@ EARLY = 2 * S
 HOME = (0, 1, 2, 3, 4, 5, 1, 0)
 AHEAD = 3
 PAIRED = 2
+FIRST = 256
 LAST = 384
 
 FLOPS = 2 * SLOTS * (N * H + 2 * H * K)
@@ -84,21 +85,26 @@ def tile_moe_bdx_glu_relu_kernel(
                 src.bitcast(I32).rearrange("e s f col -> f (e s) col")[4 * q : 4 * q + 4, passes],
             )
 
-        load_gate(0, nc.scalar)
-        for first_e, last_e in ((2, E), (0, 2)):
+        nc.scalar.dma_start(gates[0][:, 0:FIRST], gate[0:P, 0:FIRST])
+        for first_e, last_e in ((0, 2), (2, E)):
             for q in (0, 2, 1, 3):
                 load_scales(w2_sc, w2_scales, q, nc.gpsimd, slice(S * first_e, S * last_e))
+            if first_e == 0:
+                load_gate(1, nc.gpsimd)
         for s in range(S):
             for t in range(4):
                 nc.sync.dma_start(planes[4 * s + t][:, 0:T], dy_rows[s, t])
-                if t == 2 and s < S - 1:
+                if (s, t) == (0, 0):
+                    nc.sync.dma_start(gates[0][:, FIRST:CUT], gate[0:P, FIRST:CUT])
+                if 4 * s + t in (2, 5):
                     load_saved(s, "a1", a1, a1_t)
-                if t == (3 if s < S - 1 else 2):
-                    load_saved(s, "a3", a3, a3_t)
-        load_gate(1, nc.sync)
+                if 4 * s + t in (7, 9):
+                    load_saved(s - 1 if t == 1 else 0, "a3", a3, a3_t)
         load_w2(0)
-        load_saved(S - 1, "a1", a1, a1_t)
         load_w2(1)
+        load_saved(S - 1, "a3", a3, a3_t)
+        load_saved(S - 1, "a1", a1, a1_t)
+        load_w2(2)
         load_saved(E - 1, "a1", a1, a1_t)
         load_saved(E - 1, "a3", a3, a3_t)
         for tile, src in ((w1_t, w1_words), (w3_t, w3_words)):
@@ -106,13 +112,13 @@ def tile_moe_bdx_glu_relu_kernel(
         for q in range(4):
             load_scales(w1_sc, w1_scales, q, nc.sync)
             load_scales(w3_sc, w3_scales, q, nc.sync)
-        load_w2(2)
         load_w2(3)
         for tile, src in zip(pos_t, (pos1, pos2)):
             nc.sync.dma_start(tile[:], src)
 
         g_raw, g_woven, g_codes, g_scales = {}, {}, {}, {}
         factors, relu_mask, dh, dh_turned, da, da_codes, da_scales, dx_banks = {}, {}, {}, {}, {}, {}, {}, {}
+        held = []
         dx = []
 
         shared = keep.tile([P, 4 * REST], F32, name="shared", align_bytes=64)
@@ -126,12 +132,13 @@ def tile_moe_bdx_glu_relu_kernel(
             else:
                 g_raw[c, s] = work.tile([P, 4, REST], F32, name="g_late", tag=f"factors{AFTER[s]}", bufs=1)
             for t in range(4):
-                nc.vector.tensor_tensor(
-                    g_raw[c, s][:, t, :],
-                    planes[4 * s + t][:].indirect(offs_t[:, lo // 16 : hi // 16]),
-                    gates[c][:],
-                    MULT,
-                )
+                for a, b in ((0, FIRST), (FIRST, CUT)) if (c, s, t) == (0, 0, 0) else ((lo, hi),):
+                    nc.vector.tensor_tensor(
+                        g_raw[c, s][:, t, a - lo : b - lo],
+                        planes[4 * s + t][:].indirect(offs_t[:, a // 16 : b // 16]),
+                        gates[c][:, a - lo : b - lo],
+                        MULT,
+                    )
 
         def weave(c, s, a, b):
             base = RANGES[c][0]
@@ -144,6 +151,11 @@ def tile_moe_bdx_glu_relu_kernel(
             elif s < S - 1 and a == HALF:
                 g_woven[a, s] = keep.tile([P, HALF, 4], BF16, name=f"g_upper{s}", align_bytes=64)
                 woven = g_woven[a, s][:, 0 : CUT - HALF, :]
+            elif c == 1:
+                if a == CUT:
+                    held.append(work.tile([P, REST * 4], BF16, name="g_held", tag="hold", bufs=1, align_bytes=64))
+                woven = held[0][:, 4 * (a - CUT) : 4 * (b - CUT)].rearrange("p (x t) -> p x t", t=4)
+                g_woven[a, s] = woven
             else:
                 woven = work.tile([P, b - a, 4], BF16, name="g_woven", tag="g_woven", bufs=3, align_bytes=64)
                 g_woven[a, s] = woven
@@ -214,7 +226,12 @@ def tile_moe_bdx_glu_relu_kernel(
                 )
 
         def turn(m):
-            sorted_dh = work.tile([P, 4, P], F32, name="sorted_dh", bufs=2)
+            if m < 2:
+                sorted_dh = work.tile([P, 4, P], F32, name="sorted_first", tag=f"factors{4 + m}", bufs=1)
+            elif m == CUT // P - 1:
+                sorted_dh = work.tile([P, 4, P], F32, name="sorted_last", tag="hold", bufs=1, align_bytes=64)
+            else:
+                sorted_dh = work.tile([P, 4, P], F32, name="sorted_dh", bufs=2)
             nc.scalar.copy(
                 sorted_dh[:].rearrange("x t (g r) -> x g t r", r=4),
                 dh[m][:].rearrange("x (g r t) -> x g t r", r=4, t=4),
@@ -289,17 +306,16 @@ def tile_moe_bdx_glu_relu_kernel(
 
         def step(n):
             for d, stage in enumerate(stages):
-                if 0 <= n - d < TILES:
+                if 0 <= n - d < TILES and (stage, n - d) != (turn, CUT // P - 1):
                     stage(n - d)
-            if 6 <= n + AHEAD < TILES:
-                saved_a3(n + AHEAD)
             if 4 <= n + AHEAD < TILES:
+                saved_a3(n + AHEAD)
                 saved_a1(n + AHEAD)
 
         for s in range(S):
             for m in (2 * s, 2 * s + 1):
-                saved_a3(m)
                 if s < S - 1:
+                    saved_a3(m)
                     saved_a1(m)
             gather(0, s)
             pack(0, s)
@@ -312,6 +328,7 @@ def tile_moe_bdx_glu_relu_kernel(
             step(AFTER[s] + lag)
             done = AFTER[s] + lag + 1
             gather(1, s)
+        turn(CUT // P - 1)
         pack(1, S - 1)
         for n in range(done, TILES + len(stages) - 1):
             step(n)

@@ -267,18 +267,20 @@ def tile_moe_bdx_glu_relu_kernel(
 
         def masked(m):
             e, tiles = m // 2, group(m)
-            if m == TILES - 1:
-                quantize_da(e, 3, 4)
             if tiles:
                 da1 = da[e][:, tiles.start : tiles.stop, 0].rearrange("p j x t -> p j (x t)")
                 nc.vector.tensor_tensor(da1, da1, relu_mask[e][:, tiles.start : tiles.stop, :], MULT)
+            if m == TILES - 1:
+                quantize_da(e, 3, 4)
 
         def second(m):
             e, tiles = m // 2, group(m)
             if tiles:
                 quantize_da(e, 2 * tiles.start, 2 * tiles.stop - (1 if m == TILES - 1 else 0))
-            for j in tiles:
-                back(e, j)
+
+        def third(m):
+            for j in group(m):
+                back(m // 2, j)
 
         def back(e, j):
             if j == 0 and e == E - 1:
@@ -301,11 +303,11 @@ def tile_moe_bdx_glu_relu_kernel(
                 for kt in range(4):
                     nc.scalar.copy(dx[kt][:, C * e : C * (e + 1)], dx_banks[e][kt])
 
-        stages = (first, turn, products, masked, second)
+        stages = (first, turn, products, second, masked, third)
         lag = stages.index(products)
 
         def step(n):
-            for d, stage in enumerate(stages):
+            for d, stage in zip((0, 1, 2, 3, 2, 4), stages):
                 if 0 <= n - d < TILES and (stage, n - d) != (turn, CUT // P - 1):
                     stage(n - d)
             if 4 <= n + AHEAD < TILES:

@@ -12,11 +12,14 @@ TILES = SLOTS // P
 CUT = 640
 REST = SLOTS - CUT
 RANGES = ((0, CUT), (CUT, SLOTS))
-WINDOW = CUT + 16
+WINDOW = CUT + 1
 AFTER = {1: 0, 2: 2}
-EARLY = 2 * S
-HOME = (0, 1, 2, 3, 4, 5, 1, 0)
+EARLY = 4
 AHEAD = 3
+HOME = (0, 1, 2, 3, 4, 5, 1, 0)
+END = CUT // P - 1
+A1_BEHIND = (2, 5)
+A3_BEHIND = (7, 9)
 PAIRED = 2
 FIRST = 256
 LAST = 384
@@ -69,8 +72,8 @@ def tile_moe_bdx_glu_relu_kernel(
         pos_t = [keep.tile([P, T // 16], U16, name=f"pos_t{r}") for r in range(2)]
         a1_t, a3_t = {}, {}
 
-        def load_gate(c, queue):
-            queue.dma_start(gates[c][:], gate[0:P, RANGES[c][0] : RANGES[c][1]])
+        def load_gate(c, a, b, queue):
+            queue.dma_start(gates[c][:, a - RANGES[c][0] : b - RANGES[c][0]], gate[0:P, a:b])
 
         def load_w2(e):
             nc.sync.dma_start(w2_t[e][:].bitcast(I32), w2_words[e].bitcast(I32).rearrange("s p col -> p s col"))
@@ -85,28 +88,27 @@ def tile_moe_bdx_glu_relu_kernel(
                 src.bitcast(I32).rearrange("e s f col -> f (e s) col")[4 * q : 4 * q + 4, passes],
             )
 
-        nc.scalar.dma_start(gates[0][:, 0:FIRST], gate[0:P, 0:FIRST])
-        for first_e, last_e in ((0, 2), (2, E)):
+        load_gate(0, 0, FIRST, nc.scalar)
+        for half in range(2):
             for q in (0, 2, 1, 3):
-                load_scales(w2_sc, w2_scales, q, nc.gpsimd, slice(S * first_e, S * last_e))
-            if first_e == 0:
-                load_gate(1, nc.gpsimd)
-        for s in range(S):
-            for t in range(4):
-                nc.sync.dma_start(planes[4 * s + t][:, 0:T], dy_rows[s, t])
-                if (s, t) == (0, 0):
-                    nc.sync.dma_start(gates[0][:, FIRST:CUT], gate[0:P, FIRST:CUT])
-                if 4 * s + t in (2, 5):
-                    load_saved(s, "a1", a1, a1_t)
-                if 4 * s + t in (7, 9):
-                    load_saved(s - 1 if t == 1 else 0, "a3", a3, a3_t)
+                load_scales(w2_sc, w2_scales, q, nc.gpsimd, slice(2 * S * half, 2 * S * (half + 1)))
+            if half == 0:
+                load_gate(1, CUT, SLOTS, nc.gpsimd)
+        for row in range(4 * S):
+            nc.sync.dma_start(planes[row][:, 0:T], dy_rows[row // 4, row % 4])
+            if row == 0:
+                load_gate(0, FIRST, CUT, nc.sync)
+            if row in A1_BEHIND:
+                load_saved(A1_BEHIND.index(row), "a1", a1, a1_t)
+            if row in A3_BEHIND:
+                load_saved(A3_BEHIND.index(row), "a3", a3, a3_t)
         load_w2(0)
         load_w2(1)
-        load_saved(S - 1, "a3", a3, a3_t)
-        load_saved(S - 1, "a1", a1, a1_t)
+        load_saved(2, "a3", a3, a3_t)
+        load_saved(2, "a1", a1, a1_t)
         load_w2(2)
-        load_saved(E - 1, "a1", a1, a1_t)
-        load_saved(E - 1, "a3", a3, a3_t)
+        load_saved(3, "a1", a1, a1_t)
+        load_saved(3, "a3", a3, a3_t)
         for tile, src in ((w1_t, w1_words), (w3_t, w3_words)):
             nc.sync.dma_start(tile[:].bitcast(I32), src.bitcast(I32).rearrange("e s p col -> p (e s) col"))
         for q in range(4):
@@ -118,7 +120,6 @@ def tile_moe_bdx_glu_relu_kernel(
 
         g_raw, g_woven, g_codes, g_scales = {}, {}, {}, {}
         factors, relu_mask, dh, dh_turned, da, da_codes, da_scales, dx_banks = {}, {}, {}, {}, {}, {}, {}, {}
-        held = []
         dx = []
 
         shared = keep.tile([P, 4 * REST], F32, name="shared", align_bytes=64)
@@ -153,8 +154,8 @@ def tile_moe_bdx_glu_relu_kernel(
                 woven = g_woven[a, s][:, 0 : CUT - HALF, :]
             elif c == 1:
                 if a == CUT:
-                    held.append(work.tile([P, REST * 4], BF16, name="g_held", tag="hold", bufs=1, align_bytes=64))
-                woven = held[0][:, 4 * (a - CUT) : 4 * (b - CUT)].rearrange("p (x t) -> p x t", t=4)
+                    g_woven["last"] = work.tile([P, REST * 4], BF16, name="g_last", tag="hold", bufs=1, align_bytes=64)
+                woven = g_woven["last"][:, 4 * (a - CUT) : 4 * (b - CUT)].rearrange("p (x t) -> p x t", t=4)
                 g_woven[a, s] = woven
             else:
                 woven = work.tile([P, b - a, 4], BF16, name="g_woven", tag="g_woven", bufs=3, align_bytes=64)
@@ -189,16 +190,13 @@ def tile_moe_bdx_glu_relu_kernel(
                 weave(c, s, CUT, SLOTS)
                 quantize_g(s, HALF, SLOTS)
 
-        def saved_a3(m):
+        def saved(m):
             e, cols = m // 2, slice(P * (m % 2), P * (m % 2 + 1))
             factors[m] = work.tile([P, 2, P, 4], F32, name="factors", tag=f"factors{HOME[m]}", bufs=1)
             nc.scalar.copy(
                 factors[m][:, 0].rearrange("p (g r) t -> p g t r", r=4),
                 a3_t[e][:, :, cols].rearrange("p t (g r) -> p g t r", r=4),
             )
-
-        def saved_a1(m):
-            e, cols = m // 2, slice(P * (m % 2), P * (m % 2 + 1))
             if m % 2 == 0:
                 relu_mask[e] = work.tile([P, 2, H], BF16, name="relu_mask", bufs=E)
             nc.scalar.activation(
@@ -227,8 +225,8 @@ def tile_moe_bdx_glu_relu_kernel(
 
         def turn(m):
             if m < 2:
-                sorted_dh = work.tile([P, 4, P], F32, name="sorted_first", tag=f"factors{4 + m}", bufs=1)
-            elif m == CUT // P - 1:
+                sorted_dh = work.tile([P, 4, P], F32, name="sorted_first", tag=f"factors{HOME[EARLY + m]}", bufs=1)
+            elif m == END:
                 sorted_dh = work.tile([P, 4, P], F32, name="sorted_last", tag="hold", bufs=1, align_bytes=64)
             else:
                 sorted_dh = work.tile([P, 4, P], F32, name="sorted_dh", bufs=2)
@@ -273,12 +271,12 @@ def tile_moe_bdx_glu_relu_kernel(
             if m == TILES - 1:
                 quantize_da(e, 3, 4)
 
-        def second(m):
+        def quantized(m):
             e, tiles = m // 2, group(m)
             if tiles:
                 quantize_da(e, 2 * tiles.start, 2 * tiles.stop - (1 if m == TILES - 1 else 0))
 
-        def third(m):
+        def second(m):
             for j in group(m):
                 back(m // 2, j)
 
@@ -303,22 +301,19 @@ def tile_moe_bdx_glu_relu_kernel(
                 for kt in range(4):
                     nc.scalar.copy(dx[kt][:, C * e : C * (e + 1)], dx_banks[e][kt])
 
-        stages = (first, turn, products, second, masked, third)
-        lag = stages.index(products)
+        lag = 2
+        stages = ((first, 0), (turn, 1), (products, lag), (quantized, lag + 1), (masked, lag), (second, lag + 2))
 
         def step(n):
-            for d, stage in zip((0, 1, 2, 3, 2, 4), stages):
-                if 0 <= n - d < TILES and (stage, n - d) != (turn, CUT // P - 1):
+            for stage, d in stages:
+                if 0 <= n - d < TILES and (stage, n - d) != (turn, END):
                     stage(n - d)
-            if 4 <= n + AHEAD < TILES:
-                saved_a3(n + AHEAD)
-                saved_a1(n + AHEAD)
+            if EARLY <= n + AHEAD < TILES:
+                saved(n + AHEAD)
 
         for s in range(S):
-            for m in (2 * s, 2 * s + 1):
-                if s < S - 1:
-                    saved_a3(m)
-                    saved_a1(m)
+            for m in range(2 * s, min(2 * s + 2, EARLY)):
+                saved(m)
             gather(0, s)
             pack(0, s)
         gather(1, 0)
@@ -330,9 +325,9 @@ def tile_moe_bdx_glu_relu_kernel(
             step(AFTER[s] + lag)
             done = AFTER[s] + lag + 1
             gather(1, s)
-        turn(CUT // P - 1)
+        turn(END)
         pack(1, S - 1)
-        for n in range(done, TILES + len(stages) - 1):
+        for n in range(done, TILES + lag + 2):
             step(n)
 
         by_pos1 = {}

@@ -226,6 +226,8 @@ def tile_moe_bdx_glu_relu_kernel(
         def turn(m):
             if m < 2:
                 sorted_dh = work.tile([P, 4, P], F32, name="sorted_first", tag=f"factors{HOME[EARLY + m]}", bufs=1)
+            elif m == END + 1:
+                sorted_dh = work.tile([P, 4, P], F32, name="sorted_next", tag=f"factors{HOME[-1]}", bufs=1)
             elif m == END:
                 sorted_dh = work.tile([P, 4, P], F32, name="sorted_last", tag="hold", bufs=1, align_bytes=64)
             else:
@@ -308,8 +310,10 @@ def tile_moe_bdx_glu_relu_kernel(
             for stage, d in stages:
                 if 0 <= n - d < TILES and (stage, n - d) != (turn, END):
                     stage(n - d)
-            if EARLY <= n + AHEAD < TILES:
+            if EARLY <= n + AHEAD < TILES - 1:
                 saved(n + AHEAD)
+            if n == TILES - 1:
+                saved(n)
 
         for s in range(S):
             for m in range(2 * s, min(2 * s + 2, EARLY)):

@@ -7,22 +7,14 @@ K, T, E, C, H, N = 512, 512, 4, 256, 512, 1536
 P = 128
 S = N // 512
 SLOTS = E * C
-HALF = SLOTS // 2
 TILES = SLOTS // P
-CUT = 640
-REST = SLOTS - CUT
-RANGES = ((0, CUT), (CUT, SLOTS))
-WINDOW = CUT + 1
-AFTER = {1: 0, 2: 2}
-EARLY = 4
-AHEAD = 3
-HOME = (0, 1, 2, 3, 4, 5, 1, 0)
-END = CUT // P - 1
-A1_BEHIND = (2, 5)
-A3_BEHIND = (7, 9)
-PAIRED = 2
+HEAD = 384
 FIRST = 256
-LAST = 384
+WINDOWS = (SLOTS - HEAD + 1, T, T)
+DH_BANK = ("dh0", "dh1", "dh0", "dx0", "dx1", "dx2", "dx3", "dh1")
+RUN = 2
+FETCH = (0, 256, 512)
+FETCH_LAST = (0, 256, 384, 512)
 
 FLOPS = 2 * SLOTS * (N * H + 2 * H * K)
 BYTES = 11210752
@@ -37,8 +29,8 @@ FP8 = mybir.dt.float8_e4m3fn_x4
 FP4 = mybir.dt.float4_e2m1fn_x4
 MULT = mybir.AluOpType.mult
 ADD = mybir.AluOpType.add
-RELU = mybir.ActivationFunctionType.Relu
-SIGN = mybir.ActivationFunctionType.Sign
+IS_GT = mybir.AluOpType.is_gt
+COPY = mybir.ActivationFunctionType.Copy
 
 
 def tile_moe_bdx_glu_relu_kernel(
@@ -47,309 +39,301 @@ def tile_moe_bdx_glu_relu_kernel(
     nc = tc.nc
     with ExitStack() as ctx:
         keep = ctx.enter_context(tc.tile_pool(name="keep", bufs=1))
-        work = ctx.enter_context(tc.tile_pool(name="work", bufs=3))
+        work = ctx.enter_context(tc.tile_pool(name="work", bufs=1))
         psum = ctx.enter_context(tc.psum_pool(name="psum", bufs=1))
 
         offs_t = keep.tile([P, SLOTS // 16], U16, name="offs_t")
         nc.sync.dma_start(offs_t[:], offs)
 
-        planes = [keep.tile([P, WINDOW], F32, name=f"plane{row}") for row in range(4 * S)]
-        for plane in planes:
-            nc.vector.memset(plane[:, T:WINDOW], 0.0)
-        w2_sc = keep.tile([P, E * S, H], U8, name="w2_sc", align_bytes=64)
+        planes = [keep.tile([P, WINDOWS[row // 4]], F32, name=f"plane{row}") for row in range(4 * S)]
+        w2_sc = [keep.tile([P, 2 * S, H], U8, name=f"w2_sc{half}", align_bytes=64) for half in range(2)]
+        for row in range(4):
+            nc.vector.memset(planes[row][:, T : WINDOWS[row // 4]], 0.0)
         w1_sc = keep.tile([P, E, K], U8, name="w1_sc", align_bytes=64)
         w3_sc = keep.tile([P, E, K], U8, name="w3_sc", align_bytes=64)
         ident = keep.tile([P, P], F32, name="ident")
         make_identity(nc, ident[:])
-        for sc in (w2_sc, w1_sc, w3_sc):
-            nc.gpsimd.memset(sc[:].rearrange("p pas col -> p (pas col)").bitcast(I32), 0)
 
         dy_rows = dyT.rearrange("(s p t) token -> s t p token", p=P, t=4)
-        gates = [keep.tile([P, hi - lo], F32, name=f"gate{c}") for c, (lo, hi) in enumerate(RANGES)]
+        gate_t = keep.tile([P, SLOTS], F32, name="gate_t")
+        g_codes = [keep.tile([P, SLOTS], U32, name=f"g_codes{s}", align_bytes=64) for s in range(S)]
+        g_scales = [keep.tile([P, SLOTS], U8, name=f"g_scales{s}", align_bytes=64) for s in range(S)]
         w2_t = [keep.tile([P, S, 2 * H], U8, name=f"w2_{e}", align_bytes=64) for e in range(E)]
         w1_t = keep.tile([P, E, 2 * K], U8, name="w1_t", align_bytes=64)
         w3_t = keep.tile([P, E, 2 * K], U8, name="w3_t", align_bytes=64)
         pos_t = [keep.tile([P, T // 16], U16, name=f"pos_t{r}") for r in range(2)]
-        a1_t, a3_t = {}, {}
+        a1_t = [keep.tile([P, 4, C], F32, name=f"a1_{e}") for e in range(E)]
+        a3_t = [keep.tile([P, 4, C], F32, name=f"a3_{e}") for e in range(E)]
 
-        def load_gate(c, a, b, queue):
-            queue.dma_start(gates[c][:, a - RANGES[c][0] : b - RANGES[c][0]], gate[0:P, a:b])
+        def load_gate(a, b, queue):
+            queue.dma_start(gate_t[:, a:b], gate[0:P, a:b])
 
         def load_w2(e):
             nc.sync.dma_start(w2_t[e][:].bitcast(I32), w2_words[e].bitcast(I32).rearrange("s p col -> p s col"))
 
-        def load_saved(e, name, src, tiles):
-            tiles[e] = work.tile([P, 4, C], F32, name=name, tag=f"{name}_{e}", bufs=1)
-            nc.sync.dma_start(tiles[e][:], src.rearrange("(p t) x -> p t x", t=4)[:, :, C * e : C * (e + 1)])
+        def load_saved(e):
+            for tiles, src in ((a1_t, a1), (a3_t, a3)):
+                nc.sync.dma_start(tiles[e][:], src.rearrange("(p t) x -> p t x", t=4)[:, :, C * e : C * (e + 1)])
 
-        def load_scales(sc, src, q, queue, passes=slice(None)):
-            queue.dma_start(
-                sc[32 * q : 32 * q + 4, passes].bitcast(I32),
-                src.bitcast(I32).rearrange("e s f col -> f (e s) col")[4 * q : 4 * q + 4, passes],
-            )
+        def zero(sc):
+            nc.gpsimd.memset(sc[:].rearrange("p pas col -> p (pas col)").bitcast(I32), 0)
 
-        load_gate(0, 0, FIRST, nc.scalar)
-        for half in range(2):
+        def load_scales(sc, src, queue, passes=slice(None)):
             for q in (0, 2, 1, 3):
-                load_scales(w2_sc, w2_scales, q, nc.gpsimd, slice(2 * S * half, 2 * S * (half + 1)))
-            if half == 0:
-                load_gate(1, CUT, SLOTS, nc.gpsimd)
+                queue.dma_start(
+                    sc[32 * q : 32 * q + 4].bitcast(I32),
+                    src.bitcast(I32).rearrange("e s f col -> f (e s) col")[4 * q : 4 * q + 4, passes],
+                )
+
+        load_gate(HEAD, HEAD + FIRST, nc.scalar)
+        zero(w2_sc[0])
+        load_scales(w2_sc[0], w2_scales, nc.gpsimd, slice(0, 2 * S))
+        for sc in (w2_sc[1], w1_sc, w3_sc):
+            zero(sc)
+        load_scales(w2_sc[1], w2_scales, nc.gpsimd, slice(2 * S, 4 * S))
         for row in range(4 * S):
             nc.sync.dma_start(planes[row][:, 0:T], dy_rows[row // 4, row % 4])
             if row == 0:
-                load_gate(0, FIRST, CUT, nc.sync)
-            if row in A1_BEHIND:
-                load_saved(A1_BEHIND.index(row), "a1", a1, a1_t)
-            if row in A3_BEHIND:
-                load_saved(A3_BEHIND.index(row), "a3", a3, a3_t)
-        load_w2(0)
+                load_gate(HEAD + FIRST, SLOTS, nc.sync)
+            if row == 2:
+                load_gate(0, HEAD, nc.sync)
+            if row == 9:
+                load_w2(0)
         load_w2(1)
-        load_saved(2, "a3", a3, a3_t)
-        load_saved(2, "a1", a1, a1_t)
+        load_saved(0)
+        load_saved(1)
         load_w2(2)
-        load_saved(3, "a1", a1, a1_t)
-        load_saved(3, "a3", a3, a3_t)
-        for tile, src in ((w1_t, w1_words), (w3_t, w3_words)):
+        for tile, src in ((w3_t, w3_words), (w1_t, w1_words)):
             nc.sync.dma_start(tile[:].bitcast(I32), src.bitcast(I32).rearrange("e s p col -> p (e s) col"))
-        for q in range(4):
-            load_scales(w1_sc, w1_scales, q, nc.sync)
-            load_scales(w3_sc, w3_scales, q, nc.sync)
+        load_scales(w3_sc, w3_scales, nc.sync)
+        load_scales(w1_sc, w1_scales, nc.sync)
         load_w2(3)
+        load_saved(2)
+        load_saved(3)
         for tile, src in zip(pos_t, (pos1, pos2)):
             nc.sync.dma_start(tile[:], src)
 
-        g_raw, g_woven, g_codes, g_scales = {}, {}, {}, {}
-        factors, relu_mask, dh, dh_turned, da, da_codes, da_scales, dx_banks = {}, {}, {}, {}, {}, {}, {}, {}
-        dx = []
+        raw, woven = {}, {}
+        dh, turned, masked_dh, da, da_codes, da_scales, dx_banks = {}, {}, {}, {}, {}, {}, {}
+        dx = [keep.tile([P, SLOTS], F32, name=f"dx{kt}") for kt in range(4)]
 
-        shared = keep.tile([P, 4 * REST], F32, name="shared", align_bytes=64)
+        def runs(ap):
+            return ap.rearrange("p t (g r) -> p g t r", r=RUN)
 
-        def gather(c, s):
-            lo, hi = RANGES[c]
-            if c == 0:
-                g_raw[c, s] = work.tile([P, 4, CUT], F32, name="g_raw", tag="g_raw", bufs=2)
-            elif s == 0:
-                g_raw[c, s] = shared[:].rearrange("p (t x) -> p t x", t=4)
-            else:
-                g_raw[c, s] = work.tile([P, 4, REST], F32, name="g_late", tag=f"factors{AFTER[s]}", bufs=1)
+        def weaving(ap):
+            return ap.rearrange("p (g r) t -> p g t r", r=RUN)
+
+        def gather(s, lo, hi, home):
+            raw[s, lo] = work.tile([P, 4, P * (hi - lo)], F32, name="raw", tag=home, align_bytes=64)
             for t in range(4):
-                for a, b in ((0, FIRST), (FIRST, CUT)) if (c, s, t) == (0, 0, 0) else ((lo, hi),):
+                nc.scalar.activation(
+                    raw[s, lo][:, t, :], planes[4 * s + t][:].indirect(offs_t[:, P * lo // 16 : P * hi // 16]), COPY
+                )
+
+        def gather_gated(s, lo, hi, home):
+            raw[s, lo] = work.tile([P, 4, P * (hi - lo)], F32, name="raw", tag=home, align_bytes=64)
+            for t in range(4):
+                cuts = (P * lo, P * lo + FIRST, P * hi) if t == 0 else (P * lo, P * hi)
+                for a, b in zip(cuts, cuts[1:]):
                     nc.vector.tensor_tensor(
-                        g_raw[c, s][:, t, a - lo : b - lo],
+                        raw[s, lo][:, t, a - P * lo : b - P * lo],
                         planes[4 * s + t][:].indirect(offs_t[:, a // 16 : b // 16]),
-                        gates[c][:, a - lo : b - lo],
+                        gate_t[:, a:b],
                         MULT,
                     )
 
-        def weave(c, s, a, b):
-            base = RANGES[c][0]
-            if (c, s) == (0, S - 1) and b < CUT:
-                at = REST * (1 if a == 0 else 2)
-                woven = shared[:, at : at + 2 * (b - a)].bitcast(BF16).rearrange("p (x t) -> p x t", t=4)
-                g_woven[a, s] = woven
-            elif s < S - 1 and a == CUT:
-                woven = g_woven[HALF, s][:, CUT - HALF :, :]
-            elif s < S - 1 and a == HALF:
-                g_woven[a, s] = keep.tile([P, HALF, 4], BF16, name=f"g_upper{s}", align_bytes=64)
-                woven = g_woven[a, s][:, 0 : CUT - HALF, :]
-            elif c == 1:
-                if a == CUT:
-                    g_woven["last"] = work.tile([P, REST * 4], BF16, name="g_last", tag="hold", bufs=1, align_bytes=64)
-                woven = g_woven["last"][:, 4 * (a - CUT) : 4 * (b - CUT)].rearrange("p (x t) -> p x t", t=4)
-                g_woven[a, s] = woven
-            else:
-                woven = work.tile([P, b - a, 4], BF16, name="g_woven", tag="g_woven", bufs=3, align_bytes=64)
-                g_woven[a, s] = woven
-            nc.scalar.copy(
-                woven[:].rearrange("p (g r) t -> p g t r", r=4),
-                g_raw[c, s][:, :, a - base : b - base].rearrange("p t (g r) -> p g t r", r=4),
+        def weave(s, lo, hi, home):
+            woven[s, lo] = work.tile([P, P * (hi - lo), 4], BF16, name="woven", tag=home, align_bytes=64)
+            nc.vector.tensor_copy(
+                woven[s, lo][:].rearrange("p (g r) t -> p g t r", r=4),
+                raw[s, lo][:].rearrange("p t (g r) -> p g t r", r=4),
             )
 
-        def quantize_g(s, a, b):
-            codes = keep.tile([P, b - a], U32, name=f"g_codes{s}_{a}", align_bytes=64)
-            scales = keep.tile([P, b - a], U8, name=f"g_scales{s}_{a}", align_bytes=64)
-            for m in range(a // P, b // P):
-                g_codes[m, s] = codes[:, P * m - a : P * m - a + P]
-                g_scales[m, s] = scales[:, P * m - a : P * m - a + P]
+        def gated(s, lo, hi, home, base=None):
+            base = lo if base is None else base
+            woven[s, lo] = work.tile([P, P * (hi - lo), 4], BF16, name="woven", tag=home, align_bytes=64)
+            nc.vector.tensor_tensor(
+                weaving(woven[s, lo][:]),
+                runs(raw[s, base][:, :, P * (lo - base) : P * (hi - base)]),
+                gate_t[:, P * lo : P * hi]
+                .rearrange("p (g r) -> p g r", r=RUN)
+                .unsqueeze(2)
+                .to_broadcast([P, P * (hi - lo) // RUN, 4, RUN]),
+                MULT,
+            )
+
+        def quantize_g(s, lo, hi, base=None):
+            base = lo if base is None else base
             nc.vector.quantize_mx(
-                out=codes[:].bitcast(FP8), scales=scales[:], in_=g_woven[a, s][:].rearrange("p x t -> p (x t)")
+                out=g_codes[s][:, P * lo : P * hi].bitcast(FP8),
+                scales=g_scales[s][:, P * lo : P * hi],
+                in_=woven[s, base][:, P * (lo - base) : P * (hi - base), :].rearrange("p x t -> p (x t)"),
             )
-
-        def pack(c, s):
-            lo, hi = RANGES[c]
-            if s == S - 1:
-                cuts = [lo] + list(range(lo + P, hi, C if c == 0 else P)) + [hi]
-                for a, b in zip(cuts, cuts[1:]):
-                    weave(c, s, a, b)
-                    quantize_g(s, a, b)
-            elif c == 0:
-                weave(c, s, 0, HALF)
-                quantize_g(s, 0, HALF)
-                weave(c, s, HALF, CUT)
-            else:
-                weave(c, s, CUT, SLOTS)
-                quantize_g(s, HALF, SLOTS)
-
-        def saved(m):
-            e, cols = m // 2, slice(P * (m % 2), P * (m % 2 + 1))
-            factors[m] = work.tile([P, 2, P, 4], F32, name="factors", tag=f"factors{HOME[m]}", bufs=1)
-            nc.scalar.copy(
-                factors[m][:, 0].rearrange("p (g r) t -> p g t r", r=4),
-                a3_t[e][:, :, cols].rearrange("p t (g r) -> p g t r", r=4),
-            )
-            if m % 2 == 0:
-                relu_mask[e] = work.tile([P, 2, H], BF16, name="relu_mask", bufs=E)
-            nc.scalar.activation(
-                factors[m][:, 1].rearrange("p (g r) t -> p g t r", r=4),
-                a1_t[e][:, :, cols].rearrange("p t (g r) -> p g t r", r=4),
-                RELU,
-            )
-            nc.scalar.activation(relu_mask[e][:, m % 2, :], factors[m][:, 1].rearrange("p x t -> p (x t)"), SIGN)
-            if m % 2 == 1 and e < 2:
-                for name in ("a1", "a3"):
-                    dx.append(work.tile([P, SLOTS], F32, name="dx", tag=f"{name}_{e}", bufs=1))
 
         def first(m):
-            e = m // 2
-            dh[m] = psum.tile([P, H], F32, name="dh", bufs=4)
+            e, cols = m // 2, slice(P * m, P * (m + 1))
+            dh[m] = psum.tile([P, H], F32, name="dh", tag=DH_BANK[m])
             for s in range(S):
                 nc.tensor.matmul_mx(
                     out=dh[m][:],
-                    lhsT=g_codes[m, s].bitcast(FP8),
-                    lhsT_scale=g_scales[m, s],
+                    lhsT=g_codes[s][:, cols].bitcast(FP8),
+                    lhsT_scale=g_scales[s][:, cols],
                     rhs=w2_t[e][:, s, :].bitcast(FP4),
-                    rhs_scale=w2_sc[:, S * e + s, :],
+                    rhs_scale=w2_sc[e // 2][:, S * (e % 2) + s, :],
                     start=(s == 0),
                     stop=(s == S - 1),
                 )
 
-        def turn(m):
-            if m < 2:
-                sorted_dh = work.tile([P, 4, P], F32, name="sorted_first", tag=f"factors{HOME[EARLY + m]}", bufs=1)
-            elif m == END + 1:
-                sorted_dh = work.tile([P, 4, P], F32, name="sorted_next", tag=f"factors{HOME[-1]}", bufs=1)
-            elif m == END:
-                sorted_dh = work.tile([P, 4, P], F32, name="sorted_last", tag="hold", bufs=1, align_bytes=64)
-            else:
-                sorted_dh = work.tile([P, 4, P], F32, name="sorted_dh", bufs=2)
+        def turn(m, home):
+            sorted_dh = work.tile([P, 4, P], F32, name="sorted_dh", tag=home, align_bytes=64)
             nc.scalar.copy(
                 sorted_dh[:].rearrange("x t (g r) -> x g t r", r=4),
                 dh[m][:].rearrange("x (g r t) -> x g t r", r=4, t=4),
             )
-            dh_turned[m] = psum.tile([P, 4, P], F32, name="dh_turned", bufs=2)
+            turned[m] = psum.tile([P, 4, P], F32, name="turned", tag=f"turned{m % 2}")
             for t in range(4):
-                nc.tensor.transpose(dh_turned[m][:, t, :], sorted_dh[:, t, :], ident[:])
+                nc.tensor.transpose(turned[m][:, t, :], sorted_dh[:, t, :], ident[:])
+
+        def mask(m, home):
+            e, cols = m // 2, slice(P * (m % 2), P * (m % 2 + 1))
+            masked_dh[m] = work.tile([P, 4, P], F32, name="masked_dh", tag=home, align_bytes=64)
+            nc.vector.scalar_tensor_tensor(masked_dh[m][:], a1_t[e][:, :, cols], 0.0, turned[m][:], IS_GT, MULT)
 
         def products(m):
-            e, j = m // 2, m % 2
-            if j == 0:
-                da[e] = work.tile([P, 2, 2, P, 4], BF16, name="da", bufs=3, align_bytes=64)
-                da_codes[e] = keep.tile([P, 4 * P], U32, name=f"da_codes{e}", align_bytes=64)
-                da_scales[e] = keep.tile([P, 4 * P], U8, name=f"da_scales{e}", align_bytes=64)
-            nc.vector.tensor_tensor(
-                da[e][:, j],
-                dh_turned[m][:].rearrange("p t x -> p x t").unsqueeze(1).to_broadcast([P, 2, P, 4]),
-                factors[m][:],
-                MULT,
-            )
+            e, cols = m // 2, slice(P * (m % 2), P * (m % 2 + 1))
+            da[m] = work.tile([P, 2, P, 4], BF16, name="da", tag=f"da{m % 2}", align_bytes=64)
+            for w, tiles in enumerate((a1_t, a3_t)):
+                nc.vector.tensor_tensor(weaving(da[m][:, w]), runs(masked_dh[m][:]), runs(tiles[e][:, :, cols]), MULT)
 
-        def group(m):
-            if m // 2 < PAIRED:
-                return range(2 * (m % 2))
-            return range(m % 2, m % 2 + 1)
-
-        def quantize_da(e, a, b):
+        def quantize_da(m, sides=slice(0, 2)):
+            if sides.start == 0:
+                da_codes[m] = keep.tile([P, 2 * P], U32, name=f"da_codes{m}", align_bytes=64)
+                da_scales[m] = keep.tile([P, 2 * P], U8, name=f"da_scales{m}", align_bytes=64)
             nc.vector.quantize_mx(
-                out=da_codes[e][:, P * a : P * b].bitcast(FP8),
-                scales=da_scales[e][:, P * a : P * b],
-                in_=da[e][:].rearrange("p j w x t -> p (j w x t)")[:, H * a : H * b],
+                out=da_codes[m][:, P * sides.start : P * sides.stop].bitcast(FP8),
+                scales=da_scales[m][:, P * sides.start : P * sides.stop],
+                in_=da[m][:, sides].rearrange("p w x t -> p (w x t)"),
             )
 
-        def masked(m):
-            e, tiles = m // 2, group(m)
-            if tiles:
-                da1 = da[e][:, tiles.start : tiles.stop, 0].rearrange("p j x t -> p j (x t)")
-                nc.vector.tensor_tensor(da1, da1, relu_mask[e][:, tiles.start : tiles.stop, :], MULT)
+        def back(m):
+            e, j = m // 2, m % 2
             if m == TILES - 1:
-                quantize_da(e, 3, 4)
-
-        def quantized(m):
-            e, tiles = m // 2, group(m)
-            if tiles:
-                quantize_da(e, 2 * tiles.start, 2 * tiles.stop - (1 if m == TILES - 1 else 0))
-
-        def second(m):
-            for j in group(m):
-                back(m // 2, j)
-
-        def back(e, j):
-            if j == 0 and e == E - 1:
-                dx_banks[e] = [psum.tile([P, C], F32, name="dx_last", tag="dh", bufs=4)[:] for kt in range(4)]
-            elif j == 0:
-                pairs = [psum.tile([P, 2, C], F32, name=f"dx_pair{b}", bufs=1) for b in range(2)]
-                dx_banks[e] = [pairs[kt // 2][:, kt % 2, :] for kt in range(4)]
+                banks = [psum.tile([P, P], F32, name="dx_last", tag=tag)[:] for tag in ("dh0", "dh1", "turned0", "dx3")]
+            elif m == TILES - 2:
+                bank = psum.tile([P, 4, P], F32, name="dx_next", tag="dx2")
+                banks = [bank[:, kt, :] for kt in range(4)]
+            else:
+                if j == 0:
+                    dx_banks[e] = [
+                        psum.tile([P, 2, C], F32, name="dx_pair", tag=f"dx{2 * (e % 2) + b}") for b in range(2)
+                    ]
+                banks = [dx_banks[e][kt // 2][:, kt % 2, P * j : P * (j + 1)] for kt in range(4)]
             for kt in range(4):
-                for w, words, sc in ((1, w3_t, w3_sc), (0, w1_t, w1_sc)):
+                for w, (words, sc) in enumerate(((w3_t, w3_sc), (w1_t, w1_sc))):
                     nc.tensor.matmul_mx(
-                        out=dx_banks[e][kt][:, P * j : P * (j + 1)],
+                        out=banks[kt],
                         lhsT=words[:, e, 2 * P * kt : 2 * P * (kt + 1)].bitcast(FP4),
                         lhsT_scale=sc[:, e, P * kt : P * (kt + 1)],
-                        rhs=da_codes[e][:, P * (2 * j + w) : P * (2 * j + w + 1)].bitcast(FP8),
-                        rhs_scale=da_scales[e][:, P * (2 * j + w) : P * (2 * j + w + 1)],
-                        start=(w == 1),
-                        stop=(w == 0),
+                        rhs=da_codes[m][:, P * w : P * (w + 1)].bitcast(FP8),
+                        rhs_scale=da_scales[m][:, P * w : P * (w + 1)],
+                        start=(w == 0),
+                        stop=(w == 1),
                     )
-            if j == 1:
-                for kt in range(4):
-                    nc.scalar.copy(dx[kt][:, C * e : C * (e + 1)], dx_banks[e][kt])
+            for kt in range(4):
+                if m == TILES - 1 and kt > 0:
+                    nc.vector.tensor_copy(dx[kt][:, P * m : P * (m + 1)], banks[kt])
+                elif m >= TILES - 2:
+                    nc.scalar.copy(dx[kt][:, P * m : P * (m + 1)], banks[kt])
+                elif j == 1:
+                    nc.scalar.copy(dx[kt][:, C * e : C * (e + 1)], dx_banks[e][kt // 2][:, kt % 2, :])
 
-        lag = 2
-        stages = ((first, 0), (turn, 1), (products, lag), (quantized, lag + 1), (masked, lag), (second, lag + 2))
+        def done(m):
+            quantize_da(m)
+            back(m)
 
-        def step(n):
-            for stage, d in stages:
-                if 0 <= n - d < TILES and (stage, n - d) != (turn, END):
-                    stage(n - d)
-            if EARLY <= n + AHEAD < TILES - 1:
-                saved(n + AHEAD)
-            if n == TILES - 1:
-                saved(n)
+        def through(m, home):
+            first(m)
+            turn(m, home)
 
-        for s in range(S):
-            for m in range(2 * s, min(2 * s + 2, EARLY)):
-                saved(m)
-            gather(0, s)
-            pack(0, s)
-        gather(1, 0)
-        done = 0
-        for s in sorted(AFTER):
-            for n in range(done, AFTER[s] + lag):
-                step(n)
-            pack(1, s - 1)
-            step(AFTER[s] + lag)
-            done = AFTER[s] + lag + 1
-            gather(1, s)
-        turn(END)
-        pack(1, S - 1)
-        for n in range(done, TILES + lag + 2):
-            step(n)
+        gather_gated(0, 3, 8, "raw_v")
+        gather(0, 0, 3, "raw_a")
+        gated(0, 0, 3, "woven_a")
+        quantize_g(0, 0, 3)
+        gather(1, 0, 3, "raw_b")
+        gated(1, 0, 3, "woven_b")
+        quantize_g(1, 0, 3)
+        gather(2, 0, 3, "raw_c")
+        weave(0, 3, 8, "woven_b")
+        gated(2, 0, 1, "woven_c", 0)
+        gated(2, 1, 2, "woven_d", 0)
+        quantize_g(2, 0, 1)
+        gated(2, 2, 3, "woven_e", 0)
+        quantize_g(2, 1, 2)
+        quantize_g(0, 3, 7, 3)
+        quantize_g(2, 2, 3)
+        through(0, "raw_a")
+        through(1, "raw_c")
+        gather(1, 3, 5, "raw_a")
+        through(2, "raw_b")
+        gather(2, 3, 5, "raw_c")
+        gather(1, 5, 8, "raw_b")
+        mask(0, "m0")
+        quantize_g(0, 7, 8, 3)
+        products(0)
+        mask(1, "m1")
+        quantize_da(0)
+        products(1)
+        gated(1, 3, 5, "m0")
+        gated(2, 3, 5, "m1")
+        quantize_g(1, 3, 5)
+        quantize_g(2, 3, 5)
+        through(3, "raw_d")
+        through(4, "raw_v")
+        gather(2, 5, 7, "raw_d")
+        gather(2, 7, 8, "raw_v")
+        mask(2, "m0")
+        quantize_da(1)
+        products(2)
+        gated(1, 5, 8, "m1")
+        quantize_da(2)
+        mask(3, "m2")
+        quantize_g(1, 5, 8)
+        products(3)
+        gated(2, 5, 7, "m0")
+        quantize_da(3)
+        quantize_g(2, 5, 7)
+        through(5, "sorted")
+        through(6, "sorted_b")
+        mask(4, "m1")
+        gated(2, 7, 8, "m2")
+        products(4)
+        quantize_g(2, 7, 8)
+        through(7, "sorted")
+        for m in range(4):
+            back(m)
+        mask(5, "m0")
+        done(4)
+        products(5)
+        mask(6, "m1")
+        done(5)
+        products(6)
+        mask(7, "m0")
+        done(6)
+        products(7)
+        quantize_da(7, slice(0, 1))
+        quantize_da(7, slice(1, 2))
+        back(7)
 
-        by_pos1 = {}
-
-        def fetch(kt):
-            by_pos1[kt] = work.tile([P, T], F32, name="by_pos1", bufs=3)
-            nc.vector.tensor_copy(by_pos1[kt][:], dx[kt][:].indirect(pos_t[0][:]))
-
-        def combine(kt):
-            total = work.tile([P, T], F32, name="total", tag=f"factors{HOME[TILES - 4 + kt]}", bufs=1)
-            for a, b in ((0, LAST), (LAST, T)) if kt == 3 else ((0, T),):
-                nc.vector.tensor_tensor(
-                    total[:, a:b], dx[kt][:].indirect(pos_t[1][:, a // 16 : b // 16]), by_pos1[kt][:, a:b], ADD
-                )
-                nc.sync.dma_start(out[P * kt : P * (kt + 1), a:b], total[:, a:b])
-
-        fetch(0)
         for kt in range(4):
+            by_pos1 = keep.tile([P, T], F32, name=f"by_pos1_{kt}")
+            total = keep.tile([P, T], F32, name=f"total{kt}")
+            cuts = FETCH_LAST if kt == 3 else FETCH
+            for a, b in zip(cuts, cuts[1:]):
+                nc.scalar.activation(by_pos1[:, a:b], dx[kt][:].indirect(pos_t[0][:, a // 16 : b // 16]), COPY)
+                nc.vector.tensor_tensor(
+                    total[:, a:b], dx[kt][:].indirect(pos_t[1][:, a // 16 : b // 16]), by_pos1[:, a:b], ADD
+                )
+                if kt == 3:
+                    nc.sync.dma_start(out[P * kt : P * (kt + 1), a:b], total[:, a:b])
             if kt < 3:
-                fetch(kt + 1)
-            combine(kt)
+                nc.sync.dma_start(out[P * kt : P * (kt + 1), :], total[:])

@@ -45,6 +45,10 @@ def tile_moe_bdx_glu_relu_kernel(
         offs_t = keep.tile([P, SLOTS // 16], U16, name="offs_t")
         nc.sync.dma_start(offs_t[:], offs)
 
+        warm = keep.tile([P, 2], F32, name="warm")
+        nc.vector.memset(warm[:, 0:1], 0.0)
+        nc.scalar.activation(warm[:, 1:2], warm[:, 0:1], COPY)
+
         planes = [keep.tile([P, WINDOWS[row // 4]], F32, name=f"plane{row}") for row in range(4 * S)]
         w2_sc = [keep.tile([P, 2 * S, H], U8, name=f"w2_sc{half}", align_bytes=64) for half in range(2)]
         for row in range(4):

@@ -62,7 +62,13 @@ def tile_moe_bdx_glu_relu_kernel(
         gate_t = keep.tile([P, SLOTS], F32, name="gate_t")
         g_codes = [keep.tile([P, SLOTS], U32, name=f"g_codes{s}", align_bytes=64) for s in range(S)]
         g_scales = [keep.tile([P, SLOTS], U8, name=f"g_scales{s}", align_bytes=64) for s in range(S)]
-        w2_t = [keep.tile([P, S, 2 * H], U8, name=f"w2_{e}", align_bytes=64) for e in range(E)]
+        w2_t = [keep.tile([P, S, 2 * H], U8, name=f"w2_{e}", align_bytes=64) for e in range(1, E)]
+        w2_first = work.tile([P, 2 * H], U8, name="w2_first", tag="raw_e", align_bytes=64)
+        w2_rest = work.tile([P, S - 1, 2 * H], U8, name="w2_rest", tag="raw_f", align_bytes=64)
+        w2_pass = {(e, s): w2_t[e - 1][:, s, :] for e in range(1, E) for s in range(S)}
+        w2_pass[0, 0] = w2_first[:]
+        for s in range(1, S):
+            w2_pass[0, s] = w2_rest[:, s - 1, :]
         w1_t = keep.tile([P, E, 2 * K], U8, name="w1_t", align_bytes=64)
         w3_t = keep.tile([P, E, 2 * K], U8, name="w3_t", align_bytes=64)
         pos_t = [keep.tile([P, T // 16], U16, name=f"pos_t{r}") for r in range(2)]
@@ -73,7 +79,7 @@ def tile_moe_bdx_glu_relu_kernel(
             queue.dma_start(gate_t[:, a:b], gate[0:P, a:b])
 
         def load_w2(e):
-            nc.sync.dma_start(w2_t[e][:].bitcast(I32), w2_words[e].bitcast(I32).rearrange("s p col -> p s col"))
+            nc.sync.dma_start(w2_t[e - 1][:].bitcast(I32), w2_words[e].bitcast(I32).rearrange("s p col -> p s col"))
 
         def load_saved(e):
             for tiles, src in ((a1_t, a1), (a3_t, a3)):
@@ -102,7 +108,10 @@ def tile_moe_bdx_glu_relu_kernel(
             if row == 2:
                 load_gate(0, HEAD, nc.sync)
             if row == 9:
-                load_w2(0)
+                nc.sync.dma_start(
+                    w2_rest[:].bitcast(I32), w2_words[0, 1:S].bitcast(I32).rearrange("s p col -> p s col")
+                )
+        nc.sync.dma_start(w2_first[:].bitcast(I32), w2_words[0, 0].bitcast(I32))
         load_w2(1)
         load_saved(0)
         load_saved(1)
@@ -146,11 +155,11 @@ def tile_moe_bdx_glu_relu_kernel(
                         MULT,
                     )
 
-        def weave(s, lo, hi, home):
+        def weave(s, lo, hi, home, base):
             woven[s, lo] = work.tile([P, P * (hi - lo), 4], BF16, name="woven", tag=home, align_bytes=64)
             nc.vector.tensor_copy(
                 woven[s, lo][:].rearrange("p (g r) t -> p g t r", r=4),
-                raw[s, lo][:].rearrange("p t (g r) -> p g t r", r=4),
+                raw[s, base][:, :, P * (lo - base) : P * (hi - base)].rearrange("p t (g r) -> p g t r", r=4),
             )
 
         def gated(s, lo, hi, home, base=None):
@@ -174,19 +183,21 @@ def tile_moe_bdx_glu_relu_kernel(
                 in_=woven[s, base][:, P * (lo - base) : P * (hi - base), :].rearrange("p x t -> p (x t)"),
             )
 
-        def first(m):
-            e, cols = m // 2, slice(P * m, P * (m + 1))
-            dh[m] = psum.tile([P, H], F32, name="dh", tag=DH_BANK[m])
-            for s in range(S):
-                nc.tensor.matmul_mx(
-                    out=dh[m][:],
-                    lhsT=g_codes[s][:, cols].bitcast(FP8),
-                    lhsT_scale=g_scales[s][:, cols],
-                    rhs=w2_t[e][:, s, :].bitcast(FP4),
-                    rhs_scale=w2_sc[e // 2][:, S * (e % 2) + s, :],
-                    start=(s == 0),
-                    stop=(s == S - 1),
-                )
+        def first(tiles, order=(0, 1, 2)):
+            for m in tiles:
+                dh[m] = psum.tile([P, H], F32, name="dh", tag=DH_BANK[m])
+            for s in order:
+                for m in tiles:
+                    e, cols = m // 2, slice(P * m, P * (m + 1))
+                    nc.tensor.matmul_mx(
+                        out=dh[m][:],
+                        lhsT=g_codes[s][:, cols].bitcast(FP8),
+                        lhsT_scale=g_scales[s][:, cols],
+                        rhs=w2_pass[e, s].bitcast(FP4),
+                        rhs_scale=w2_sc[e // 2][:, S * (e % 2) + s, :],
+                        start=(s == order[0]),
+                        stop=(s == order[-1]),
+                    )
 
         def turn(m, home):
             sorted_dh = work.tile([P, 4, P], F32, name="sorted_dh", tag=home, align_bytes=64)
@@ -256,7 +267,7 @@ def tile_moe_bdx_glu_relu_kernel(
             back(m)
 
         def through(m, home):
-            first(m)
+            first((m,))
             turn(m, home)
 
         gather_gated(0, 3, 8, "raw_v")
@@ -267,61 +278,63 @@ def tile_moe_bdx_glu_relu_kernel(
         gated(1, 0, 3, "woven_b")
         quantize_g(1, 0, 3)
         gather(2, 0, 3, "raw_c")
-        weave(0, 3, 8, "woven_b")
+        weave(0, 3, 5, "woven_b", 3)
+        quantize_g(0, 3, 5)
         gated(2, 0, 1, "woven_c", 0)
         gated(2, 1, 2, "woven_d", 0)
         quantize_g(2, 0, 1)
         gated(2, 2, 3, "woven_e", 0)
         quantize_g(2, 1, 2)
-        quantize_g(0, 3, 7, 3)
+        weave(0, 5, 8, "woven_c", 3)
         quantize_g(2, 2, 3)
-        through(0, "raw_a")
-        through(1, "raw_c")
-        gather(1, 3, 5, "raw_a")
+        first((0, 1))
+        gather(1, 3, 5, "raw_e")
+        turn(0, "raw_a")
+        turn(1, "raw_c")
+        gather(2, 3, 5, "raw_f")
         through(2, "raw_b")
-        gather(2, 3, 5, "raw_c")
-        gather(1, 5, 8, "raw_b")
+        gather(1, 5, 8, "raw_c")
+        gated(1, 3, 5, "woven_d")
+        quantize_g(0, 5, 8)
         mask(0, "m0")
-        quantize_g(0, 7, 8, 3)
+        quantize_g(1, 3, 5)
         products(0)
         mask(1, "m1")
         quantize_da(0)
         products(1)
-        gated(1, 3, 5, "m0")
-        gated(2, 3, 5, "m1")
-        quantize_g(1, 3, 5)
+        gated(2, 3, 5, "m0")
+        quantize_da(1)
         quantize_g(2, 3, 5)
         through(3, "raw_d")
         through(4, "raw_v")
         gather(2, 5, 7, "raw_d")
         gather(2, 7, 8, "raw_v")
-        mask(2, "m0")
-        quantize_da(1)
+        mask(2, "m1")
+        gated(1, 5, 8, "m0")
         products(2)
-        gated(1, 5, 8, "m1")
-        quantize_da(2)
-        mask(3, "m2")
         quantize_g(1, 5, 8)
+        mask(3, "m2")
+        quantize_da(2)
         products(3)
-        gated(2, 5, 7, "m0")
+        gated(2, 5, 7, "m1")
         quantize_da(3)
         quantize_g(2, 5, 7)
         through(5, "sorted")
         through(6, "sorted_b")
-        mask(4, "m1")
+        mask(4, "m0")
         gated(2, 7, 8, "m2")
         products(4)
         quantize_g(2, 7, 8)
         through(7, "sorted")
         for m in range(4):
             back(m)
-        mask(5, "m0")
+        mask(5, "m1")
         done(4)
         products(5)
-        mask(6, "m1")
+        mask(6, "m0")
         done(5)
         products(6)
-        mask(7, "m0")
+        mask(7, "m1")
         done(6)
         products(7)
         quantize_da(7, slice(0, 1))

@@ -11,7 +11,7 @@ TILES = SLOTS // P
 HEAD = 384
 FIRST = 256
 WINDOWS = (SLOTS - HEAD + 1, T, T)
-DH_BANK = ("dh0", "dh1", "dh0", "dx0", "dx1", "dx2", "dx3", "dh1")
+DH_BANK = ("dh0", "dh1", "dh0", "dx0", "dx1", "dh1", "dh0", "dh1")
 RUN = 2
 FETCH = (0, 256, 512)
 FETCH_LAST = (0, 256, 384, 512)
@@ -31,6 +31,8 @@ MULT = mybir.AluOpType.mult
 ADD = mybir.AluOpType.add
 IS_GT = mybir.AluOpType.is_gt
 COPY = mybir.ActivationFunctionType.Copy
+RELU = mybir.ActivationFunctionType.Relu
+SIGN = mybir.ActivationFunctionType.Sign
 
 
 def tile_moe_bdx_glu_relu_kernel(
@@ -62,7 +64,7 @@ def tile_moe_bdx_glu_relu_kernel(
         gate_t = keep.tile([P, SLOTS], F32, name="gate_t")
         g_codes = [keep.tile([P, SLOTS], U32, name=f"g_codes{s}", align_bytes=64) for s in range(S)]
         g_scales = [keep.tile([P, SLOTS], U8, name=f"g_scales{s}", align_bytes=64) for s in range(S)]
-        w2_t = [keep.tile([P, S, 2 * H], U8, name=f"w2_{e}", align_bytes=64) for e in range(1, E)]
+        w2_t = [work.tile([P, S, 2 * H], U8, name=f"w2_{e}", tag=f"w2_{e}", align_bytes=64) for e in range(1, E)]
         w2_first = work.tile([P, 2 * H], U8, name="w2_first", tag="raw_e", align_bytes=64)
         w2_rest = work.tile([P, S - 1, 2 * H], U8, name="w2_rest", tag="raw_f", align_bytes=64)
         w2_pass = {(e, s): w2_t[e - 1][:, s, :] for e in range(1, E) for s in range(S)}
@@ -126,7 +128,7 @@ def tile_moe_bdx_glu_relu_kernel(
         for tile, src in zip(pos_t, (pos1, pos2)):
             nc.sync.dma_start(tile[:], src)
 
-        raw, woven = {}, {}
+        raw, woven, relu_a1, relu_mask = {}, {}, {}, {}
         dh, turned, masked_dh, da, da_codes, da_scales, dx_banks = {}, {}, {}, {}, {}, {}, {}
         dx = [keep.tile([P, SLOTS], F32, name=f"dx{kt}") for kt in range(4)]
 
@@ -220,6 +222,26 @@ def tile_moe_bdx_glu_relu_kernel(
             for w, tiles in enumerate((a1_t, a3_t)):
                 nc.vector.tensor_tensor(weaving(da[m][:, w]), runs(masked_dh[m][:]), runs(tiles[e][:, :, cols]), MULT)
 
+        def prepare(m, home):
+            e, cols = m // 2, slice(P * (m % 2), P * (m % 2 + 1))
+            relu_a1[m] = work.tile([P, 4, P], F32, name="relu_a1", tag=home, align_bytes=64)
+            relu_mask[m] = keep.tile([P, P, 4], BF16, name=f"relu_mask{m}")
+            nc.scalar.activation(relu_a1[m][:], a1_t[e][:, :, cols], RELU)
+            nc.scalar.activation(
+                relu_mask[m][:].rearrange("p (g r) t -> p g t r", r=4),
+                relu_a1[m][:].rearrange("p t (g r) -> p g t r", r=4),
+                SIGN,
+            )
+
+        def products_late(m):
+            e, cols = m // 2, slice(P * (m % 2), P * (m % 2 + 1))
+            da[m] = work.tile([P, 2, P, 4], BF16, name="da", tag=f"da{m % 2}", align_bytes=64)
+            nc.vector.tensor_tensor(weaving(da[m][:, 1]), runs(turned[m][:]), runs(a3_t[e][:, :, cols]), MULT)
+
+        def products_rest(m):
+            nc.vector.tensor_tensor(weaving(da[m][:, 0]), runs(turned[m][:]), runs(relu_a1[m][:]), MULT)
+            nc.vector.tensor_tensor(da[m][:, 1], da[m][:, 1], relu_mask[m][:], MULT)
+
         def quantize_da(m, sides=slice(0, 2)):
             if sides.start == 0:
                 da_codes[m] = keep.tile([P, 2 * P], U32, name=f"da_codes{m}", align_bytes=64)
@@ -307,8 +329,8 @@ def tile_moe_bdx_glu_relu_kernel(
         quantize_g(2, 3, 5)
         through(3, "raw_d")
         through(4, "raw_v")
-        gather(2, 5, 7, "raw_d")
-        gather(2, 7, 8, "raw_v")
+        gather(2, 5, 7, "w2_1")
+        gather(2, 7, 8, "raw_d")
         mask(2, "m1")
         gated(1, 5, 8, "m0")
         products(2)
@@ -321,22 +343,22 @@ def tile_moe_bdx_glu_relu_kernel(
         quantize_g(2, 5, 7)
         through(5, "sorted")
         through(6, "sorted_b")
+        for m in range(4):
+            back(m)
         mask(4, "m0")
         gated(2, 7, 8, "m2")
         products(4)
         quantize_g(2, 7, 8)
-        through(7, "sorted")
-        for m in range(4):
-            back(m)
+        prepare(6, "sorted")
+        through(7, "raw_v")
+        prepare(7, "sorted_b")
         mask(5, "m1")
         done(4)
         products(5)
-        mask(6, "m0")
-        done(5)
-        products(6)
-        mask(7, "m1")
-        done(6)
-        products(7)
+        for m in (6, 7):
+            products_late(m)
+            done(m - 1)
+            products_rest(m)
         quantize_da(7, slice(0, 1))
         quantize_da(7, slice(1, 2))
         back(7)

@@ -13,8 +13,7 @@ FIRST = 256
 WINDOWS = (SLOTS - HEAD + 1, T, T)
 DH_BANK = ("dh0", "dh1", "dh0", "dx0", "dx1", "dh1", "dh0", "dh1")
 RUN = 2
-FETCH = (0, 256, 512)
-FETCH_LAST = (0, 256, 384, 512)
+SPLIT = 320
 
 FLOPS = 2 * SLOTS * (N * H + 2 * H * K)
 BYTES = 11210752
@@ -57,6 +56,7 @@ def tile_moe_bdx_glu_relu_kernel(
             nc.vector.memset(planes[row][:, T : WINDOWS[row // 4]], 0.0)
         w1_sc = keep.tile([P, E, K], U8, name="w1_sc", align_bytes=64)
         w3_sc = keep.tile([P, E, K], U8, name="w3_sc", align_bytes=64)
+        nc.gpsimd.memset(w2_sc[0][:].rearrange("p pas col -> p (pas col)").bitcast(I32), 0)
         ident = keep.tile([P, P], F32, name="ident")
         make_identity(nc, ident[:])
 
@@ -98,8 +98,6 @@ def tile_moe_bdx_glu_relu_kernel(
                 )
 
         load_gate(HEAD, HEAD + FIRST, nc.scalar)
-        zero(w2_sc[0])
-        load_scales(w2_sc[0], w2_scales, nc.gpsimd, slice(0, 2 * S))
         for sc in (w2_sc[1], w1_sc, w3_sc):
             zero(sc)
         load_scales(w2_sc[1], w2_scales, nc.gpsimd, slice(2 * S, 4 * S))
@@ -109,6 +107,8 @@ def tile_moe_bdx_glu_relu_kernel(
                 load_gate(HEAD + FIRST, SLOTS, nc.sync)
             if row == 2:
                 load_gate(0, HEAD, nc.sync)
+            if row == 7:
+                load_scales(w2_sc[0], w2_scales, nc.sync, slice(0, 2 * S))
             if row == 9:
                 nc.sync.dma_start(
                     w2_rest[:].bitcast(I32), w2_words[0, 1:S].bitcast(I32).rearrange("s p col -> p s col")
@@ -265,17 +265,20 @@ def tile_moe_bdx_glu_relu_kernel(
                         psum.tile([P, 2, C], F32, name="dx_pair", tag=f"dx{2 * (e % 2) + b}") for b in range(2)
                     ]
                 banks = [dx_banks[e][kt // 2][:, kt % 2, P * j : P * (j + 1)] for kt in range(4)]
-            for kt in range(4):
-                for w, (words, sc) in enumerate(((w3_t, w3_sc), (w1_t, w1_sc))):
-                    nc.tensor.matmul_mx(
-                        out=banks[kt],
-                        lhsT=words[:, e, 2 * P * kt : 2 * P * (kt + 1)].bitcast(FP4),
-                        lhsT_scale=sc[:, e, P * kt : P * (kt + 1)],
-                        rhs=da_codes[m][:, P * w : P * (w + 1)].bitcast(FP8),
-                        rhs_scale=da_scales[m][:, P * w : P * (w + 1)],
-                        start=(w == 0),
-                        stop=(w == 1),
-                    )
+            steps = [(kt, w) for kt in range(4) for w in range(2)]
+            if m == TILES - 1:
+                steps = [(kt, w) for w in range(2) for kt in range(4)]
+            for kt, w in steps:
+                words, sc = ((w3_t, w3_sc), (w1_t, w1_sc))[w]
+                nc.tensor.matmul_mx(
+                    out=banks[kt],
+                    lhsT=words[:, e, 2 * P * kt : 2 * P * (kt + 1)].bitcast(FP4),
+                    lhsT_scale=sc[:, e, P * kt : P * (kt + 1)],
+                    rhs=da_codes[m][:, P * w : P * (w + 1)].bitcast(FP8),
+                    rhs_scale=da_scales[m][:, P * w : P * (w + 1)],
+                    start=(w == 0),
+                    stop=(w == 1),
+                )
             for kt in range(4):
                 if m == TILES - 1 and kt > 0:
                     nc.vector.tensor_copy(dx[kt][:, P * m : P * (m + 1)], banks[kt])
@@ -363,16 +366,22 @@ def tile_moe_bdx_glu_relu_kernel(
         quantize_da(7, slice(1, 2))
         back(7)
 
+        def listed(kt, r, a, b):
+            return dx[kt][:].indirect(pos_t[r][:, a // 16 : b // 16])
+
         for kt in range(4):
             by_pos1 = keep.tile([P, T], F32, name=f"by_pos1_{kt}")
             total = keep.tile([P, T], F32, name=f"total{kt}")
-            cuts = FETCH_LAST if kt == 3 else FETCH
-            for a, b in zip(cuts, cuts[1:]):
-                nc.scalar.activation(by_pos1[:, a:b], dx[kt][:].indirect(pos_t[0][:, a // 16 : b // 16]), COPY)
-                nc.vector.tensor_tensor(
-                    total[:, a:b], dx[kt][:].indirect(pos_t[1][:, a // 16 : b // 16]), by_pos1[:, a:b], ADD
-                )
-                if kt == 3:
-                    nc.sync.dma_start(out[P * kt : P * (kt + 1), a:b], total[:, a:b])
-            if kt < 3:
-                nc.sync.dma_start(out[P * kt : P * (kt + 1), :], total[:])
+            rows = out[P * kt : P * (kt + 1), :]
+            cut = SPLIT if kt == 0 else T
+            nc.scalar.activation(by_pos1[:, 0:cut], listed(kt, 0, 0, cut), COPY)
+            if kt == 0:
+                nc.vector.tensor_copy(by_pos1[:, cut:T], listed(kt, 0, cut, T))
+            cut = SPLIT if kt == 3 else T
+            nc.vector.tensor_tensor(total[:, 0:cut], listed(kt, 1, 0, cut), by_pos1[:, 0:cut], ADD)
+            nc.sync.dma_start(rows[:, 0:cut], total[:, 0:cut])
+            if kt == 3:
+                by_pos2 = keep.tile([P, T - cut], F32, name="by_pos2")
+                nc.scalar.activation(by_pos2[:], listed(kt, 1, cut, T), COPY)
+                nc.vector.tensor_tensor(total[:, cut:T], by_pos2[:], by_pos1[:, cut:T], ADD)
+                nc.sync.dma_start(rows[:, cut:T], total[:, cut:T])

@@ -56,7 +56,8 @@ def tile_moe_bdx_glu_relu_kernel(
             nc.vector.memset(planes[row][:, T : WINDOWS[row // 4]], 0.0)
         w1_sc = keep.tile([P, E, K], U8, name="w1_sc", align_bytes=64)
         w3_sc = keep.tile([P, E, K], U8, name="w3_sc", align_bytes=64)
-        nc.gpsimd.memset(w2_sc[0][:].rearrange("p pas col -> p (pas col)").bitcast(I32), 0)
+        for sc in (w2_sc[0], w3_sc, w1_sc):
+            nc.gpsimd.memset(sc[:].rearrange("p pas col -> p (pas col)").bitcast(I32), 0)
         ident = keep.tile([P, P], F32, name="ident")
         make_identity(nc, ident[:])
 
@@ -98,8 +99,7 @@ def tile_moe_bdx_glu_relu_kernel(
                 )
 
         load_gate(HEAD, HEAD + FIRST, nc.scalar)
-        for sc in (w2_sc[1], w1_sc, w3_sc):
-            zero(sc)
+        zero(w2_sc[1])
         load_scales(w2_sc[1], w2_scales, nc.gpsimd, slice(2 * S, 4 * S))
         for row in range(4 * S):
             nc.sync.dma_start(planes[row][:, 0:T], dy_rows[row // 4, row % 4])

@@ -109,11 +109,12 @@ def tile_moe_bdx_glu_relu_kernel(
                 load_gate(0, HEAD, nc.sync)
             if row == 7:
                 load_scales(w2_sc[0], w2_scales, nc.sync, slice(0, 2 * S))
-            if row == 9:
+            if row == 10:
+                nc.sync.dma_start(w2_first[:].bitcast(I32), w2_words[0, 0].bitcast(I32))
+            if row == 11:
                 nc.sync.dma_start(
                     w2_rest[:].bitcast(I32), w2_words[0, 1:S].bitcast(I32).rearrange("s p col -> p s col")
                 )
-        nc.sync.dma_start(w2_first[:].bitcast(I32), w2_words[0, 0].bitcast(I32))
         load_w2(1)
         load_saved(0)
         load_saved(1)
@@ -328,18 +329,18 @@ def tile_moe_bdx_glu_relu_kernel(
         quantize_da(0)
         products(1)
         gated(2, 3, 5, "m0")
-        quantize_da(1)
+        mask(2, "m1")
         quantize_g(2, 3, 5)
         through(3, "raw_d")
         through(4, "raw_v")
         gather(2, 5, 7, "w2_1")
         gather(2, 7, 8, "raw_d")
-        mask(2, "m1")
-        gated(1, 5, 8, "m0")
+        quantize_da(1)
         products(2)
-        quantize_g(1, 5, 8)
-        mask(3, "m2")
+        gated(1, 5, 8, "m0")
         quantize_da(2)
+        mask(3, "m2")
+        quantize_g(1, 5, 8)
         products(3)
         gated(2, 5, 7, "m1")
         quantize_da(3)
@@ -384,4 +385,4 @@ def tile_moe_bdx_glu_relu_kernel(
                 by_pos2 = keep.tile([P, T - cut], F32, name="by_pos2")
                 nc.scalar.activation(by_pos2[:], listed(kt, 1, cut, T), COPY)
                 nc.vector.tensor_tensor(total[:, cut:T], by_pos2[:], by_pos1[:, cut:T], ADD)
-                nc.sync.dma_start(rows[:, cut:T], total[:, cut:T])
+                nc.scalar.dma_start(rows[:, cut:T], total[:, cut:T])

@@ -52,14 +52,13 @@ def tile_moe_bdx_glu_relu_kernel(
 
         planes = [keep.tile([P, WINDOWS[row // 4]], F32, name=f"plane{row}") for row in range(4 * S)]
         w2_sc = [keep.tile([P, 2 * S, H], U8, name=f"w2_sc{half}", align_bytes=64) for half in range(2)]
-        for row in range(4):
-            nc.vector.memset(planes[row][:, T : WINDOWS[row // 4]], 0.0)
         w1_sc = keep.tile([P, E, K], U8, name="w1_sc", align_bytes=64)
         w3_sc = keep.tile([P, E, K], U8, name="w3_sc", align_bytes=64)
-        for sc in (w2_sc[0], w3_sc, w1_sc):
-            nc.gpsimd.memset(sc[:].rearrange("p pas col -> p (pas col)").bitcast(I32), 0)
+        for sc in (w3_sc, w1_sc):
+            nc.vector.memset(sc[:].rearrange("p pas col -> p (pas col)").bitcast(I32), 0)
+        for row in range(4):
+            nc.vector.memset(planes[row][:, T : WINDOWS[row // 4]], 0.0)
         ident = keep.tile([P, P], F32, name="ident")
-        make_identity(nc, ident[:])
 
         dy_rows = dyT.rearrange("(s p t) token -> s t p token", p=P, t=4)
         gate_t = keep.tile([P, SLOTS], F32, name="gate_t")
@@ -99,6 +98,9 @@ def tile_moe_bdx_glu_relu_kernel(
                 )
 
         load_gate(HEAD, HEAD + FIRST, nc.scalar)
+        zero(w2_sc[0])
+        load_scales(w2_sc[0], w2_scales, nc.gpsimd, slice(0, 2 * S))
+        make_identity(nc, ident[:])
         zero(w2_sc[1])
         load_scales(w2_sc[1], w2_scales, nc.gpsimd, slice(2 * S, 4 * S))
         for row in range(4 * S):
@@ -107,8 +109,6 @@ def tile_moe_bdx_glu_relu_kernel(
                 load_gate(HEAD + FIRST, SLOTS, nc.sync)
             if row == 2:
                 load_gate(0, HEAD, nc.sync)
-            if row == 7:
-                load_scales(w2_sc[0], w2_scales, nc.sync, slice(0, 2 * S))
             if row == 10:
                 nc.sync.dma_start(w2_first[:].bitcast(I32), w2_words[0, 0].bitcast(I32))
             if row == 11:

@@ -74,8 +74,12 @@ def tile_moe_bdx_glu_relu_kernel(
         w1_t = keep.tile([P, E, 2 * K], U8, name="w1_t", align_bytes=64)
         w3_t = keep.tile([P, E, 2 * K], U8, name="w3_t", align_bytes=64)
         pos_t = [keep.tile([P, T // 16], U16, name=f"pos_t{r}") for r in range(2)]
-        a1_t = [keep.tile([P, 4, C], F32, name=f"a1_{e}") for e in range(E)]
-        a3_t = [keep.tile([P, 4, C], F32, name=f"a3_{e}") for e in range(E)]
+        saved = {
+            (w, lo): keep.tile([P, 4, C * (hi - lo)], F32, name=f"saved{w}_{lo}")
+            for w in range(2)
+            for lo, hi in ((0, 1), (1, 2), (2, 3), (3, 4))
+        }
+        a1_t, a3_t = ([saved[w, e][:] for e in range(E)] for w in range(2))
 
         def load_gate(a, b, queue):
             queue.dma_start(gate_t[:, a:b], gate[0:P, a:b])
@@ -83,15 +87,18 @@ def tile_moe_bdx_glu_relu_kernel(
         def load_w2(e):
             nc.sync.dma_start(w2_t[e - 1][:].bitcast(I32), w2_words[e].bitcast(I32).rearrange("s p col -> p s col"))
 
-        def load_saved(e):
-            for tiles, src in ((a1_t, a1), (a3_t, a3)):
-                nc.sync.dma_start(tiles[e][:], src.rearrange("(p t) x -> p t x", t=4)[:, :, C * e : C * (e + 1)])
+        def load_saved(w, lo, hi):
+            rows = (a1, a3)[w].rearrange("(p t) x -> p t x", t=4)
+            nc.sync.dma_start(saved[w, lo][:], rows[:, :, C * lo : C * hi])
+
+        def load_words(tile, src):
+            nc.sync.dma_start(tile[:].bitcast(I32), src.bitcast(I32).rearrange("e s p col -> p (e s) col"))
 
         def zero(sc):
             nc.gpsimd.memset(sc[:].rearrange("p pas col -> p (pas col)").bitcast(I32), 0)
 
-        def load_scales(sc, src, queue, passes=slice(None)):
-            for q in (0, 2, 1, 3):
+        def load_scales(sc, src, queue, passes=slice(None), quadrants=(0, 2, 1, 3)):
+            for q in quadrants:
                 queue.dma_start(
                     sc[32 * q : 32 * q + 4].bitcast(I32),
                     src.bitcast(I32).rearrange("e s f col -> f (e s) col")[4 * q : 4 * q + 4, passes],
@@ -116,16 +123,20 @@ def tile_moe_bdx_glu_relu_kernel(
                     w2_rest[:].bitcast(I32), w2_words[0, 1:S].bitcast(I32).rearrange("s p col -> p s col")
                 )
         load_w2(1)
-        load_saved(0)
-        load_saved(1)
+        for e in range(2):
+            for w in range(2):
+                load_saved(w, e, e + 1)
         load_w2(2)
-        for tile, src in ((w3_t, w3_words), (w1_t, w1_words)):
-            nc.sync.dma_start(tile[:].bitcast(I32), src.bitcast(I32).rearrange("e s p col -> p (e s) col"))
-        load_scales(w3_sc, w3_scales, nc.sync)
-        load_scales(w1_sc, w1_scales, nc.sync)
+        load_scales(w3_sc, w3_scales, nc.sync, quadrants=(0, 2))
+        load_words(w3_t, w3_words)
+        load_scales(w3_sc, w3_scales, nc.sync, quadrants=(1, 3))
+        load_words(w1_t, w1_words)
+        load_scales(w1_sc, w1_scales, nc.sync, quadrants=(0, 2))
         load_w2(3)
-        load_saved(2)
-        load_saved(3)
+        load_scales(w1_sc, w1_scales, nc.sync, quadrants=(1, 3))
+        for e in range(2, E):
+            for w in range(2):
+                load_saved(w, e, e + 1)
         for tile, src in zip(pos_t, (pos1, pos2)):
             nc.sync.dma_start(tile[:], src)
 

@@ -77,9 +77,9 @@ def tile_moe_bdx_glu_relu_kernel(
         saved = {
             (w, lo): keep.tile([P, 4, C * (hi - lo)], F32, name=f"saved{w}_{lo}")
             for w in range(2)
-            for lo, hi in ((0, 1), (1, 2), (2, 3), (3, 4))
+            for lo, hi in ((0, 2), (2, 3), (3, 4))
         }
-        a1_t, a3_t = ([saved[w, e][:] for e in range(E)] for w in range(2))
+        a1_t, a3_t = ([saved[w, 0][:, :, 0:C], saved[w, 0][:, :, C : 2 * C], saved[w, 2][:], saved[w, 3][:]] for w in range(2))
 
         def load_gate(a, b, queue):
             queue.dma_start(gate_t[:, a:b], gate[0:P, a:b])
@@ -106,7 +106,6 @@ def tile_moe_bdx_glu_relu_kernel(
 
         load_gate(HEAD, HEAD + FIRST, nc.scalar)
         zero(w2_sc[0])
-        load_scales(w2_sc[0], w2_scales, nc.gpsimd, slice(0, 2 * S))
         make_identity(nc, ident[:])
         zero(w2_sc[1])
         load_scales(w2_sc[1], w2_scales, nc.gpsimd, slice(2 * S, 4 * S))
@@ -116,6 +115,8 @@ def tile_moe_bdx_glu_relu_kernel(
                 load_gate(HEAD + FIRST, SLOTS, nc.sync)
             if row == 2:
                 load_gate(0, HEAD, nc.sync)
+            if row in (5, 7):
+                load_scales(w2_sc[0], w2_scales, nc.sync, slice(0, 2 * S), (0, 2) if row == 5 else (1, 3))
             if row == 10:
                 nc.sync.dma_start(w2_first[:].bitcast(I32), w2_words[0, 0].bitcast(I32))
             if row == 11:
@@ -123,9 +124,8 @@ def tile_moe_bdx_glu_relu_kernel(
                     w2_rest[:].bitcast(I32), w2_words[0, 1:S].bitcast(I32).rearrange("s p col -> p s col")
                 )
         load_w2(1)
-        for e in range(2):
-            for w in range(2):
-                load_saved(w, e, e + 1)
+        for w in range(2):
+            load_saved(w, 0, 2)
         load_w2(2)
         load_scales(w3_sc, w3_scales, nc.sync, quadrants=(0, 2))
         load_words(w3_t, w3_words)

@@ -14,6 +14,7 @@ WINDOWS = (SLOTS - HEAD + 1, T, T)
 DH_BANK = ("dh0", "dh1", "dh0", "dx0", "dx1", "dh1", "dh0", "dh1")
 RUN = 2
 SPLIT = 320
+LAST = 256
 
 FLOPS = 2 * SLOTS * (N * H + 2 * H * K)
 BYTES = 11210752
@@ -50,8 +51,11 @@ def tile_moe_bdx_glu_relu_kernel(
         nc.vector.memset(warm[:, 0:1], 0.0)
         nc.scalar.activation(warm[:, 1:2], warm[:, 0:1], COPY)
 
-        planes = [keep.tile([P, WINDOWS[row // 4]], F32, name=f"plane{row}") for row in range(4 * S)]
-        w2_sc = [keep.tile([P, 2 * S, H], U8, name=f"w2_sc{half}", align_bytes=64) for half in range(2)]
+        planes = [
+            work.tile([P, WINDOWS[row // 4]], F32, name="plane", tag=f"plane{row}", align_bytes=64)
+            for row in range(4 * S)
+        ]
+        w2_sc = [keep.tile([P, 2 * S, H], U8, name="w2_sc0", align_bytes=64)]
         w1_sc = keep.tile([P, E, K], U8, name="w1_sc", align_bytes=64)
         w3_sc = keep.tile([P, E, K], U8, name="w3_sc", align_bytes=64)
         for sc in (w3_sc, w1_sc):
@@ -107,13 +111,11 @@ def tile_moe_bdx_glu_relu_kernel(
         load_gate(HEAD, HEAD + FIRST, nc.scalar)
         zero(w2_sc[0])
         make_identity(nc, ident[:])
-        zero(w2_sc[1])
-        load_scales(w2_sc[1], w2_scales, nc.gpsimd, slice(2 * S, 4 * S))
         for row in range(4 * S):
             nc.sync.dma_start(planes[row][:, 0:T], dy_rows[row // 4, row % 4])
             if row == 0:
                 load_gate(HEAD + FIRST, SLOTS, nc.sync)
-            if row == 2:
+            if row == 4:
                 load_gate(0, HEAD, nc.sync)
             if row in (5, 7):
                 load_scales(w2_sc[0], w2_scales, nc.sync, slice(0, 2 * S), (0, 2) if row == 5 else (1, 3))
@@ -309,6 +311,9 @@ def tile_moe_bdx_glu_relu_kernel(
 
         gather_gated(0, 3, 8, "raw_v")
         gather(0, 0, 3, "raw_a")
+        w2_sc.append(work.tile([P, 2 * S, H], U8, name="w2_sc1", tag="plane0", align_bytes=64))
+        zero(w2_sc[1])
+        load_scales(w2_sc[1], w2_scales, nc.gpsimd, slice(2 * S, 4 * S))
         gated(0, 0, 3, "woven_a")
         quantize_g(0, 0, 3)
         gather(1, 0, 3, "raw_b")
@@ -344,15 +349,16 @@ def tile_moe_bdx_glu_relu_kernel(
         quantize_g(2, 3, 5)
         through(3, "raw_d")
         through(4, "raw_v")
+        prepare(3, "raw_f")
         gather(2, 5, 7, "w2_1")
         gather(2, 7, 8, "raw_d")
         quantize_da(1)
         products(2)
         gated(1, 5, 8, "m0")
         quantize_da(2)
-        mask(3, "m2")
+        products_late(3)
         quantize_g(1, 5, 8)
-        products(3)
+        products_rest(3)
         gated(2, 5, 7, "m1")
         quantize_da(3)
         quantize_g(2, 5, 7)
@@ -389,7 +395,7 @@ def tile_moe_bdx_glu_relu_kernel(
             nc.scalar.activation(by_pos1[:, 0:cut], listed(kt, 0, 0, cut), COPY)
             if kt == 0:
                 nc.vector.tensor_copy(by_pos1[:, cut:T], listed(kt, 0, cut, T))
-            cut = SPLIT if kt == 3 else T
+            cut = LAST if kt == 3 else T
             nc.vector.tensor_tensor(total[:, 0:cut], listed(kt, 1, 0, cut), by_pos1[:, 0:cut], ADD)
             nc.sync.dma_start(rows[:, 0:cut], total[:, 0:cut])
             if kt == 3:

@@ -315,13 +315,13 @@ def tile_moe_bdx_glu_relu_kernel(
         zero(w2_sc[1])
         load_scales(w2_sc[1], w2_scales, nc.gpsimd, slice(2 * S, 4 * S))
         gated(0, 0, 3, "woven_a")
+        weave(0, 3, 5, "woven_b", 3)
         quantize_g(0, 0, 3)
         gather(1, 0, 3, "raw_b")
-        gated(1, 0, 3, "woven_b")
+        gated(1, 0, 3, "woven_f")
+        quantize_g(0, 3, 5)
         quantize_g(1, 0, 3)
         gather(2, 0, 3, "raw_c")
-        weave(0, 3, 5, "woven_b", 3)
-        quantize_g(0, 3, 5)
         gated(2, 0, 1, "woven_c", 0)
         gated(2, 1, 2, "woven_d", 0)
         quantize_g(2, 0, 1)

from contextlib import ExitStack

import concourse.mybir as mybir
from concourse.masks import make_identity

K, T, E, C, H, N = 512, 512, 4, 256, 512, 1536
P = 128
S = N // 512
SLOTS = E * C
TILES = SLOTS // P
HEAD = 384
FIRST = 256
WINDOWS = (SLOTS - HEAD + 1, T, T)
DH_BANK = ("dh0", "dh1", "dh0", "dx0", "dx1", "dh1", "dh0", "dh1")
RUN = 2
SPLIT = 320
LAST = 256

FLOPS = 2 * SLOTS * (N * H + 2 * H * K)
BYTES = 11210752

F32 = mybir.dt.float32
BF16 = mybir.dt.bfloat16
I32 = mybir.dt.int32
U32 = mybir.dt.uint32
U16 = mybir.dt.uint16
U8 = mybir.dt.uint8
FP8 = mybir.dt.float8_e4m3fn_x4
FP4 = mybir.dt.float4_e2m1fn_x4
MULT = mybir.AluOpType.mult
ADD = mybir.AluOpType.add
IS_GT = mybir.AluOpType.is_gt
COPY = mybir.ActivationFunctionType.Copy
RELU = mybir.ActivationFunctionType.Relu
SIGN = mybir.ActivationFunctionType.Sign


def tile_moe_bdx_glu_relu_kernel(
    tc, dyT, a1, a3, w2_words, w2_scales, w1_words, w1_scales, w3_words, w3_scales, gate, offs, pos1, pos2, out
):
    nc = tc.nc
    with ExitStack() as ctx:
        keep = ctx.enter_context(tc.tile_pool(name="keep", bufs=1))
        work = ctx.enter_context(tc.tile_pool(name="work", bufs=1))
        psum = ctx.enter_context(tc.psum_pool(name="psum", bufs=1))

        offs_t = keep.tile([P, SLOTS // 16], U16, name="offs_t")
        nc.sync.dma_start(offs_t[:], offs)

        warm = keep.tile([P, 2], F32, name="warm")
        nc.vector.memset(warm[:, 0:1], 0.0)
        nc.scalar.activation(warm[:, 1:2], warm[:, 0:1], COPY)

        planes = [
            work.tile([P, WINDOWS[row // 4]], F32, name="plane", tag=f"plane{row}", align_bytes=64)
            for row in range(4 * S)
        ]
        w2_sc = [keep.tile([P, 2 * S, H], U8, name="w2_sc0", align_bytes=64)]
        w1_sc = keep.tile([P, E, K], U8, name="w1_sc", align_bytes=64)
        w3_sc = keep.tile([P, E, K], U8, name="w3_sc", align_bytes=64)
        for sc in (w3_sc, w1_sc):
            nc.vector.memset(sc[:].rearrange("p pas col -> p (pas col)").bitcast(I32), 0)
        for row in range(4):
            nc.vector.memset(planes[row][:, T : WINDOWS[row // 4]], 0.0)
        ident = keep.tile([P, P], F32, name="ident")

        dy_rows = dyT.rearrange("(s p t) token -> s t p token", p=P, t=4)
        gate_t = keep.tile([P, SLOTS], F32, name="gate_t")
        g_codes = [keep.tile([P, SLOTS], U32, name=f"g_codes{s}", align_bytes=64) for s in range(S)]
        g_scales = [keep.tile([P, SLOTS], U8, name=f"g_scales{s}", align_bytes=64) for s in range(S)]
        w2_t = [work.tile([P, S, 2 * H], U8, name=f"w2_{e}", tag=f"w2_{e}", align_bytes=64) for e in range(1, E)]
        w2_first = work.tile([P, 2 * H], U8, name="w2_first", tag="raw_e", align_bytes=64)
        w2_rest = work.tile([P, S - 1, 2 * H], U8, name="w2_rest", tag="raw_f", align_bytes=64)
        w2_pass = {(e, s): w2_t[e - 1][:, s, :] for e in range(1, E) for s in range(S)}
        w2_pass[0, 0] = w2_first[:]
        for s in range(1, S):
            w2_pass[0, s] = w2_rest[:, s - 1, :]
        w1_t = keep.tile([P, E, 2 * K], U8, name="w1_t", align_bytes=64)
        w3_t = keep.tile([P, E, 2 * K], U8, name="w3_t", align_bytes=64)
        pos_t = [keep.tile([P, T // 16], U16, name=f"pos_t{r}") for r in range(2)]
        saved = {
            (w, lo): keep.tile([P, 4, C * (hi - lo)], F32, name=f"saved{w}_{lo}")
            for w in range(2)
            for lo, hi in ((0, 2), (2, 3), (3, 4))
        }
        a1_t, a3_t = ([saved[w, 0][:, :, 0:C], saved[w, 0][:, :, C : 2 * C], saved[w, 2][:], saved[w, 3][:]] for w in range(2))

        def load_gate(a, b, queue):
            queue.dma_start(gate_t[:, a:b], gate[0:P, a:b])

        def load_w2(e):
            nc.sync.dma_start(w2_t[e - 1][:].bitcast(I32), w2_words[e].bitcast(I32).rearrange("s p col -> p s col"))

        def load_saved(w, lo, hi):
            rows = (a1, a3)[w].rearrange("(p t) x -> p t x", t=4)
            nc.sync.dma_start(saved[w, lo][:], rows[:, :, C * lo : C * hi])

        def load_words(tile, src):
            nc.sync.dma_start(tile[:].bitcast(I32), src.bitcast(I32).rearrange("e s p col -> p (e s) col"))

        def zero(sc):
            nc.gpsimd.memset(sc[:].rearrange("p pas col -> p (pas col)").bitcast(I32), 0)

        def load_scales(sc, src, queue, passes=slice(None), quadrants=(0, 2, 1, 3)):
            for q in quadrants:
                queue.dma_start(
                    sc[32 * q : 32 * q + 4].bitcast(I32),
                    src.bitcast(I32).rearrange("e s f col -> f (e s) col")[4 * q : 4 * q + 4, passes],
                )

        load_gate(HEAD, HEAD + FIRST, nc.scalar)
        zero(w2_sc[0])
        make_identity(nc, ident[:])
        for row in range(4 * S):
            nc.sync.dma_start(planes[row][:, 0:T], dy_rows[row // 4, row % 4])
            if row == 0:
                load_gate(HEAD + FIRST, SLOTS, nc.sync)
            if row == 4:
                load_gate(0, HEAD, nc.sync)
            if row in (5, 7):
                load_scales(w2_sc[0], w2_scales, nc.sync, slice(0, 2 * S), (0, 2) if row == 5 else (1, 3))
            if row == 10:
                nc.sync.dma_start(w2_first[:].bitcast(I32), w2_words[0, 0].bitcast(I32))
            if row == 11:
                nc.sync.dma_start(
                    w2_rest[:].bitcast(I32), w2_words[0, 1:S].bitcast(I32).rearrange("s p col -> p s col")
                )
        load_w2(1)
        for w in range(2):
            load_saved(w, 0, 2)
        load_w2(2)
        load_scales(w3_sc, w3_scales, nc.sync, quadrants=(0, 2))
        load_words(w3_t, w3_words)
        load_scales(w3_sc, w3_scales, nc.sync, quadrants=(1, 3))
        load_words(w1_t, w1_words)
        load_scales(w1_sc, w1_scales, nc.sync, quadrants=(0, 2))
        load_w2(3)
        load_scales(w1_sc, w1_scales, nc.sync, quadrants=(1, 3))
        for e in range(2, E):
            for w in range(2):
                load_saved(w, e, e + 1)
        for tile, src in zip(pos_t, (pos1, pos2)):
            nc.sync.dma_start(tile[:], src)

        raw, woven, relu_a1, relu_mask = {}, {}, {}, {}
        dh, turned, masked_dh, da, da_codes, da_scales, dx_banks = {}, {}, {}, {}, {}, {}, {}
        dx = [keep.tile([P, SLOTS], F32, name=f"dx{kt}") for kt in range(4)]

        def runs(ap):
            return ap.rearrange("p t (g r) -> p g t r", r=RUN)

        def weaving(ap):
            return ap.rearrange("p (g r) t -> p g t r", r=RUN)

        def gather(s, lo, hi, home):
            raw[s, lo] = work.tile([P, 4, P * (hi - lo)], F32, name="raw", tag=home, align_bytes=64)
            for t in range(4):
                nc.scalar.activation(
                    raw[s, lo][:, t, :], planes[4 * s + t][:].indirect(offs_t[:, P * lo // 16 : P * hi // 16]), COPY
                )

        def gather_gated(s, lo, hi, home):
            raw[s, lo] = work.tile([P, 4, P * (hi - lo)], F32, name="raw", tag=home, align_bytes=64)
            for t in range(4):
                cuts = (P * lo, P * lo + FIRST, P * hi) if t == 0 else (P * lo, P * hi)
                for a, b in zip(cuts, cuts[1:]):
                    nc.vector.tensor_tensor(
                        raw[s, lo][:, t, a - P * lo : b - P * lo],
                        planes[4 * s + t][:].indirect(offs_t[:, a // 16 : b // 16]),
                        gate_t[:, a:b],
                        MULT,
                    )

        def weave(s, lo, hi, home, base):
            woven[s, lo] = work.tile([P, P * (hi - lo), 4], BF16, name="woven", tag=home, align_bytes=64)
            nc.vector.tensor_copy(
                woven[s, lo][:].rearrange("p (g r) t -> p g t r", r=4),
                raw[s, base][:, :, P * (lo - base) : P * (hi - base)].rearrange("p t (g r) -> p g t r", r=4),
            )

        def gated(s, lo, hi, home, base=None):
            base = lo if base is None else base
            woven[s, lo] = work.tile([P, P * (hi - lo), 4], BF16, name="woven", tag=home, align_bytes=64)
            nc.vector.tensor_tensor(
                weaving(woven[s, lo][:]),
                runs(raw[s, base][:, :, P * (lo - base) : P * (hi - base)]),
                gate_t[:, P * lo : P * hi]
                .rearrange("p (g r) -> p g r", r=RUN)
                .unsqueeze(2)
                .to_broadcast([P, P * (hi - lo) // RUN, 4, RUN]),
                MULT,
            )

        def quantize_g(s, lo, hi, base=None):
            base = lo if base is None else base
            nc.vector.quantize_mx(
                out=g_codes[s][:, P * lo : P * hi].bitcast(FP8),
                scales=g_scales[s][:, P * lo : P * hi],
                in_=woven[s, base][:, P * (lo - base) : P * (hi - base), :].rearrange("p x t -> p (x t)"),
            )

        def first(tiles, order=(0, 1, 2)):
            for m in tiles:
                dh[m] = psum.tile([P, H], F32, name="dh", tag=DH_BANK[m])
            for s in order:
                for m in tiles:
                    e, cols = m // 2, slice(P * m, P * (m + 1))
                    nc.tensor.matmul_mx(
                        out=dh[m][:],
                        lhsT=g_codes[s][:, cols].bitcast(FP8),
                        lhsT_scale=g_scales[s][:, cols],
                        rhs=w2_pass[e, s].bitcast(FP4),
                        rhs_scale=w2_sc[e // 2][:, S * (e % 2) + s, :],
                        start=(s == order[0]),
                        stop=(s == order[-1]),
                    )

        def turn(m, home):
            sorted_dh = work.tile([P, 4, P], F32, name="sorted_dh", tag=home, align_bytes=64)
            nc.scalar.copy(
                sorted_dh[:].rearrange("x t (g r) -> x g t r", r=4),
                dh[m][:].rearrange("x (g r t) -> x g t r", r=4, t=4),
            )
            turned[m] = psum.tile([P, 4, P], F32, name="turned", tag=f"turned{m % 2}")
            for t in range(4):
                nc.tensor.transpose(turned[m][:, t, :], sorted_dh[:, t, :], ident[:])

        def mask(m, home):
            e, cols = m // 2, slice(P * (m % 2), P * (m % 2 + 1))
            masked_dh[m] = work.tile([P, 4, P], F32, name="masked_dh", tag=home, align_bytes=64)
            nc.vector.scalar_tensor_tensor(masked_dh[m][:], a1_t[e][:, :, cols], 0.0, turned[m][:], IS_GT, MULT)

        def products(m):
            e, cols = m // 2, slice(P * (m % 2), P * (m % 2 + 1))
            da[m] = work.tile([P, 2, P, 4], BF16, name="da", tag=f"da{m % 2}", align_bytes=64)
            for w, tiles in enumerate((a1_t, a3_t)):
                nc.vector.tensor_tensor(weaving(da[m][:, w]), runs(masked_dh[m][:]), runs(tiles[e][:, :, cols]), MULT)

        def prepare(m, home):
            e, cols = m // 2, slice(P * (m % 2), P * (m % 2 + 1))
            relu_a1[m] = work.tile([P, 4, P], F32, name="relu_a1", tag=home, align_bytes=64)
            relu_mask[m] = keep.tile([P, P, 4], BF16, name=f"relu_mask{m}")
            nc.scalar.activation(relu_a1[m][:], a1_t[e][:, :, cols], RELU)
            nc.scalar.activation(
                relu_mask[m][:].rearrange("p (g r) t -> p g t r", r=4),
                relu_a1[m][:].rearrange("p t (g r) -> p g t r", r=4),
                SIGN,
            )

        def products_late(m):
            e, cols = m // 2, slice(P * (m % 2), P * (m % 2 + 1))
            da[m] = work.tile([P, 2, P, 4], BF16, name="da", tag=f"da{m % 2}", align_bytes=64)
            nc.vector.tensor_tensor(weaving(da[m][:, 1]), runs(turned[m][:]), runs(a3_t[e][:, :, cols]), MULT)

        def products_rest(m):
            nc.vector.tensor_tensor(weaving(da[m][:, 0]), runs(turned[m][:]), runs(relu_a1[m][:]), MULT)
            nc.vector.tensor_tensor(da[m][:, 1], da[m][:, 1], relu_mask[m][:], MULT)

        def quantize_da(m, sides=slice(0, 2)):
            if sides.start == 0:
                da_codes[m] = keep.tile([P, 2 * P], U32, name=f"da_codes{m}", align_bytes=64)
                da_scales[m] = keep.tile([P, 2 * P], U8, name=f"da_scales{m}", align_bytes=64)
            nc.vector.quantize_mx(
                out=da_codes[m][:, P * sides.start : P * sides.stop].bitcast(FP8),
                scales=da_scales[m][:, P * sides.start : P * sides.stop],
                in_=da[m][:, sides].rearrange("p w x t -> p (w x t)"),
            )

        def back(m):
            e, j = m // 2, m % 2
            if m == TILES - 1:
                banks = [psum.tile([P, P], F32, name="dx_last", tag=tag)[:] for tag in ("dh0", "dh1", "turned0", "dx3")]
            elif m == TILES - 2:
                bank = psum.tile([P, 4, P], F32, name="dx_next", tag="dx2")
                banks = [bank[:, kt, :] for kt in range(4)]
            else:
                if j == 0:
                    dx_banks[e] = [
                        psum.tile([P, 2, C], F32, name="dx_pair", tag=f"dx{2 * (e % 2) + b}") for b in range(2)
                    ]
                banks = [dx_banks[e][kt // 2][:, kt % 2, P * j : P * (j + 1)] for kt in range(4)]
            steps = [(kt, w) for kt in range(4) for w in range(2)]
            if m == TILES - 1:
                steps = [(kt, w) for w in range(2) for kt in range(4)]
            for kt, w in steps:
                words, sc = ((w3_t, w3_sc), (w1_t, w1_sc))[w]
                nc.tensor.matmul_mx(
                    out=banks[kt],
                    lhsT=words[:, e, 2 * P * kt : 2 * P * (kt + 1)].bitcast(FP4),
                    lhsT_scale=sc[:, e, P * kt : P * (kt + 1)],
                    rhs=da_codes[m][:, P * w : P * (w + 1)].bitcast(FP8),
                    rhs_scale=da_scales[m][:, P * w : P * (w + 1)],
                    start=(w == 0),
                    stop=(w == 1),
                )
            for kt in range(4):
                if m == TILES - 1 and kt > 0:
                    nc.vector.tensor_copy(dx[kt][:, P * m : P * (m + 1)], banks[kt])
                elif m >= TILES - 2:
                    nc.scalar.copy(dx[kt][:, P * m : P * (m + 1)], banks[kt])
                elif j == 1:
                    nc.scalar.copy(dx[kt][:, C * e : C * (e + 1)], dx_banks[e][kt // 2][:, kt % 2, :])

        def done(m):
            quantize_da(m)
            back(m)

        def through(m, home):
            first((m,))
            turn(m, home)

        gather_gated(0, 3, 8, "raw_v")
        gather(0, 0, 3, "raw_a")
        w2_sc.append(work.tile([P, 2 * S, H], U8, name="w2_sc1", tag="plane0", align_bytes=64))
        zero(w2_sc[1])
        load_scales(w2_sc[1], w2_scales, nc.gpsimd, slice(2 * S, 4 * S))
        gated(0, 0, 3, "woven_a")
        weave(0, 3, 5, "woven_b", 3)
        quantize_g(0, 0, 3)
        gather(1, 0, 3, "raw_b")
        gated(1, 0, 3, "woven_f")
        quantize_g(0, 3, 5)
        quantize_g(1, 0, 3)
        gather(2, 0, 3, "raw_c")
        gated(2, 0, 1, "woven_c", 0)
        gated(2, 1, 2, "woven_d", 0)
        quantize_g(2, 0, 1)
        gated(2, 2, 3, "woven_e", 0)
        quantize_g(2, 1, 2)
        weave(0, 5, 8, "woven_c", 3)
        quantize_g(2, 2, 3)
        first((0, 1))
        gather(1, 3, 5, "raw_e")
        turn(0, "raw_a")
        turn(1, "raw_c")
        gather(2, 3, 5, "raw_f")
        through(2, "raw_b")
        gather(1, 5, 8, "raw_c")
        gated(1, 3, 5, "woven_d")
        quantize_g(0, 5, 8)
        mask(0, "m0")
        quantize_g(1, 3, 5)
        products(0)
        mask(1, "m1")
        quantize_da(0)
        products(1)
        gated(2, 3, 5, "m0")
        mask(2, "m1")
        quantize_g(2, 3, 5)
        through(3, "raw_d")
        through(4, "raw_v")
        prepare(3, "raw_f")
        gather(2, 5, 7, "w2_1")
        gather(2, 7, 8, "raw_d")
        quantize_da(1)
        products(2)
        gated(1, 5, 8, "m0")
        quantize_da(2)
        products_late(3)
        quantize_g(1, 5, 8)
        products_rest(3)
        gated(2, 5, 7, "m1")
        quantize_da(3)
        quantize_g(2, 5, 7)
        through(5, "sorted")
        through(6, "sorted_b")
        for m in range(4):
            back(m)
        mask(4, "m0")
        gated(2, 7, 8, "m2")
        products(4)
        quantize_g(2, 7, 8)
        prepare(6, "sorted")
        through(7, "raw_v")
        prepare(7, "sorted_b")
        mask(5, "m1")
        done(4)
        products(5)
        for m in (6, 7):
            products_late(m)
            done(m - 1)
            products_rest(m)
        quantize_da(7, slice(0, 1))
        quantize_da(7, slice(1, 2))
        back(7)

        def listed(kt, r, a, b):
            return dx[kt][:].indirect(pos_t[r][:, a // 16 : b // 16])

        for kt in range(4):
            by_pos1 = keep.tile([P, T], F32, name=f"by_pos1_{kt}")
            total = keep.tile([P, T], F32, name=f"total{kt}")
            rows = out[P * kt : P * (kt + 1), :]
            cut = SPLIT if kt == 0 else T
            nc.scalar.activation(by_pos1[:, 0:cut], listed(kt, 0, 0, cut), COPY)
            if kt == 0:
                nc.vector.tensor_copy(by_pos1[:, cut:T], listed(kt, 0, cut, T))
            cut = LAST if kt == 3 else T
            nc.vector.tensor_tensor(total[:, 0:cut], listed(kt, 1, 0, cut), by_pos1[:, 0:cut], ADD)
            nc.sync.dma_start(rows[:, 0:cut], total[:, 0:cut])
            if kt == 3:
                by_pos2 = keep.tile([P, T - cut], F32, name="by_pos2")
                nc.scalar.activation(by_pos2[:], listed(kt, 1, cut, T), COPY)
                nc.vector.tensor_tensor(total[:, cut:T], by_pos2[:], by_pos1[:, cut:T], ADD)
                nc.scalar.dma_start(rows[:, cut:T], total[:, cut:T])
